import numpy as np
import ml_dtypes


def mxq(x, axis, fmt="e4m3"):
    dtype, down = {"e4m3": (ml_dtypes.float8_e4m3fn, 7), "e5m2": (ml_dtypes.float8_e5m2, 14)}[fmt]
    v = np.moveaxis(np.asarray(x, np.float32).astype(ml_dtypes.bfloat16).astype(np.float64), axis, -1)
    blocks = v.reshape(v.shape[:-1] + (-1, 32))
    amax = np.abs(blocks).max(-1, keepdims=True)
    byte = np.maximum(np.where(amax > 0, np.frexp(amax)[1] - 1 + 127, 0) - down, 1)
    scale = np.exp2(byte - 127.0)
    codes = (blocks / scale).astype(np.float32).astype(dtype).astype(np.float64)
    return np.moveaxis((codes * scale).reshape(v.shape), -1, axis)


WIDE = False


def mx_kscale(k):
    if not WIDE:
        return np.ones(k)
    levels = np.array([10, -10, 5, -5, 0])
    if k % 512:
        return np.exp2(np.random.permutation(np.resize(levels, k // 32))).repeat(32)
    a = np.empty((k // 512, 16))
    for p in range(k // 512):
        a[p, :8] = np.random.permutation(np.resize(levels, 8))
        for g in range(8):
            far = levels[np.abs(levels - a[p, g]) >= 10]
            a[p, g + 8] = far[np.random.randint(len(far))]
    return np.exp2(a.ravel()).repeat(32)


def f64(x):
    return np.asarray(x).astype(np.float64)


def striped(idx):
    return np.tile(idx.reshape(-1, 16).T, (8, 1)).astype(np.uint16)


def unstriped(offs):
    return offs[:16].T.reshape(-1).astype(np.int64)


def pack_weight(w):
    k, n = w.shape
    w = f64(np.asarray(w, np.float32).astype(ml_dtypes.bfloat16)).reshape(k // 32, 32, n)
    amax = np.abs(w).max(1)
    byte = np.clip(np.where(amax > 0, np.frexp(amax)[1] - 1 + 127 - 7, 1), 1, 254)
    scaled = (w * np.exp2(127.0 - byte)[:, None, :]).reshape(k, n).astype(np.float32)
    words = np.ascontiguousarray(scaled.reshape(k // 512, 128, 4, n).transpose(0, 1, 3, 2)).astype(ml_dtypes.float8_e4m3fn).view(np.uint8)
    return words, np.ascontiguousarray(byte.astype(np.uint8).reshape(k // 512, 16, n))


def unpack_weight(words, scales):
    g, p, n, _ = words.shape
    vals = np.ascontiguousarray(words).view(ml_dtypes.float8_e4m3fn).astype(np.float64) * np.repeat(np.exp2(scales.astype(np.float64) - 127.0), 8, axis=1)[..., None]
    return vals.transpose(0, 1, 3, 2).reshape(g * 512, n)


def relu(v):
    return np.maximum(v, 0.0)


K, T, S, H, N = 1024, 2048, 1024, 512, 128


def setup_inputs():
    n = np.random.standard_normal
    s = mx_kscale(K)[:, None]
    u = mx_kscale(H)
    packed_w2 = pack_weight(n((H, N)) / np.sqrt(H) / u[:, None])
    return {
        "xT": (n((K, T)) * s).astype(np.float32),
        "w1": (n((K, H)) / np.sqrt(K) / s * u).astype(np.float32),
        "w2_words": packed_w2[0],
        "w2_scales": packed_w2[1],
        "offs": striped(np.random.permutation(T)[:S]),
    }


def reference(xT, w1, w2_words, w2_scales, offs):
    xq = mxq(f64(xT)[:, unstriped(offs)], 0, "e4m3")
    h = relu(mxq(f64(w1), 0, "e4m3").T @ xq)
    z = h - h.mean(axis=1, keepdims=True)
    return unpack_weight(w2_words, w2_scales).T @ mxq(z, 0, "e4m3")

@@ -1,0 +1,204 @@
+from contextlib import ExitStack
+
+import concourse.mybir as mybir
+
+K, T, S, H, N = 1024, 2048, 1024, 512, 128
+FLOPS = 2 * K * H * S + 2 * H * N * S
+
+F32 = mybir.dt.float32
+BF16 = mybir.dt.bfloat16
+I32 = mybir.dt.int32
+U32 = mybir.dt.uint32
+U16 = mybir.dt.uint16
+U8 = mybir.dt.uint8
+FP8X4 = mybir.dt.float8_e4m3fn_x4
+ALU = mybir.AluOpType
+ACT = mybir.ActivationFunctionType
+
+P = 128
+PACK = 4
+K_PASS = P * PACK
+PASSES = K // K_PASS
+HALF = 512
+HALVES = S // HALF
+LIST_COLS = HALF // 16
+OUT_CHUNK = 256
+X_CHUNKS = [[512, 512, 512, 512], [512, 512, 512, 256, 256]]
+W_CHUNKS = [[256, 256], [256, 128, 128]]
+WARM = 16
+
+
+def tile_picked_deepset_relu_e_kernel(tc, xT, w1, w2_words, w2_scales, offs, out):
+    nc = tc.nc
+    with ExitStack() as ctx:
+        keep = ctx.enter_context(tc.tile_pool(name="keep", bufs=1))
+        psum = ctx.enter_context(tc.psum_pool(name="psum", bufs=1))
+
+        offsets = keep.tile([P, S // 16], U16, name="offsets")
+        x_scales = keep.tile([P, T], U8, name="x_scales", align_bytes=64)
+        nc.vector.memset(x_scales[:].bitcast(I32), 0)
+        w2_sc = keep.tile([P, N], U8, name="w2_sc", align_bytes=64)
+        nc.vector.memset(w2_sc[:].bitcast(I32), 0)
+        w2_w = keep.tile([P, N], U32, name="w2_w", align_bytes=64)
+
+        for q in range(4):
+            nc.scalar.dma_start(out=w2_sc[32 * q:32 * q + 4, :].bitcast(I32), in_=w2_scales[0, 4 * q:4 * q + 4, :].bitcast(I32))
+        x_raw = {}
+        for g in range(PASSES):
+            c0 = 0
+            for c, width in enumerate(X_CHUNKS[g]):
+                raw = keep.tile([P, PACK, width], F32, name=f"x_raw{g}_{c}")
+                nc.sync.dma_start(out=raw[:], in_=xT[g * K_PASS:(g + 1) * K_PASS, c0:c0 + width].rearrange("(p j) w -> p j w", j=PACK))
+                x_raw[g, c] = (raw, c0, width)
+                c0 = c0 + width
+                if g == 0 and c == 0:
+                    nc.sync.dma_start(offsets[:], offs)
+        w_raw = {}
+        for g in range(PASSES):
+            c0 = 0
+            for b, width in enumerate(W_CHUNKS[g]):
+                raw = keep.tile([P, PACK, width], F32, name=f"w_raw{g}_{b}")
+                nc.sync.dma_start(out=raw[:], in_=w1[g * K_PASS:(g + 1) * K_PASS, c0:c0 + width].rearrange("(p j) w -> p j w", j=PACK))
+                w_raw[g, b] = (raw, c0, width)
+                c0 = c0 + width
+                if g == 0 and b == 0:
+                    nc.sync.dma_start(out=w2_w[:].bitcast(I32), in_=w2_words[0].rearrange("p n t -> p (n t)").bitcast(I32))
+
+        x_words = [keep.tile([P, T], U32, name=f"x_words{g}", align_bytes=64) for g in range(PASSES)]
+        g_words = {}
+        g_scales = {}
+
+        def round_x(g, c):
+            raw, c0, width = x_raw[g, c]
+            grouped = keep.tile([P, width * PACK], BF16, name=f"x_bf{g}_{c}", align_bytes=64)
+            dst = grouped[:].rearrange("p (c i j) -> p c j i", i=4, j=PACK)
+            src = raw[:].rearrange("p j (c i) -> p c j i", i=4)
+            split = (width * 5 // 8 if width == 512 else width // 2) // 4
+            nc.scalar.activation(out=dst[:, :split], in_=src[:, :split], func=ACT.Copy)
+            nc.vector.tensor_copy(out=dst[:, split:], in_=src[:, split:])
+            return grouped
+
+        def quantise_x(g, c, grouped):
+            raw, c0, width = x_raw[g, c]
+            nc.vector.quantize_mx(out=x_words[g][:, c0:c0 + width].bitcast(FP8X4), scales=x_scales[4 * g:, c0:c0 + width], in_=grouped[:])
+
+        def gather_words(g, a):
+            picked = keep.tile([P, HALF], U32, name=f"g_words{g}_{a}", tag=(f"w_bf{a}" if g == 1 else f"g_words{a}"), align_bytes=64)
+            nc.vector.tensor_copy(out=picked[:], in_=x_words[g][:].indirect(offsets[:, a * LIST_COLS:(a + 1) * LIST_COLS]))
+            g_words[g, a] = picked
+
+        def gather_scales(a):
+            picked = keep.tile([P, HALF], U8, name=f"g_scales{a}", align_bytes=64)
+            nc.vector.tensor_copy(out=picked[:], in_=x_scales[:].indirect(offsets[:, a * LIST_COLS:(a + 1) * LIST_COLS]))
+            g_scales[a] = picked
+
+        for g in range(PASSES):
+            for c in range(len(X_CHUNKS[g])):
+                quantise_x(g, c, round_x(g, c))
+                if g == 1 and c < HALVES:
+                    gather_words(0, c)
+
+        w_bf = [keep.tile([P, H * PACK], BF16, name=f"w_bf{g}", tag=f"w_bf{g}", align_bytes=64) for g in range(PASSES)]
+        w_words = [keep.tile([P, H], U32, name=f"w_words{g}", align_bytes=64) for g in range(PASSES)]
+        w_scales = [keep.tile([P, H], U8, name=f"w_scales{g}", align_bytes=64) for g in range(PASSES)]
+
+        def round_w(g):
+            dst = w_bf[g][:].rearrange("p (t m j) -> p m j t", t=PACK, j=PACK)
+            for b in range(len(W_CHUNKS[g])):
+                raw, c0, width = w_raw[g, b]
+                nc.scalar.activation(out=dst[:, c0 // PACK:(c0 + width) // PACK], in_=raw[:].rearrange("p j (m t) -> p m j t", t=PACK), func=ACT.Copy)
+
+        def quantise_w(g):
+            for t in range(PACK):
+                nc.vector.quantize_mx(out=w_words[g][:, t * P:(t + 1) * P].bitcast(FP8X4), scales=w_scales[g][:, t * P:(t + 1) * P], in_=w_bf[g][:, t * K_PASS:(t + 1) * K_PASS])
+
+        banks = {}
+        for t in range(PACK):
+            for a in range(HALVES):
+                banks[t, a] = psum.tile([P, HALF], F32, name=f"bank{t}_{a}", tag=f"bank{t}_{a}")
+
+        def first_product(g, t, a):
+            nc.tensor.matmul_mx(out=banks[t, a][:], lhsT=w_words[g][:, t * P:(t + 1) * P].bitcast(FP8X4), lhsT_scale=w_scales[g][:, t * P:(t + 1) * P],
+                                rhs=g_words[g, a][:].bitcast(FP8X4), rhs_scale=g_scales[a][4 * g:, :], start=(g == 0), stop=(g == PASSES - 1))
+
+        for i in range(WARM):
+            nc.tensor.matmul_mx(out=banks[3, 1][:, (i % 4) * N:(i % 4 + 1) * N], lhsT=w2_w[:].bitcast(FP8X4), lhsT_scale=w2_sc[:], rhs=w2_w[:].bitcast(FP8X4), rhs_scale=w2_sc[:], start=True, stop=True)
+        gather_scales(0)
+        gather_scales(1)
+        round_w(0)
+        quantise_w(0)
+        for a in range(HALVES):
+            for t in range(PACK):
+                first_product(0, t, a)
+        gather_words(1, 0)
+        round_w(1)
+        quantise_w(1)
+        gather_words(1, 1)
+        for a in range(HALVES):
+            for t in range(PACK):
+                first_product(1, t, a)
+
+        h = [keep.tile([P, S], F32, name=f"h{t}") for t in range(PACK)]
+        sums = [keep.tile([P, HALVES], F32, name=f"sums{t}") for t in range(PACK)]
+        neg_mean = [keep.tile([P, 1], F32, name=f"neg_mean{t}") for t in range(PACK)]
+        z_all = keep.tile([P, 2 * S * 2], BF16, name="z_all")
+        z_pairs = [z_all[:, u * 2 * S:(u + 1) * 2 * S].rearrange("p (s e) -> p s e", e=2) for u in range(2)]
+
+        def relu_out(t, a, on_vector):
+            dst = h[t][:, a * HALF:(a + 1) * HALF]
+            if on_vector:
+                nc.vector.tensor_scalar(out=dst, in0=banks[t, a][:], scalar1=0.0, scalar2=None, op0=ALU.max, op1=ALU.add, accum_out=sums[t][:, a:a + 1])
+            else:
+                nc.scalar.activation(out=dst, in_=banks[t, a][:], func=ACT.Relu, accum_out=sums[t][:, a:a + 1])
+
+        def mean(t):
+            nc.vector.tensor_scalar(out=neg_mean[t][:], in0=sums[t][:, 0:1], scalar1=sums[t][:, 1:2], scalar2=-1.0 / S, op0=ALU.add, op1=ALU.mult)
+
+        def centre(t, lo, hi, on_vector=True):
+            if on_vector:
+                nc.vector.tensor_scalar(out=z_pairs[t // 2][:, lo:hi, t % 2], in0=h[t][:, lo:hi], scalar1=neg_mean[t][:], scalar2=None, op0=ALU.add)
+            else:
+                nc.scalar.activation(out=z_pairs[t // 2][:, lo:hi, t % 2], in_=h[t][:, lo:hi], func=ACT.Identity, bias=neg_mean[t][:], scale=1.0)
+
+        for t in range(PACK):
+            relu_out(t, 0, False)
+        relu_out(0, 1, True)
+        relu_out(1, 1, True)
+        relu_out(2, 1, False)
+        mean(0)
+        mean(1)
+        relu_out(3, 1, True)
+        mean(2)
+        mean(3)
+
+        z_words = keep.tile([P, S], U32, name="z_words", align_bytes=64)
+        z_scales = keep.tile([P, S], U8, name="z_scales", align_bytes=64)
+        z_bf = {}
+
+        def weave(lo, hi):
+            z_bf[lo] = keep.tile([P, (hi - lo) * PACK], BF16, name=f"z_bf{lo}", align_bytes=64)
+            dst = z_bf[lo][:].bitcast(U32).rearrange("p (s u) -> p s u", u=2)
+            nc.scalar.copy(out=dst, in_=z_all[:].bitcast(U32).rearrange("p (u s) -> p s u", u=2)[:, lo:hi])
+
+        def second_product(lo, hi, bank, on_vector):
+            nc.vector.quantize_mx(out=z_words[:, lo:hi].bitcast(FP8X4), scales=z_scales[:, lo:hi], in_=z_bf[lo][:])
+            acc = psum.tile([P, HALF], F32, name=f"acc{lo}", tag=bank)
+            nc.tensor.matmul_mx(out=acc[:, :hi - lo], lhsT=w2_w[:].bitcast(FP8X4), lhsT_scale=w2_sc[:], rhs=z_words[:, lo:hi].bitcast(FP8X4), rhs_scale=z_scales[:, lo:hi], start=True, stop=True)
+            res = keep.tile([P, hi - lo], F32, name=f"res{lo}")
+            if on_vector:
+                nc.vector.tensor_copy(out=res[:], in_=acc[:, :hi - lo])
+            else:
+                nc.scalar.copy(out=res[:], in_=acc[:, :hi - lo])
+            nc.sync.dma_start(out=out[:, lo:hi], in_=res[:])
+
+        for t in range(PACK):
+            centre(t, 768, 1024, False)
+        for t in range(PACK):
+            centre(t, 0, 256)
+        for t in range(PACK):
+            centre(t, 256, 768)
+        pieces = [(0, 256), (768, 1024), (256, 512), (512, 640), (640, 768)]
+        for lo, hi in pieces:
+            weave(lo, hi)
+        for i, (lo, hi) in enumerate(pieces):
+            second_product(lo, hi, f"bank{i % 4}_{i // 4}", i >= 3)

@@ -23,9 +23,11 @@ HALF = 512
 HALVES = S // HALF
 LIST_COLS = HALF // 16
 OUT_CHUNK = 256
-X_CHUNKS = [[512, 512, 512, 512], [512, 512, 512, 256, 256]]
+X_CHUNKS = [[1024, 512, 512], [1024, 512, 256, 256]]
+X_UNIT = 512
 W_CHUNKS = [[256, 256], [256, 128, 128]]
-WARM = 16
+WARM = 3
+Z_SPLIT = 640
 
 
 def tile_picked_deepset_relu_e_kernel(tc, xT, w1, w2_words, w2_scales, offs, out):
@@ -61,26 +63,23 @@ def tile_picked_deepset_relu_e_kernel(tc, xT, w1, w2_words, w2_scales, offs, out
                 nc.sync.dma_start(out=raw[:], in_=w1[g * K_PASS:(g + 1) * K_PASS, c0:c0 + width].rearrange("(p j) w -> p j w", j=PACK))
                 w_raw[g, b] = (raw, c0, width)
                 c0 = c0 + width
-                if g == 0 and b == 0:
-                    nc.sync.dma_start(out=w2_w[:].bitcast(I32), in_=w2_words[0].rearrange("p n t -> p (n t)").bitcast(I32))
+
+        nc.sync.dma_start(out=w2_w[:].bitcast(I32), in_=w2_words[0].rearrange("p n t -> p (n t)").bitcast(I32))
 
         x_words = [keep.tile([P, T], U32, name=f"x_words{g}", align_bytes=64) for g in range(PASSES)]
         g_words = {}
         g_scales = {}
 
-        def round_x(g, c):
-            raw, c0, width = x_raw[g, c]
-            grouped = keep.tile([P, width * PACK], BF16, name=f"x_bf{g}_{c}", align_bytes=64)
+        def quantise_x(g, c, u0, width, scalar_share):
+            raw, c0, load_width = x_raw[g, c]
+            grouped = keep.tile([P, width * PACK], BF16, name=f"x_bf{g}_{c}_{u0}", align_bytes=64)
             dst = grouped[:].rearrange("p (c i j) -> p c j i", i=4, j=PACK)
-            src = raw[:].rearrange("p j (c i) -> p c j i", i=4)
-            split = (width * 5 // 8 if width == 512 else width // 2) // 4
+            src = raw[:, :, u0:u0 + width].rearrange("p j (c i) -> p c j i", i=4)
+            split = scalar_share // 4
             nc.scalar.activation(out=dst[:, :split], in_=src[:, :split], func=ACT.Copy)
             nc.vector.tensor_copy(out=dst[:, split:], in_=src[:, split:])
-            return grouped
-
-        def quantise_x(g, c, grouped):
-            raw, c0, width = x_raw[g, c]
-            nc.vector.quantize_mx(out=x_words[g][:, c0:c0 + width].bitcast(FP8X4), scales=x_scales[4 * g:, c0:c0 + width], in_=grouped[:])
+            lo = c0 + u0
+            nc.vector.quantize_mx(out=x_words[g][:, lo:lo + width].bitcast(FP8X4), scales=x_scales[4 * g:, lo:lo + width], in_=grouped[:])
 
         def gather_words(g, a):
             picked = keep.tile([P, HALF], U32, name=f"g_words{g}_{a}", tag=(f"w_bf{a}" if g == 1 else f"g_words{a}"), align_bytes=64)
@@ -93,10 +92,13 @@ def tile_picked_deepset_relu_e_kernel(tc, xT, w1, w2_words, w2_scales, offs, out
             g_scales[a] = picked
 
         for g in range(PASSES):
-            for c in range(len(X_CHUNKS[g])):
-                quantise_x(g, c, round_x(g, c))
-                if g == 1 and c < HALVES:
-                    gather_words(0, c)
+            for c, load_width in enumerate(X_CHUNKS[g]):
+                width = min(load_width, X_UNIT)
+                for u0 in range(0, load_width, width):
+                    quantise_x(g, c, u0, width, width * 9 // 16 if width == X_UNIT else width // 2)
+            if g == 0:
+                gather_words(0, 0)
+                gather_words(0, 1)
 
         w_bf = [keep.tile([P, H * PACK], BF16, name=f"w_bf{g}", tag=f"w_bf{g}", align_bytes=64) for g in range(PASSES)]
         w_words = [keep.tile([P, H], U32, name=f"w_words{g}", align_bytes=64) for g in range(PASSES)]
@@ -121,9 +123,9 @@ def tile_picked_deepset_relu_e_kernel(tc, xT, w1, w2_words, w2_scales, offs, out
             nc.tensor.matmul_mx(out=banks[t, a][:], lhsT=w_words[g][:, t * P:(t + 1) * P].bitcast(FP8X4), lhsT_scale=w_scales[g][:, t * P:(t + 1) * P],
                                 rhs=g_words[g, a][:].bitcast(FP8X4), rhs_scale=g_scales[a][4 * g:, :], start=(g == 0), stop=(g == PASSES - 1))
 
-        for i in range(WARM):
-            nc.tensor.matmul_mx(out=banks[3, 1][:, (i % 4) * N:(i % 4 + 1) * N], lhsT=w2_w[:].bitcast(FP8X4), lhsT_scale=w2_sc[:], rhs=w2_w[:].bitcast(FP8X4), rhs_scale=w2_sc[:], start=True, stop=True)
         gather_scales(0)
+        for i in range(WARM):
+            nc.tensor.matmul_mx(out=banks[3, 1][:], lhsT=g_words[0, 0][:, :P].bitcast(FP8X4), lhsT_scale=g_scales[0][:, :P], rhs=g_words[0, 0][:].bitcast(FP8X4), rhs_scale=g_scales[0][:], start=True, stop=True)
         gather_scales(1)
         round_w(0)
         quantise_w(0)
@@ -138,27 +140,19 @@ def tile_picked_deepset_relu_e_kernel(tc, xT, w1, w2_words, w2_scales, offs, out
             for t in range(PACK):
                 first_product(1, t, a)
 
-        h = [keep.tile([P, S], F32, name=f"h{t}") for t in range(PACK)]
-        sums = [keep.tile([P, HALVES], F32, name=f"sums{t}") for t in range(PACK)]
-        neg_mean = [keep.tile([P, 1], F32, name=f"neg_mean{t}") for t in range(PACK)]
-        z_all = keep.tile([P, 2 * S * 2], BF16, name="z_all")
-        z_pairs = [z_all[:, u * 2 * S:(u + 1) * 2 * S].rearrange("p (s e) -> p s e", e=2) for u in range(2)]
+        h = keep.tile([P, PACK, S], F32, name="h")
+        sums = keep.tile([P, PACK, HALVES], F32, name="sums")
+        neg_mean = keep.tile([P, PACK], F32, name="neg_mean")
 
         def relu_out(t, a, on_vector):
-            dst = h[t][:, a * HALF:(a + 1) * HALF]
+            dst = h[:, t, a * HALF:(a + 1) * HALF]
             if on_vector:
-                nc.vector.tensor_scalar(out=dst, in0=banks[t, a][:], scalar1=0.0, scalar2=None, op0=ALU.max, op1=ALU.add, accum_out=sums[t][:, a:a + 1])
+                nc.vector.tensor_scalar(out=dst, in0=banks[t, a][:], scalar1=0.0, scalar2=None, op0=ALU.max, op1=ALU.add, accum_out=sums[:, t, a:a + 1])
             else:
-                nc.scalar.activation(out=dst, in_=banks[t, a][:], func=ACT.Relu, accum_out=sums[t][:, a:a + 1])
+                nc.scalar.activation(out=dst, in_=banks[t, a][:], func=ACT.Relu, accum_out=sums[:, t, a:a + 1])
 
         def mean(t):
-            nc.vector.tensor_scalar(out=neg_mean[t][:], in0=sums[t][:, 0:1], scalar1=sums[t][:, 1:2], scalar2=-1.0 / S, op0=ALU.add, op1=ALU.mult)
-
-        def centre(t, lo, hi, on_vector=True):
-            if on_vector:
-                nc.vector.tensor_scalar(out=z_pairs[t // 2][:, lo:hi, t % 2], in0=h[t][:, lo:hi], scalar1=neg_mean[t][:], scalar2=None, op0=ALU.add)
-            else:
-                nc.scalar.activation(out=z_pairs[t // 2][:, lo:hi, t % 2], in_=h[t][:, lo:hi], func=ACT.Identity, bias=neg_mean[t][:], scale=1.0)
+            nc.vector.tensor_scalar(out=neg_mean[:, t:t + 1], in0=sums[:, t, 0:1], scalar1=sums[:, t, 1:2], scalar2=-1.0 / S, op0=ALU.add, op1=ALU.mult)
 
         for t in range(PACK):
             relu_out(t, 0, False)
@@ -173,32 +167,41 @@ def tile_picked_deepset_relu_e_kernel(tc, xT, w1, w2_words, w2_scales, offs, out
 
         z_words = keep.tile([P, S], U32, name="z_words", align_bytes=64)
         z_scales = keep.tile([P, S], U8, name="z_scales", align_bytes=64)
-        z_bf = {}
+        chunks = S // OUT_CHUNK
+        z_bf = [keep.tile([P, OUT_CHUNK * PACK], BF16, name=f"z_bf{c}", align_bytes=64) for c in range(chunks)]
+        z_planes = keep.tile([P, PACK, S - Z_SPLIT], BF16, name="z_planes")
 
-        def weave(lo, hi):
-            z_bf[lo] = keep.tile([P, (hi - lo) * PACK], BF16, name=f"z_bf{lo}", align_bytes=64)
-            dst = z_bf[lo][:].bitcast(U32).rearrange("p (s u) -> p s u", u=2)
-            nc.scalar.copy(out=dst, in_=z_all[:].bitcast(U32).rearrange("p (u s) -> p s u", u=2)[:, lo:hi])
+        def z_view(lo, hi):
+            c = lo // OUT_CHUNK
+            return z_bf[c][:, (lo - c * OUT_CHUNK) * PACK:(hi - c * OUT_CHUNK) * PACK].rearrange("p (c i t) -> p c t i", i=4, t=PACK)
 
-        def second_product(lo, hi, bank, on_vector):
-            nc.vector.quantize_mx(out=z_words[:, lo:hi].bitcast(FP8X4), scales=z_scales[:, lo:hi], in_=z_bf[lo][:])
-            acc = psum.tile([P, HALF], F32, name=f"acc{lo}", tag=bank)
-            nc.tensor.matmul_mx(out=acc[:, :hi - lo], lhsT=w2_w[:].bitcast(FP8X4), lhsT_scale=w2_sc[:], rhs=z_words[:, lo:hi].bitcast(FP8X4), rhs_scale=z_scales[:, lo:hi], start=True, stop=True)
-            res = keep.tile([P, hi - lo], F32, name=f"res{lo}")
+        def centre_vector(lo, hi):
+            nc.vector.tensor_tensor(out=z_view(lo, hi), in0=h[:, :, lo:hi].rearrange("p t (c i) -> p c t i", i=4),
+                                    in1=neg_mean[:].unsqueeze(1).unsqueeze(3).to_broadcast([P, (hi - lo) // 4, PACK, 4]), op=ALU.add)
+
+        def weave_scalar(lo, hi):
+            nc.scalar.copy(out=z_view(lo, hi), in_=z_planes[:, :, lo - Z_SPLIT:hi - Z_SPLIT].rearrange("p t (c i) -> p c t i", i=4))
+
+        def second_product(c, on_vector):
+            lo, hi = c * OUT_CHUNK, (c + 1) * OUT_CHUNK
+            nc.vector.quantize_mx(out=z_words[:, lo:hi].bitcast(FP8X4), scales=z_scales[:, lo:hi], in_=z_bf[c][:])
+            acc = psum.tile([P, HALF], F32, name=f"acc{c}", tag=f"bank{c}_0")
+            nc.tensor.matmul_mx(out=acc[:, :OUT_CHUNK], lhsT=w2_w[:].bitcast(FP8X4), lhsT_scale=w2_sc[:], rhs=z_words[:, lo:hi].bitcast(FP8X4), rhs_scale=z_scales[:, lo:hi], start=True, stop=True)
+            res = keep.tile([P, OUT_CHUNK], F32, name=f"res{c}")
             if on_vector:
-                nc.vector.tensor_copy(out=res[:], in_=acc[:, :hi - lo])
+                nc.vector.tensor_copy(out=res[:], in_=acc[:, :OUT_CHUNK])
             else:
-                nc.scalar.copy(out=res[:], in_=acc[:, :hi - lo])
+                nc.scalar.copy(out=res[:], in_=acc[:, :OUT_CHUNK])
             nc.sync.dma_start(out=out[:, lo:hi], in_=res[:])
 
         for t in range(PACK):
-            centre(t, 768, 1024, False)
-        for t in range(PACK):
-            centre(t, 0, 256)
-        for t in range(PACK):
-            centre(t, 256, 768)
-        pieces = [(0, 256), (768, 1024), (256, 512), (512, 640), (640, 768)]
-        for lo, hi in pieces:
-            weave(lo, hi)
-        for i, (lo, hi) in enumerate(pieces):
-            second_product(lo, hi, f"bank{i % 4}_{i // 4}", i >= 3)
+            nc.scalar.activation(out=z_planes[:, t, :], in_=h[:, t, Z_SPLIT:], func=ACT.Identity, bias=neg_mean[:, t:t + 1], scale=1.0)
+        weave_scalar(768, S)
+        weave_scalar(Z_SPLIT, 768)
+        centre_vector(0, 256)
+        centre_vector(256, 512)
+        second_product(0, False)
+        centre_vector(512, Z_SPLIT)
+        second_product(1, False)
+        second_product(3, False)
+        second_product(2, True)

@@ -22,12 +22,11 @@ PASSES = K // K_PASS
 HALF = 512
 HALVES = S // HALF
 LIST_COLS = HALF // 16
-OUT_CHUNK = 256
-X_CHUNKS = [[1024, 512, 512], [1024, 512, 256, 256]]
-X_UNIT = 512
-W_CHUNKS = [[256, 256], [256, 128, 128]]
-WARM = 3
-Z_SPLIT = 640
+X_LOADS = [[1024, 1024], [1024, 512, 512]]
+SCALAR_SIXTEENTHS = [[8, 8], [10, 8, 8]]
+WARM = 4
+Z_SPLIT = 656
+Z_PIECES = [(0, 256), (256, 512), (512, 768), (768, 896), (896, 1024)]
 
 
 def tile_picked_deepset_relu_e_kernel(tc, xT, w1, w2_words, w2_scales, offs, out):
@@ -43,28 +42,24 @@ def tile_picked_deepset_relu_e_kernel(tc, xT, w1, w2_words, w2_scales, offs, out
         nc.vector.memset(w2_sc[:].bitcast(I32), 0)
         w2_w = keep.tile([P, N], U32, name="w2_w", align_bytes=64)
 
-        for q in range(4):
-            nc.scalar.dma_start(out=w2_sc[32 * q:32 * q + 4, :].bitcast(I32), in_=w2_scales[0, 4 * q:4 * q + 4, :].bitcast(I32))
         x_raw = {}
         for g in range(PASSES):
             c0 = 0
-            for c, width in enumerate(X_CHUNKS[g]):
+            for c, width in enumerate(X_LOADS[g]):
                 raw = keep.tile([P, PACK, width], F32, name=f"x_raw{g}_{c}")
                 nc.sync.dma_start(out=raw[:], in_=xT[g * K_PASS:(g + 1) * K_PASS, c0:c0 + width].rearrange("(p j) w -> p j w", j=PACK))
                 x_raw[g, c] = (raw, c0, width)
                 c0 = c0 + width
                 if g == 0 and c == 0:
                     nc.sync.dma_start(offsets[:], offs)
-        w_raw = {}
+        w_raw = []
         for g in range(PASSES):
-            c0 = 0
-            for b, width in enumerate(W_CHUNKS[g]):
-                raw = keep.tile([P, PACK, width], F32, name=f"w_raw{g}_{b}")
-                nc.sync.dma_start(out=raw[:], in_=w1[g * K_PASS:(g + 1) * K_PASS, c0:c0 + width].rearrange("(p j) w -> p j w", j=PACK))
-                w_raw[g, b] = (raw, c0, width)
-                c0 = c0 + width
-
+            raw = keep.tile([P, PACK * H], F32, name=f"w_raw{g}")
+            nc.sync.dma_start(out=raw[:], in_=w1[g * K_PASS:(g + 1) * K_PASS, :].rearrange("(p j) w -> p (j w)", j=PACK))
+            w_raw.append(raw)
         nc.sync.dma_start(out=w2_w[:].bitcast(I32), in_=w2_words[0].rearrange("p n t -> p (n t)").bitcast(I32))
+        for q in range(4):
+            nc.sync.dma_start(out=w2_sc[32 * q:32 * q + 4, :].bitcast(I32), in_=w2_scales[0, 4 * q:4 * q + 4, :].bitcast(I32))
 
         x_words = [keep.tile([P, T], U32, name=f"x_words{g}", align_bytes=64) for g in range(PASSES)]
         g_words = {}
@@ -82,7 +77,7 @@ def tile_picked_deepset_relu_e_kernel(tc, xT, w1, w2_words, w2_scales, offs, out
             nc.vector.quantize_mx(out=x_words[g][:, lo:lo + width].bitcast(FP8X4), scales=x_scales[4 * g:, lo:lo + width], in_=grouped[:])
 
         def gather_words(g, a):
-            picked = keep.tile([P, HALF], U32, name=f"g_words{g}_{a}", tag=(f"w_bf{a}" if g == 1 else f"g_words{a}"), align_bytes=64)
+            picked = keep.tile([P, HALF], U32, name=f"g_words{g}_{a}", tag=("w_bf0" if (g, a) == (1, 1) else f"g_words{g}_{a}"), align_bytes=64)
             nc.vector.tensor_copy(out=picked[:], in_=x_words[g][:].indirect(offsets[:, a * LIST_COLS:(a + 1) * LIST_COLS]))
             g_words[g, a] = picked
 
@@ -92,10 +87,11 @@ def tile_picked_deepset_relu_e_kernel(tc, xT, w1, w2_words, w2_scales, offs, out
             g_scales[a] = picked
 
         for g in range(PASSES):
-            for c, load_width in enumerate(X_CHUNKS[g]):
-                width = min(load_width, X_UNIT)
+            for c, load_width in enumerate(X_LOADS[g]):
+                last = g == PASSES - 1 and c == len(X_LOADS[g]) - 1
+                width = 256 if last else 512
                 for u0 in range(0, load_width, width):
-                    quantise_x(g, c, u0, width, width * 9 // 16 if width == X_UNIT else width // 2)
+                    quantise_x(g, c, u0, width, width * SCALAR_SIXTEENTHS[g][c] // 16)
             if g == 0:
                 gather_words(0, 0)
                 gather_words(0, 1)
@@ -106,9 +102,7 @@ def tile_picked_deepset_relu_e_kernel(tc, xT, w1, w2_words, w2_scales, offs, out
 
         def round_w(g):
             dst = w_bf[g][:].rearrange("p (t m j) -> p m j t", t=PACK, j=PACK)
-            for b in range(len(W_CHUNKS[g])):
-                raw, c0, width = w_raw[g, b]
-                nc.scalar.activation(out=dst[:, c0 // PACK:(c0 + width) // PACK], in_=raw[:].rearrange("p j (m t) -> p m j t", t=PACK), func=ACT.Copy)
+            nc.scalar.activation(out=dst, in_=w_raw[g][:].rearrange("p (j m t) -> p m j t", j=PACK, t=PACK), func=ACT.Copy)
 
         def quantise_w(g):
             for t in range(PACK):
@@ -127,17 +121,17 @@ def tile_picked_deepset_relu_e_kernel(tc, xT, w1, w2_words, w2_scales, offs, out
         for i in range(WARM):
             nc.tensor.matmul_mx(out=banks[3, 1][:], lhsT=g_words[0, 0][:, :P].bitcast(FP8X4), lhsT_scale=g_scales[0][:, :P], rhs=g_words[0, 0][:].bitcast(FP8X4), rhs_scale=g_scales[0][:], start=True, stop=True)
         gather_scales(1)
+        gather_words(1, 0)
         round_w(0)
         quantise_w(0)
-        for a in range(HALVES):
-            for t in range(PACK):
+        for t in range(PACK):
+            for a in range(HALVES):
                 first_product(0, t, a)
-        gather_words(1, 0)
+        gather_words(1, 1)
         round_w(1)
         quantise_w(1)
-        gather_words(1, 1)
-        for a in range(HALVES):
-            for t in range(PACK):
+        for t in range(PACK):
+            for a in range(HALVES):
                 first_product(1, t, a)
 
         h = keep.tile([P, PACK, S], F32, name="h")
@@ -155,25 +149,21 @@ def tile_picked_deepset_relu_e_kernel(tc, xT, w1, w2_words, w2_scales, offs, out
             nc.vector.tensor_scalar(out=neg_mean[:, t:t + 1], in0=sums[:, t, 0:1], scalar1=sums[:, t, 1:2], scalar2=-1.0 / S, op0=ALU.add, op1=ALU.mult)
 
         for t in range(PACK):
-            relu_out(t, 0, False)
-        relu_out(0, 1, True)
-        relu_out(1, 1, True)
-        relu_out(2, 1, False)
-        mean(0)
-        mean(1)
-        relu_out(3, 1, True)
-        mean(2)
-        mean(3)
+            relu_out(t, 0, True)
+            relu_out(t, 1, False)
+        for t in range(PACK):
+            mean(t)
 
         z_words = keep.tile([P, S], U32, name="z_words", align_bytes=64)
         z_scales = keep.tile([P, S], U8, name="z_scales", align_bytes=64)
-        chunks = S // OUT_CHUNK
-        z_bf = [keep.tile([P, OUT_CHUNK * PACK], BF16, name=f"z_bf{c}", align_bytes=64) for c in range(chunks)]
+        z_bf = {}
+        for lo, hi in Z_PIECES:
+            z_bf[lo] = keep.tile([P, (hi - lo) * PACK], BF16, name=f"z_bf{lo}", align_bytes=64)
         z_planes = keep.tile([P, PACK, S - Z_SPLIT], BF16, name="z_planes")
 
         def z_view(lo, hi):
-            c = lo // OUT_CHUNK
-            return z_bf[c][:, (lo - c * OUT_CHUNK) * PACK:(hi - c * OUT_CHUNK) * PACK].rearrange("p (c i t) -> p c t i", i=4, t=PACK)
+            base = max(b for b in z_bf if b <= lo)
+            return z_bf[base][:, (lo - base) * PACK:(hi - base) * PACK].rearrange("p (c i t) -> p c t i", i=4, t=PACK)
 
         def centre_vector(lo, hi):
             nc.vector.tensor_tensor(out=z_view(lo, hi), in0=h[:, :, lo:hi].rearrange("p t (c i) -> p c t i", i=4),
@@ -182,26 +172,28 @@ def tile_picked_deepset_relu_e_kernel(tc, xT, w1, w2_words, w2_scales, offs, out
         def weave_scalar(lo, hi):
             nc.scalar.copy(out=z_view(lo, hi), in_=z_planes[:, :, lo - Z_SPLIT:hi - Z_SPLIT].rearrange("p t (c i) -> p c t i", i=4))
 
-        def second_product(c, on_vector):
-            lo, hi = c * OUT_CHUNK, (c + 1) * OUT_CHUNK
-            nc.vector.quantize_mx(out=z_words[:, lo:hi].bitcast(FP8X4), scales=z_scales[:, lo:hi], in_=z_bf[c][:])
-            acc = psum.tile([P, HALF], F32, name=f"acc{c}", tag=f"bank{c}_0")
-            nc.tensor.matmul_mx(out=acc[:, :OUT_CHUNK], lhsT=w2_w[:].bitcast(FP8X4), lhsT_scale=w2_sc[:], rhs=z_words[:, lo:hi].bitcast(FP8X4), rhs_scale=z_scales[:, lo:hi], start=True, stop=True)
-            res = keep.tile([P, OUT_CHUNK], F32, name=f"res{c}")
+        def second_product(i, on_vector):
+            lo, hi = Z_PIECES[i]
+            nc.vector.quantize_mx(out=z_words[:, lo:hi].bitcast(FP8X4), scales=z_scales[:, lo:hi], in_=z_bf[lo][:])
+            acc = psum.tile([P, HALF], F32, name=f"acc{i}", tag=f"bank{i % PACK}_{i // PACK}")
+            nc.tensor.matmul_mx(out=acc[:, :hi - lo], lhsT=w2_w[:].bitcast(FP8X4), lhsT_scale=w2_sc[:], rhs=z_words[:, lo:hi].bitcast(FP8X4), rhs_scale=z_scales[:, lo:hi], start=True, stop=True)
+            res = keep.tile([P, hi - lo], F32, name=f"res{i}")
             if on_vector:
-                nc.vector.tensor_copy(out=res[:], in_=acc[:, :OUT_CHUNK])
+                nc.vector.tensor_copy(out=res[:], in_=acc[:, :hi - lo])
             else:
-                nc.scalar.copy(out=res[:], in_=acc[:, :OUT_CHUNK])
+                nc.scalar.copy(out=res[:], in_=acc[:, :hi - lo])
             nc.sync.dma_start(out=out[:, lo:hi], in_=res[:])
 
         for t in range(PACK):
             nc.scalar.activation(out=z_planes[:, t, :], in_=h[:, t, Z_SPLIT:], func=ACT.Identity, bias=neg_mean[:, t:t + 1], scale=1.0)
-        weave_scalar(768, S)
         weave_scalar(Z_SPLIT, 768)
+        weave_scalar(768, 896)
+        weave_scalar(896, S)
         centre_vector(0, 256)
         centre_vector(256, 512)
         second_product(0, False)
         centre_vector(512, Z_SPLIT)
         second_product(1, False)
+        second_product(2, False)
         second_product(3, False)
-        second_product(2, True)
+        second_product(4, True)

@@ -21,10 +21,10 @@ K_PASS = P * PACK
 PASSES = K // K_PASS
 HALF = 512
 HALVES = S // HALF
-LIST_COLS = HALF // 16
-X_LOADS = [[1024, 1024], [1024, 512, 512]]
-SCALAR_SIXTEENTHS = [[8, 8], [10, 8, 8]]
-WARM = 4
+X_LOADS = {(0, 0): [(2048, 704)], (0, 1): [(1024, 1024), (1024, 352)], (1, 0): [(2048, 512)], (1, 1): [(768, 768), (768, 768), (512, 384)]}
+SHARED = 128
+WARM = 2
+PAIR = 2
 Z_SPLIT = 656
 Z_PIECES = [(0, 256), (256, 512), (512, 768), (768, 896), (896, 1024)]
 
@@ -36,77 +36,101 @@ def tile_picked_deepset_relu_e_kernel(tc, xT, w1, w2_words, w2_scales, offs, out
         psum = ctx.enter_context(tc.psum_pool(name="psum", bufs=1))
 
         offsets = keep.tile([P, S // 16], U16, name="offsets")
-        x_scales = keep.tile([P, T], U8, name="x_scales", align_bytes=64)
-        nc.vector.memset(x_scales[:].bitcast(I32), 0)
         w2_sc = keep.tile([P, N], U8, name="w2_sc", align_bytes=64)
-        nc.vector.memset(w2_sc[:].bitcast(I32), 0)
+        nc.gpsimd.memset(w2_sc[:].bitcast(I32), 0)
+        for q in range(4):
+            nc.gpsimd.dma_start(out=w2_sc[32 * q:32 * q + 4, :].bitcast(I32), in_=w2_scales[0, 4 * q:4 * q + 4, :].bitcast(I32))
         w2_w = keep.tile([P, N], U32, name="w2_w", align_bytes=64)
 
         x_raw = {}
         for g in range(PASSES):
-            c0 = 0
-            for c, width in enumerate(X_LOADS[g]):
-                raw = keep.tile([P, PACK, width], F32, name=f"x_raw{g}_{c}")
-                nc.sync.dma_start(out=raw[:], in_=xT[g * K_PASS:(g + 1) * K_PASS, c0:c0 + width].rearrange("(p j) w -> p j w", j=PACK))
-                x_raw[g, c] = (raw, c0, width)
-                c0 = c0 + width
-                if g == 0 and c == 0:
+            rows = xT[g * K_PASS:(g + 1) * K_PASS, :].rearrange("(p j) w -> p j w", j=PACK)
+            for u in range(PAIR):
+                c0 = 0
+                for c, (width, share) in enumerate(X_LOADS[g, u]):
+                    raw = keep.tile([P, PAIR, width], F32, name=f"x_raw{g}_{u}_{c}", tag=f"x_raw{g}_{u}_{c}", align_bytes=64)
+                    nc.sync.dma_start(out=raw[:], in_=rows[:, PAIR * u:PAIR * (u + 1), c0:c0 + width])
+                    x_raw[g, u, c] = (raw, c0)
+                    c0 = c0 + width
+                if g == 0 and u == 0:
                     nc.sync.dma_start(offsets[:], offs)
         w_raw = []
         for g in range(PASSES):
             raw = keep.tile([P, PACK * H], F32, name=f"w_raw{g}")
             nc.sync.dma_start(out=raw[:], in_=w1[g * K_PASS:(g + 1) * K_PASS, :].rearrange("(p j) w -> p (j w)", j=PACK))
             w_raw.append(raw)
-        nc.sync.dma_start(out=w2_w[:].bitcast(I32), in_=w2_words[0].rearrange("p n t -> p (n t)").bitcast(I32))
-        for q in range(4):
-            nc.sync.dma_start(out=w2_sc[32 * q:32 * q + 4, :].bitcast(I32), in_=w2_scales[0, 4 * q:4 * q + 4, :].bitcast(I32))
+            if g == 0:
+                nc.sync.dma_start(out=w2_w[:].bitcast(I32), in_=w2_words[0].rearrange("p n t -> p (n t)").bitcast(I32))
 
-        x_words = [keep.tile([P, T], U32, name=f"x_words{g}", align_bytes=64) for g in range(PASSES)]
+        pairs = {}
+        for u in range(PAIR):
+            whole = keep.tile([P, T], U32, name=f"pairs0_{u}")
+            pairs[0, u] = whole[:]
+        ring = keep.tile([P, 2 * T - SHARED], U32, name="pairs1")
+        pairs[1, 0] = ring[:, T - SHARED:]
+        pairs[1, 1] = ring[:, :T]
+        picked = {(g, a): keep.tile([P, PAIR, HALF], U32, name=f"picked{g}_{a}") for g in range(PASSES) for a in range(HALVES)}
+        woven = {}
         g_words = {}
         g_scales = {}
 
-        def quantise_x(g, c, u0, width, scalar_share):
-            raw, c0, load_width = x_raw[g, c]
-            grouped = keep.tile([P, width * PACK], BF16, name=f"x_bf{g}_{c}_{u0}", align_bytes=64)
-            dst = grouped[:].rearrange("p (c i j) -> p c j i", i=4, j=PACK)
-            src = raw[:, :, u0:u0 + width].rearrange("p j (c i) -> p c j i", i=4)
-            split = scalar_share // 4
-            nc.scalar.activation(out=dst[:, :split], in_=src[:, :split], func=ACT.Copy)
-            nc.vector.tensor_copy(out=dst[:, split:], in_=src[:, split:])
-            lo = c0 + u0
-            nc.vector.quantize_mx(out=x_words[g][:, lo:lo + width].bitcast(FP8X4), scales=x_scales[4 * g:, lo:lo + width], in_=grouped[:])
+        def round_pair(g, u):
+            both = pairs[g, u].bitcast(BF16).rearrange("p (w e) -> p w e", e=PAIR)
+            for c, (width, share) in enumerate(X_LOADS[g, u]):
+                raw, c0 = x_raw[g, u, c]
+                src = raw[:].rearrange("p e w -> p w e")
+                if share > 0:
+                    nc.scalar.activation(out=both[:, c0:c0 + share], in_=src[:, :share], func=ACT.Copy)
+                if share < width:
+                    nc.vector.tensor_copy(out=both[:, c0 + share:c0 + width], in_=src[:, share:])
 
-        def gather_words(g, a):
-            picked = keep.tile([P, HALF], U32, name=f"g_words{g}_{a}", tag=("w_bf0" if (g, a) == (1, 1) else f"g_words{g}_{a}"), align_bytes=64)
-            nc.vector.tensor_copy(out=picked[:], in_=x_words[g][:].indirect(offsets[:, a * LIST_COLS:(a + 1) * LIST_COLS]))
-            g_words[g, a] = picked
+        def gather(g, u, a):
+            nc.vector.tensor_copy(out=picked[g, a][:, u, :], in_=pairs[g, u].indirect(offsets[:, a * HALF // 16:(a + 1) * HALF // 16]))
 
-        def gather_scales(a):
-            picked = keep.tile([P, HALF], U8, name=f"g_scales{a}", align_bytes=64)
-            nc.vector.tensor_copy(out=picked[:], in_=x_scales[:].indirect(offsets[:, a * LIST_COLS:(a + 1) * LIST_COLS]))
-            g_scales[a] = picked
-
-        for g in range(PASSES):
-            for c, load_width in enumerate(X_LOADS[g]):
-                last = g == PASSES - 1 and c == len(X_LOADS[g]) - 1
-                width = 256 if last else 512
-                for u0 in range(0, load_width, width):
-                    quantise_x(g, c, u0, width, width * SCALAR_SIXTEENTHS[g][c] // 16)
+        def weave(g, a, tag):
+            woven[g, a] = keep.tile([P, HALF * PAIR], U32, name=f"woven{g}_{a}", tag=tag, align_bytes=64)
+            dst = woven[g, a][:].rearrange("p (n u) -> p n u", u=PAIR)
+            src = picked[g, a][:].rearrange("p u n -> p n u")
             if g == 0:
-                gather_words(0, 0)
-                gather_words(0, 1)
+                nc.scalar.copy(out=dst, in_=src)
+            else:
+                nc.vector.tensor_copy(out=woven[g, a][:].bitcast(I32).rearrange("p (n u) -> p n u", u=PAIR),
+                                      in_=picked[g, a][:].bitcast(I32).rearrange("p u n -> p n u"))
 
-        w_bf = [keep.tile([P, H * PACK], BF16, name=f"w_bf{g}", tag=f"w_bf{g}", align_bytes=64) for g in range(PASSES)]
-        w_words = [keep.tile([P, H], U32, name=f"w_words{g}", align_bytes=64) for g in range(PASSES)]
-        w_scales = [keep.tile([P, H], U8, name=f"w_scales{g}", align_bytes=64) for g in range(PASSES)]
+        def quantise_x(g, a, tag):
+            g_words[g, a] = keep.tile([P, HALF], U32, name=f"g_words{g}_{a}", tag=tag, align_bytes=64)
+            g_scales[g, a] = keep.tile([P, HALF], U8, name=f"g_scales{g}_{a}", align_bytes=64)
+            nc.vector.quantize_mx(out=g_words[g, a][:].bitcast(FP8X4), scales=g_scales[g, a][:], in_=woven[g, a][:].bitcast(BF16))
 
-        def round_w(g):
-            dst = w_bf[g][:].rearrange("p (t m j) -> p m j t", t=PACK, j=PACK)
-            nc.scalar.activation(out=dst, in_=w_raw[g][:].rearrange("p (j m t) -> p m j t", j=PACK, t=PACK), func=ACT.Copy)
+        round_pair(0, 0)
+        gather(0, 0, 0)
+        gather(0, 0, 1)
+        round_pair(0, 1)
+        gather(0, 1, 0)
+        weave(0, 0, "woven0_0")
+        gather(0, 1, 1)
+        weave(0, 1, "woven0_1")
+        quantise_x(0, 0, "g_words0_0")
+        round_pair(1, 0)
+        quantise_x(0, 1, "x_raw1_0_0")
+        gather(1, 0, 0)
+        gather(1, 0, 1)
+        round_pair(1, 1)
+        gather(1, 1, 0)
+        gather(1, 1, 1)
+        weave(1, 0, "woven1_0")
 
-        def quantise_w(g):
-            for t in range(PACK):
-                nc.vector.quantize_mx(out=w_words[g][:, t * P:(t + 1) * P].bitcast(FP8X4), scales=w_scales[g][:, t * P:(t + 1) * P], in_=w_bf[g][:, t * K_PASS:(t + 1) * K_PASS])
+        w_words = {}
+        w_scales = {}
+
+        def quantise_w(g, u):
+            w_bf = keep.tile([P, PAIR * K_PASS], BF16, name=f"w_bf{g}_{u}", tag=f"w_bf{g}_{u}", align_bytes=64)
+            w_words[g, u] = keep.tile([P, PAIR * P], U32, name=f"w_words{g}_{u}", align_bytes=64)
+            w_scales[g, u] = keep.tile([P, PAIR * P], U8, name=f"w_scales{g}_{u}", align_bytes=64)
+            dst = w_bf[:].rearrange("p (t m j) -> p m j t", t=PAIR, j=PACK)
+            src = w_raw[g][:].rearrange("p (j m t) -> p m j t", j=PACK, t=PACK)
+            nc.scalar.activation(out=dst, in_=src[:, :, :, PAIR * u:PAIR * (u + 1)], func=ACT.Copy)
+            nc.vector.quantize_mx(out=w_words[g, u][:].bitcast(FP8X4), scales=w_scales[g, u][:], in_=w_bf[:])
 
         banks = {}
         for t in range(PACK):
@@ -114,25 +138,24 @@ def tile_picked_deepset_relu_e_kernel(tc, xT, w1, w2_words, w2_scales, offs, out
                 banks[t, a] = psum.tile([P, HALF], F32, name=f"bank{t}_{a}", tag=f"bank{t}_{a}")
 
         def first_product(g, t, a):
-            nc.tensor.matmul_mx(out=banks[t, a][:], lhsT=w_words[g][:, t * P:(t + 1) * P].bitcast(FP8X4), lhsT_scale=w_scales[g][:, t * P:(t + 1) * P],
-                                rhs=g_words[g, a][:].bitcast(FP8X4), rhs_scale=g_scales[a][4 * g:, :], start=(g == 0), stop=(g == PASSES - 1))
+            u, cols = t // PAIR, slice(t % PAIR * P, (t % PAIR + 1) * P)
+            nc.tensor.matmul_mx(out=banks[t, a][:], lhsT=w_words[g, u][:, cols].bitcast(FP8X4), lhsT_scale=w_scales[g, u][:, cols],
+                                rhs=g_words[g, a][:].bitcast(FP8X4), rhs_scale=g_scales[g, a][:], start=(g == 0), stop=(g == PASSES - 1))
 
-        gather_scales(0)
         for i in range(WARM):
-            nc.tensor.matmul_mx(out=banks[3, 1][:], lhsT=g_words[0, 0][:, :P].bitcast(FP8X4), lhsT_scale=g_scales[0][:, :P], rhs=g_words[0, 0][:].bitcast(FP8X4), rhs_scale=g_scales[0][:], start=True, stop=True)
-        gather_scales(1)
-        gather_words(1, 0)
-        round_w(0)
-        quantise_w(0)
+            nc.tensor.matmul_mx(out=banks[3, 1][:], lhsT=w2_w[:].bitcast(FP8X4), lhsT_scale=w2_sc[:], rhs=g_words[0, 0][:].bitcast(FP8X4), rhs_scale=g_scales[0, 0][:], start=True, stop=True)
+        quantise_w(0, 0)
+        quantise_x(1, 0, "w_bf0_0")
+        quantise_w(0, 1)
+        weave(1, 1, "w_bf0_1")
         for t in range(PACK):
             for a in range(HALVES):
                 first_product(0, t, a)
-        gather_words(1, 1)
-        round_w(1)
-        quantise_w(1)
-        for t in range(PACK):
-            for a in range(HALVES):
-                first_product(1, t, a)
+        quantise_w(1, 0)
+        quantise_x(1, 1, "w_bf1_0")
+        quantise_w(1, 1)
+        for t, a in [(0, 0), (1, 0), (0, 1), (1, 1), (2, 0), (2, 1), (3, 0), (3, 1)]:
+            first_product(1, t, a)
 
         h = keep.tile([P, PACK, S], F32, name="h")
         sums = keep.tile([P, PACK, HALVES], F32, name="sums")
@@ -148,9 +171,14 @@ def tile_picked_deepset_relu_e_kernel(tc, xT, w1, w2_words, w2_scales, offs, out
         def mean(t):
             nc.vector.tensor_scalar(out=neg_mean[:, t:t + 1], in0=sums[:, t, 0:1], scalar1=sums[:, t, 1:2], scalar2=-1.0 / S, op0=ALU.add, op1=ALU.mult)
 
-        for t in range(PACK):
-            relu_out(t, 0, True)
-            relu_out(t, 1, False)
+        relu_out(0, 0, False)
+        relu_out(1, 0, True)
+        relu_out(0, 1, False)
+        relu_out(1, 1, True)
+        relu_out(2, 0, False)
+        relu_out(2, 1, True)
+        relu_out(3, 0, True)
+        relu_out(3, 1, False)
         for t in range(PACK):
             mean(t)
 

@@ -21,8 +21,8 @@ K_PASS = P * PACK
 PASSES = K // K_PASS
 HALF = 512
 HALVES = S // HALF
-X_LOADS = {(0, 0): [(2048, 704)], (0, 1): [(1024, 1024), (1024, 352)], (1, 0): [(2048, 512)], (1, 1): [(768, 768), (768, 768), (512, 384)]}
-SHARED = 128
+X_LOADS = {(0, 0): [(2048, 704)], (0, 1): [(1024, 1024), (1024, 352)], (1, 0): [(2048, 512)], (1, 1): [(768, 768), (768, 768), (512, 288)]}
+SHARED = 224
 WARM = 2
 PAIR = 2
 Z_SPLIT = 656
@@ -69,7 +69,8 @@ def tile_picked_deepset_relu_e_kernel(tc, xT, w1, w2_words, w2_scales, offs, out
         ring = keep.tile([P, 2 * T - SHARED], U32, name="pairs1")
         pairs[1, 0] = ring[:, T - SHARED:]
         pairs[1, 1] = ring[:, :T]
-        picked = {(g, a): keep.tile([P, PAIR, HALF], U32, name=f"picked{g}_{a}") for g in range(PASSES) for a in range(HALVES)}
+        picked0 = [keep.tile([P, PAIR, HALF], U32, name=f"picked0_{a}") for a in range(HALVES)]
+        picked1 = keep.tile([P, PAIR, S], U32, name="picked1")
         woven = {}
         g_words = {}
         g_scales = {}
@@ -84,41 +85,42 @@ def tile_picked_deepset_relu_e_kernel(tc, xT, w1, w2_words, w2_scales, offs, out
                 if share < width:
                     nc.vector.tensor_copy(out=both[:, c0 + share:c0 + width], in_=src[:, share:])
 
-        def gather(g, u, a):
-            nc.vector.tensor_copy(out=picked[g, a][:, u, :], in_=pairs[g, u].indirect(offsets[:, a * HALF // 16:(a + 1) * HALF // 16]))
+        def gather_half(u, a):
+            nc.vector.tensor_copy(out=picked0[a][:, u, :], in_=pairs[0, u].indirect(offsets[:, a * HALF // 16:(a + 1) * HALF // 16]))
 
-        def weave(g, a, tag):
-            woven[g, a] = keep.tile([P, HALF * PAIR], U32, name=f"woven{g}_{a}", tag=tag, align_bytes=64)
-            dst = woven[g, a][:].rearrange("p (n u) -> p n u", u=PAIR)
-            src = picked[g, a][:].rearrange("p u n -> p n u")
-            if g == 0:
-                nc.scalar.copy(out=dst, in_=src)
-            else:
-                nc.vector.tensor_copy(out=woven[g, a][:].bitcast(I32).rearrange("p (n u) -> p n u", u=PAIR),
-                                      in_=picked[g, a][:].bitcast(I32).rearrange("p u n -> p n u"))
+        def gather_all(u):
+            nc.vector.tensor_copy(out=picked1[:, u, :], in_=pairs[1, u].indirect(offsets[:]))
+
+        def weave_half(a):
+            tile = keep.tile([P, HALF * PAIR], U32, name=f"woven0_{a}", align_bytes=64)
+            nc.scalar.copy(out=tile[:].rearrange("p (n u) -> p n u", u=PAIR), in_=picked0[a][:].rearrange("p u n -> p n u"))
+            woven[0, a] = tile[:]
+
+        def weave_all(tag):
+            tile = keep.tile([P, S * PAIR], U32, name="woven1", tag=tag, align_bytes=64)
+            nc.vector.tensor_copy(out=tile[:].bitcast(I32).rearrange("p (n u) -> p n u", u=PAIR), in_=picked1[:].bitcast(I32).rearrange("p u n -> p n u"))
+            for a in range(HALVES):
+                woven[1, a] = tile[:, a * HALF * PAIR:(a + 1) * HALF * PAIR]
 
         def quantise_x(g, a, tag):
             g_words[g, a] = keep.tile([P, HALF], U32, name=f"g_words{g}_{a}", tag=tag, align_bytes=64)
             g_scales[g, a] = keep.tile([P, HALF], U8, name=f"g_scales{g}_{a}", align_bytes=64)
-            nc.vector.quantize_mx(out=g_words[g, a][:].bitcast(FP8X4), scales=g_scales[g, a][:], in_=woven[g, a][:].bitcast(BF16))
+            nc.vector.quantize_mx(out=g_words[g, a][:].bitcast(FP8X4), scales=g_scales[g, a][:], in_=woven[g, a].bitcast(BF16))
 
         round_pair(0, 0)
-        gather(0, 0, 0)
-        gather(0, 0, 1)
+        gather_half(0, 0)
+        gather_half(0, 1)
         round_pair(0, 1)
-        gather(0, 1, 0)
-        weave(0, 0, "woven0_0")
-        gather(0, 1, 1)
-        weave(0, 1, "woven0_1")
+        gather_half(1, 0)
+        weave_half(0)
+        gather_half(1, 1)
+        weave_half(1)
         quantise_x(0, 0, "g_words0_0")
         round_pair(1, 0)
+        gather_all(0)
         quantise_x(0, 1, "x_raw1_0_0")
-        gather(1, 0, 0)
-        gather(1, 0, 1)
         round_pair(1, 1)
-        gather(1, 1, 0)
-        gather(1, 1, 1)
-        weave(1, 0, "woven1_0")
+        gather_all(1)
 
         w_words = {}
         w_scales = {}
@@ -145,9 +147,9 @@ def tile_picked_deepset_relu_e_kernel(tc, xT, w1, w2_words, w2_scales, offs, out
         for i in range(WARM):
             nc.tensor.matmul_mx(out=banks[3, 1][:], lhsT=w2_w[:].bitcast(FP8X4), lhsT_scale=w2_sc[:], rhs=g_words[0, 0][:].bitcast(FP8X4), rhs_scale=g_scales[0, 0][:], start=True, stop=True)
         quantise_w(0, 0)
-        quantise_x(1, 0, "w_bf0_0")
+        weave_all("w_bf0_0")
         quantise_w(0, 1)
-        weave(1, 1, "w_bf0_1")
+        quantise_x(1, 0, "w_bf0_1")
         for t in range(PACK):
             for a in range(HALVES):
                 first_product(0, t, a)

@@ -21,11 +21,11 @@ K_PASS = P * PACK
 PASSES = K // K_PASS
 HALF = 512
 HALVES = S // HALF
-X_LOADS = {(0, 0): [(2048, 704)], (0, 1): [(1024, 1024), (1024, 352)], (1, 0): [(2048, 512)], (1, 1): [(768, 768), (768, 768), (512, 288)]}
-SHARED = 224
+X_LOADS = {(0, 0): [(2048, 704)], (0, 1): [(1024, 1024), (1024, 352)], (1, 0): [(2048, 704)], (1, 1): [(1024, 1024), (1024, 512)]}
+SHARED = 512
 WARM = 2
 PAIR = 2
-Z_SPLIT = 656
+Z_SPLIT = 608
 Z_PIECES = [(0, 256), (256, 512), (512, 768), (768, 896), (896, 1024)]
 
 
@@ -37,10 +37,11 @@ def tile_picked_deepset_relu_e_kernel(tc, xT, w1, w2_words, w2_scales, offs, out
 
         offsets = keep.tile([P, S // 16], U16, name="offsets")
         w2_sc = keep.tile([P, N], U8, name="w2_sc", align_bytes=64)
-        nc.gpsimd.memset(w2_sc[:].bitcast(I32), 0)
-        for q in range(4):
-            nc.gpsimd.dma_start(out=w2_sc[32 * q:32 * q + 4, :].bitcast(I32), in_=w2_scales[0, 4 * q:4 * q + 4, :].bitcast(I32))
+        nc.vector.memset(w2_sc[:].bitcast(I32), 0)
         w2_w = keep.tile([P, N], U32, name="w2_w", align_bytes=64)
+
+        def load_scales(q):
+            nc.sync.dma_start(out=w2_sc[32 * q:32 * q + 4, :].bitcast(I32), in_=w2_scales[0, 4 * q:4 * q + 4, :].bitcast(I32))
 
         x_raw = {}
         for g in range(PASSES):
@@ -48,8 +49,12 @@ def tile_picked_deepset_relu_e_kernel(tc, xT, w1, w2_words, w2_scales, offs, out
             for u in range(PAIR):
                 c0 = 0
                 for c, (width, share) in enumerate(X_LOADS[g, u]):
-                    raw = keep.tile([P, PAIR, width], F32, name=f"x_raw{g}_{u}_{c}", tag=f"x_raw{g}_{u}_{c}", align_bytes=64)
-                    nc.sync.dma_start(out=raw[:], in_=rows[:, PAIR * u:PAIR * (u + 1), c0:c0 + width])
+                    lead = HALF if (g, u) == (1, 0) else 0
+                    flat = keep.tile([P, lead + PAIR * width], F32, name=f"x_raw{g}_{u}_{c}", align_bytes=64)
+                    if lead:
+                        third = flat
+                    raw = flat[:, lead:].rearrange("p (e w) -> p e w", e=PAIR)
+                    nc.sync.dma_start(out=raw, in_=rows[:, PAIR * u:PAIR * (u + 1), c0:c0 + width])
                     x_raw[g, u, c] = (raw, c0)
                     c0 = c0 + width
                 if g == 0 and u == 0:
@@ -60,7 +65,8 @@ def tile_picked_deepset_relu_e_kernel(tc, xT, w1, w2_words, w2_scales, offs, out
             nc.sync.dma_start(out=raw[:], in_=w1[g * K_PASS:(g + 1) * K_PASS, :].rearrange("(p j) w -> p (j w)", j=PACK))
             w_raw.append(raw)
             if g == 0:
-                nc.sync.dma_start(out=w2_w[:].bitcast(I32), in_=w2_words[0].rearrange("p n t -> p (n t)").bitcast(I32))
+                load_scales(0)
+        nc.sync.dma_start(out=w2_w[:].bitcast(I32), in_=w2_words[0].rearrange("p n t -> p (n t)").bitcast(I32))
 
         pairs = {}
         for u in range(PAIR):
@@ -71,7 +77,8 @@ def tile_picked_deepset_relu_e_kernel(tc, xT, w1, w2_words, w2_scales, offs, out
         pairs[1, 1] = ring[:, :T]
         picked0 = [keep.tile([P, PAIR, HALF], U32, name=f"picked0_{a}") for a in range(HALVES)]
         picked1 = keep.tile([P, PAIR, S], U32, name="picked1")
-        woven = {}
+        woven_first = keep.tile([P, HALF * PAIR], U32, name="woven_first", align_bytes=64)
+        woven = {(0, 0): woven_first[:], (0, 1): third[:, :HALF * PAIR].bitcast(U32)}
         g_words = {}
         g_scales = {}
 
@@ -79,7 +86,7 @@ def tile_picked_deepset_relu_e_kernel(tc, xT, w1, w2_words, w2_scales, offs, out
             both = pairs[g, u].bitcast(BF16).rearrange("p (w e) -> p w e", e=PAIR)
             for c, (width, share) in enumerate(X_LOADS[g, u]):
                 raw, c0 = x_raw[g, u, c]
-                src = raw[:].rearrange("p e w -> p w e")
+                src = raw.rearrange("p e w -> p w e")
                 if share > 0:
                     nc.scalar.activation(out=both[:, c0:c0 + share], in_=src[:, :share], func=ACT.Copy)
                 if share < width:
@@ -91,10 +98,8 @@ def tile_picked_deepset_relu_e_kernel(tc, xT, w1, w2_words, w2_scales, offs, out
         def gather_all(u):
             nc.vector.tensor_copy(out=picked1[:, u, :], in_=pairs[1, u].indirect(offsets[:]))
 
-        def weave_half(a):
-            tile = keep.tile([P, HALF * PAIR], U32, name=f"woven0_{a}", align_bytes=64)
-            nc.scalar.copy(out=tile[:].rearrange("p (n u) -> p n u", u=PAIR), in_=picked0[a][:].rearrange("p u n -> p n u"))
-            woven[0, a] = tile[:]
+        def weave_first(a, lo, hi):
+            nc.scalar.copy(out=woven[0, a].rearrange("p (n u) -> p n u", u=PAIR)[:, lo:hi], in_=picked0[a][:].rearrange("p u n -> p n u")[:, lo:hi])
 
         def weave_all(tag):
             tile = keep.tile([P, S * PAIR], U32, name="woven1", tag=tag, align_bytes=64)
@@ -112,13 +117,14 @@ def tile_picked_deepset_relu_e_kernel(tc, xT, w1, w2_words, w2_scales, offs, out
         gather_half(0, 1)
         round_pair(0, 1)
         gather_half(1, 0)
-        weave_half(0)
+        weave_first(0, 0, HALF)
         gather_half(1, 1)
-        weave_half(1)
+        weave_first(1, 0, HALF // 2)
         quantise_x(0, 0, "g_words0_0")
         round_pair(1, 0)
+        weave_first(1, HALF // 2, HALF)
         gather_all(0)
-        quantise_x(0, 1, "x_raw1_0_0")
+        quantise_x(0, 1, "g_words0_1")
         round_pair(1, 1)
         gather_all(1)
 
@@ -145,7 +151,9 @@ def tile_picked_deepset_relu_e_kernel(tc, xT, w1, w2_words, w2_scales, offs, out
                                 rhs=g_words[g, a][:].bitcast(FP8X4), rhs_scale=g_scales[g, a][:], start=(g == 0), stop=(g == PASSES - 1))
 
         for i in range(WARM):
-            nc.tensor.matmul_mx(out=banks[3, 1][:], lhsT=w2_w[:].bitcast(FP8X4), lhsT_scale=w2_sc[:], rhs=g_words[0, 0][:].bitcast(FP8X4), rhs_scale=g_scales[0, 0][:], start=True, stop=True)
+            nc.tensor.matmul_mx(out=banks[3, 1][:], lhsT=g_words[0, 0][:, :P].bitcast(FP8X4), lhsT_scale=w2_sc[:], rhs=g_words[0, 0][:].bitcast(FP8X4), rhs_scale=g_scales[0, 0][:], start=True, stop=True)
+        for q in range(1, 4):
+            load_scales(q)
         quantise_w(0, 0)
         weave_all("w_bf0_0")
         quantise_w(0, 1)
@@ -225,5 +233,5 @@ def tile_picked_deepset_relu_e_kernel(tc, xT, w1, w2_words, w2_scales, offs, out
         centre_vector(512, Z_SPLIT)
         second_product(1, False)
         second_product(2, False)
-        second_product(3, False)
+        second_product(3, True)
         second_product(4, True)

@@ -25,7 +25,7 @@ X_LOADS = {(0, 0): [(2048, 704)], (0, 1): [(1024, 1024), (1024, 352)], (1, 0): [
 SHARED = 512
 WARM = 2
 PAIR = 2
-Z_SPLIT = 608
+Z_SPLIT = 512
 Z_PIECES = [(0, 256), (256, 512), (512, 768), (768, 896), (896, 1024)]
 
 
@@ -61,7 +61,7 @@ def tile_picked_deepset_relu_e_kernel(tc, xT, w1, w2_words, w2_scales, offs, out
                     nc.sync.dma_start(offsets[:], offs)
         w_raw = []
         for g in range(PASSES):
-            raw = keep.tile([P, PACK * H], F32, name=f"w_raw{g}")
+            raw = keep.tile([P, PACK * H], F32, name=f"w_raw{g}", tag=f"w_raw{g}", align_bytes=64)
             nc.sync.dma_start(out=raw[:], in_=w1[g * K_PASS:(g + 1) * K_PASS, :].rearrange("(p j) w -> p (j w)", j=PACK))
             w_raw.append(raw)
             if g == 0:
@@ -157,7 +157,7 @@ def tile_picked_deepset_relu_e_kernel(tc, xT, w1, w2_words, w2_scales, offs, out
         quantise_w(0, 0)
         weave_all("w_bf0_0")
         quantise_w(0, 1)
-        quantise_x(1, 0, "w_bf0_1")
+        quantise_x(1, 0, "w_raw0")
         for t in range(PACK):
             for a in range(HALVES):
                 first_product(0, t, a)
@@ -181,23 +181,36 @@ def tile_picked_deepset_relu_e_kernel(tc, xT, w1, w2_words, w2_scales, offs, out
         def mean(t):
             nc.vector.tensor_scalar(out=neg_mean[:, t:t + 1], in0=sums[:, t, 0:1], scalar1=sums[:, t, 1:2], scalar2=-1.0 / S, op0=ALU.add, op1=ALU.mult)
 
+        z_planes = keep.tile([P, PACK, S - Z_SPLIT], BF16, name="z_planes")
+
+        def plane(t, on_vector):
+            if on_vector:
+                nc.vector.tensor_scalar(out=z_planes[:, t, :], in0=h[:, t, Z_SPLIT:], scalar1=neg_mean[:, t:t + 1], scalar2=None, op0=ALU.add)
+            else:
+                nc.scalar.activation(out=z_planes[:, t, :], in_=h[:, t, Z_SPLIT:], func=ACT.Identity, bias=neg_mean[:, t:t + 1], scale=1.0)
+
         relu_out(0, 0, False)
-        relu_out(1, 0, True)
-        relu_out(0, 1, False)
-        relu_out(1, 1, True)
-        relu_out(2, 0, False)
-        relu_out(2, 1, True)
+        relu_out(1, 0, False)
+        relu_out(0, 1, True)
+        relu_out(1, 1, False)
+        relu_out(2, 0, True)
+        relu_out(2, 1, False)
         relu_out(3, 0, True)
         relu_out(3, 1, False)
-        for t in range(PACK):
-            mean(t)
+        mean(0)
+        mean(1)
+        mean(2)
+        plane(0, True)
+        mean(3)
+        plane(1, True)
+        plane(2, False)
+        plane(3, False)
 
         z_words = keep.tile([P, S], U32, name="z_words", align_bytes=64)
         z_scales = keep.tile([P, S], U8, name="z_scales", align_bytes=64)
         z_bf = {}
         for lo, hi in Z_PIECES:
             z_bf[lo] = keep.tile([P, (hi - lo) * PACK], BF16, name=f"z_bf{lo}", align_bytes=64)
-        z_planes = keep.tile([P, PACK, S - Z_SPLIT], BF16, name="z_planes")
 
         def z_view(lo, hi):
             base = max(b for b in z_bf if b <= lo)
@@ -222,15 +235,12 @@ def tile_picked_deepset_relu_e_kernel(tc, xT, w1, w2_words, w2_scales, offs, out
                 nc.scalar.copy(out=res[:], in_=acc[:, :hi - lo])
             nc.sync.dma_start(out=out[:, lo:hi], in_=res[:])
 
-        for t in range(PACK):
-            nc.scalar.activation(out=z_planes[:, t, :], in_=h[:, t, Z_SPLIT:], func=ACT.Identity, bias=neg_mean[:, t:t + 1], scale=1.0)
         weave_scalar(Z_SPLIT, 768)
         weave_scalar(768, 896)
         weave_scalar(896, S)
         centre_vector(0, 256)
         centre_vector(256, 512)
         second_product(0, False)
-        centre_vector(512, Z_SPLIT)
         second_product(1, False)
         second_product(2, False)
         second_product(3, True)

@@ -21,8 +21,8 @@ K_PASS = P * PACK
 PASSES = K // K_PASS
 HALF = 512
 HALVES = S // HALF
-X_LOADS = {(0, 0): [(2048, 704)], (0, 1): [(1024, 1024), (1024, 352)], (1, 0): [(2048, 704)], (1, 1): [(1024, 1024), (1024, 512)]}
-SHARED = 512
+X_LAST = [(1280, 832), (768, 272)]
+SHARED = 1216
 WARM = 2
 PAIR = 2
 Z_SPLIT = 512
@@ -43,102 +43,104 @@ def tile_picked_deepset_relu_e_kernel(tc, xT, w1, w2_words, w2_scales, offs, out
         def load_scales(q):
             nc.sync.dma_start(out=w2_sc[32 * q:32 * q + 4, :].bitcast(I32), in_=w2_scales[0, 4 * q:4 * q + 4, :].bitcast(I32))
 
-        x_raw = {}
-        for g in range(PASSES):
-            rows = xT[g * K_PASS:(g + 1) * K_PASS, :].rearrange("(p j) w -> p j w", j=PACK)
-            for u in range(PAIR):
-                c0 = 0
-                for c, (width, share) in enumerate(X_LOADS[g, u]):
-                    lead = HALF if (g, u) == (1, 0) else 0
-                    flat = keep.tile([P, lead + PAIR * width], F32, name=f"x_raw{g}_{u}_{c}", align_bytes=64)
-                    if lead:
-                        third = flat
-                    raw = flat[:, lead:].rearrange("p (e w) -> p e w", e=PAIR)
-                    nc.sync.dma_start(out=raw, in_=rows[:, PAIR * u:PAIR * (u + 1), c0:c0 + width])
-                    x_raw[g, u, c] = (raw, c0)
-                    c0 = c0 + width
-                if g == 0 and u == 0:
-                    nc.sync.dma_start(offsets[:], offs)
-        w_raw = []
-        for g in range(PASSES):
+        def x_rows(g, u):
+            return xT[g * K_PASS:(g + 1) * K_PASS, :].rearrange("(p j) w -> p j w", j=PACK)[:, PAIR * u:PAIR * (u + 1), :]
+
+        x_tile = {}
+
+        def load_runs(g, u, cuts):
+            lead = HALF if (g, u) == (1, 0) else 0
+            whole = keep.tile([P, lead + PAIR * T], F32, name=f"x_raw{g}_{u}", align_bytes=64)
+            x_tile[g, u] = whole
+            flat = whole[:, lead:]
+            run = x_rows(g, u).rearrange("p e w -> p (e w)")
+            lo = 0
+            for done in cuts:
+                nc.sync.dma_start(out=flat[:, lo:T + done], in_=run[:, lo:T + done])
+                lo = T + done
+            return flat.rearrange("p (e w) -> p w e", e=PAIR)
+
+        def load_w(g):
             raw = keep.tile([P, PACK * H], F32, name=f"w_raw{g}", tag=f"w_raw{g}", align_bytes=64)
             nc.sync.dma_start(out=raw[:], in_=w1[g * K_PASS:(g + 1) * K_PASS, :].rearrange("(p j) w -> p (j w)", j=PACK))
-            w_raw.append(raw)
-            if g == 0:
-                load_scales(0)
+            return raw
+
+        x_raw = {}
+        w_raw = {}
+        x_raw[0, 0] = load_runs(0, 0, [T])
+        nc.sync.dma_start(offsets[:], offs)
+        x_raw[0, 1] = load_runs(0, 1, [768, T])
+        x_raw[1, 0] = load_runs(1, 0, [T])
+        w_raw[0] = load_w(0)
+        last = []
+        c0 = 0
+        for c, (width, share) in enumerate(X_LAST):
+            raw = keep.tile([P, PAIR, width], F32, name=f"x_last{c}", align_bytes=64)
+            nc.sync.dma_start(out=raw[:], in_=x_rows(1, 1)[:, :, c0:c0 + width])
+            last.append((raw[:].rearrange("p e w -> p w e"), c0, width, share))
+            c0 = c0 + width
+        w_raw[1] = load_w(1)
         nc.sync.dma_start(out=w2_w[:].bitcast(I32), in_=w2_words[0].rearrange("p n t -> p (n t)").bitcast(I32))
+        for q in range(4):
+            load_scales(q)
 
         pairs = {}
-        for u in range(PAIR):
-            whole = keep.tile([P, T], U32, name=f"pairs0_{u}")
-            pairs[0, u] = whole[:]
-        ring = keep.tile([P, 2 * T - SHARED], U32, name="pairs1")
-        pairs[1, 0] = ring[:, T - SHARED:]
-        pairs[1, 1] = ring[:, :T]
-        picked0 = [keep.tile([P, PAIR, HALF], U32, name=f"picked0_{a}") for a in range(HALVES)]
-        picked1 = keep.tile([P, PAIR, S], U32, name="picked1")
-        woven_first = keep.tile([P, HALF * PAIR], U32, name="woven_first", align_bytes=64)
-        woven = {(0, 0): woven_first[:], (0, 1): third[:, :HALF * PAIR].bitcast(U32)}
+        for g, u in [(0, 0), (0, 1)]:
+            whole = keep.tile([P, T], U32, name=f"pairs{g}_{u}")
+            pairs[g, u] = whole[:]
+        picked = {}
+        for g in range(PASSES):
+            for a in range(HALVES):
+                lead = PAIR * HALF - 16 if (g, a) == (1, 0) else 0
+                flat = keep.tile([P, 4 * HALF if lead else PAIR * HALF], U32, name=f"picked{g}_{a}", align_bytes=64)
+                picked[g, a] = flat[:, lead:lead + PAIR * HALF]
+                if lead:
+                    shared = flat
+        woven = {(1, 1): shared[:, :PAIR * HALF], (0, 1): x_tile[1, 0][:, :PAIR * HALF].bitcast(U32)}
         g_words = {}
         g_scales = {}
-
-        def round_pair(g, u):
-            both = pairs[g, u].bitcast(BF16).rearrange("p (w e) -> p w e", e=PAIR)
-            for c, (width, share) in enumerate(X_LOADS[g, u]):
-                raw, c0 = x_raw[g, u, c]
-                src = raw.rearrange("p e w -> p w e")
-                if share > 0:
-                    nc.scalar.activation(out=both[:, c0:c0 + share], in_=src[:, :share], func=ACT.Copy)
-                if share < width:
-                    nc.vector.tensor_copy(out=both[:, c0 + share:c0 + width], in_=src[:, share:])
-
-        def gather_half(u, a):
-            nc.vector.tensor_copy(out=picked0[a][:, u, :], in_=pairs[0, u].indirect(offsets[:, a * HALF // 16:(a + 1) * HALF // 16]))
-
-        def gather_all(u):
-            nc.vector.tensor_copy(out=picked1[:, u, :], in_=pairs[1, u].indirect(offsets[:]))
-
-        def weave_first(a, lo, hi):
-            nc.scalar.copy(out=woven[0, a].rearrange("p (n u) -> p n u", u=PAIR)[:, lo:hi], in_=picked0[a][:].rearrange("p u n -> p n u")[:, lo:hi])
-
-        def weave_all(tag):
-            tile = keep.tile([P, S * PAIR], U32, name="woven1", tag=tag, align_bytes=64)
-            nc.vector.tensor_copy(out=tile[:].bitcast(I32).rearrange("p (n u) -> p n u", u=PAIR), in_=picked1[:].bitcast(I32).rearrange("p u n -> p n u"))
-            for a in range(HALVES):
-                woven[1, a] = tile[:, a * HALF * PAIR:(a + 1) * HALF * PAIR]
-
-        def quantise_x(g, a, tag):
-            g_words[g, a] = keep.tile([P, HALF], U32, name=f"g_words{g}_{a}", tag=tag, align_bytes=64)
-            g_scales[g, a] = keep.tile([P, HALF], U8, name=f"g_scales{g}_{a}", align_bytes=64)
-            nc.vector.quantize_mx(out=g_words[g, a][:].bitcast(FP8X4), scales=g_scales[g, a][:], in_=woven[g, a].bitcast(BF16))
-
-        round_pair(0, 0)
-        gather_half(0, 0)
-        gather_half(0, 1)
-        round_pair(0, 1)
-        gather_half(1, 0)
-        weave_first(0, 0, HALF)
-        gather_half(1, 1)
-        weave_first(1, 0, HALF // 2)
-        quantise_x(0, 0, "g_words0_0")
-        round_pair(1, 0)
-        weave_first(1, HALF // 2, HALF)
-        gather_all(0)
-        quantise_x(0, 1, "g_words0_1")
-        round_pair(1, 1)
-        gather_all(1)
-
+        w_bf = {}
         w_words = {}
         w_scales = {}
 
-        def quantise_w(g, u):
-            w_bf = keep.tile([P, PAIR * K_PASS], BF16, name=f"w_bf{g}_{u}", tag=f"w_bf{g}_{u}", align_bytes=64)
-            w_words[g, u] = keep.tile([P, PAIR * P], U32, name=f"w_words{g}_{u}", align_bytes=64)
-            w_scales[g, u] = keep.tile([P, PAIR * P], U8, name=f"w_scales{g}_{u}", align_bytes=64)
-            dst = w_bf[:].rearrange("p (t m j) -> p m j t", t=PAIR, j=PACK)
+        def round_x(g, u, src, c0, lo, hi, on_vector):
+            dst = pairs[g, u].bitcast(BF16).rearrange("p (w e) -> p w e", e=PAIR)[:, c0 + lo:c0 + hi]
+            if on_vector:
+                nc.vector.tensor_copy(out=dst, in_=src[:, lo:hi])
+            else:
+                nc.scalar.activation(out=dst, in_=src[:, lo:hi], func=ACT.Copy)
+
+        def gather(g, u, a, lo=0, hi=HALF):
+            nc.vector.tensor_copy(out=picked[g, a][:, u * HALF + lo:u * HALF + hi], in_=pairs[g, u].indirect(offsets[:, (a * HALF + lo) // 16:(a * HALF + hi) // 16]))
+
+        def weave(g, a, on_vector, lo=0, hi=HALF):
+            if (g, a) not in woven:
+                tile = keep.tile([P, HALF * PAIR], U32, name=f"woven{g}_{a}", align_bytes=64)
+                woven[g, a] = tile[:]
+            if on_vector:
+                nc.vector.tensor_copy(out=woven[g, a].bitcast(I32).rearrange("p (n u) -> p n u", u=PAIR), in_=picked[g, a].bitcast(I32).rearrange("p (u n) -> p n u", u=PAIR))
+            else:
+                nc.scalar.copy(out=woven[g, a].rearrange("p (n u) -> p n u", u=PAIR)[:, lo:hi], in_=picked[g, a].rearrange("p (u n) -> p n u", u=PAIR)[:, lo:hi])
+
+        def quantise_x(g, a, tag=None):
+            g_words[g, a] = keep.tile([P, HALF], U32, name=f"g_words{g}_{a}", tag=tag or f"g_words{g}_{a}", align_bytes=64)
+            g_scales[g, a] = keep.tile([P, HALF], U8, name=f"g_scales{g}_{a}", align_bytes=64)
+            nc.vector.quantize_mx(out=g_words[g, a][:].bitcast(FP8X4), scales=g_scales[g, a][:], in_=woven[g, a].bitcast(BF16))
+
+        def round_w(g, u):
+            if g == 1:
+                w_bf[g, u] = shared[:, (PAIR + u) * HALF:(PAIR + u + 1) * HALF].bitcast(BF16)
+            else:
+                tile = keep.tile([P, PAIR * K_PASS], BF16, name=f"w_bf{g}_{u}", tag=f"w_bf{g}_{u}", align_bytes=64)
+                w_bf[g, u] = tile[:]
+            dst = w_bf[g, u].rearrange("p (t m j) -> p m j t", t=PAIR, j=PACK)
             src = w_raw[g][:].rearrange("p (j m t) -> p m j t", j=PACK, t=PACK)
             nc.scalar.activation(out=dst, in_=src[:, :, :, PAIR * u:PAIR * (u + 1)], func=ACT.Copy)
-            nc.vector.quantize_mx(out=w_words[g, u][:].bitcast(FP8X4), scales=w_scales[g, u][:], in_=w_bf[:])
+
+        def quantise_w(g, u):
+            w_words[g, u] = keep.tile([P, PAIR * P], U32, name=f"w_words{g}_{u}", align_bytes=64)
+            w_scales[g, u] = keep.tile([P, PAIR * P], U8, name=f"w_scales{g}_{u}", align_bytes=64)
+            nc.vector.quantize_mx(out=w_words[g, u][:].bitcast(FP8X4), scales=w_scales[g, u][:], in_=w_bf[g, u])
 
         banks = {}
         for t in range(PACK):
@@ -150,19 +152,54 @@ def tile_picked_deepset_relu_e_kernel(tc, xT, w1, w2_words, w2_scales, offs, out
             nc.tensor.matmul_mx(out=banks[t, a][:], lhsT=w_words[g, u][:, cols].bitcast(FP8X4), lhsT_scale=w_scales[g, u][:, cols],
                                 rhs=g_words[g, a][:].bitcast(FP8X4), rhs_scale=g_scales[g, a][:], start=(g == 0), stop=(g == PASSES - 1))
 
-        for i in range(WARM):
-            nc.tensor.matmul_mx(out=banks[3, 1][:], lhsT=g_words[0, 0][:, :P].bitcast(FP8X4), lhsT_scale=w2_sc[:], rhs=g_words[0, 0][:].bitcast(FP8X4), rhs_scale=g_scales[0, 0][:], start=True, stop=True)
-        for q in range(1, 4):
-            load_scales(q)
+        ring = keep.tile([P, 2 * T - SHARED], U32, name="pairs1")
+        pairs[1, 0] = ring[:, T - SHARED:]
+        pairs[1, 1] = ring[:, :T]
+        round_x(0, 0, x_raw[0, 0], 0, 0, 704, False)
+        round_x(0, 0, x_raw[0, 0], 0, 704, T, True)
+        gather(0, 0, 0)
+        gather(0, 0, 1)
+        round_x(0, 1, x_raw[0, 1], 0, 0, 768, False)
+        round_x(0, 1, x_raw[0, 1], 0, 768, 1120, False)
+        round_x(0, 1, x_raw[0, 1], 0, 1120, T, True)
+        gather(0, 1, 0)
+        weave(0, 0, False)
+        gather(0, 1, 1)
+        weave(0, 1, False, 0, HALF // 2)
+        quantise_x(0, 0)
+        round_x(1, 0, x_raw[1, 0], 0, 0, 704, False)
+        round_x(1, 0, x_raw[1, 0], 0, 704, T, True)
+        weave(0, 1, False, HALF // 2, HALF)
+        gather(1, 0, 0)
+        gather(1, 0, 1)
+        quantise_x(0, 1)
+        round_w(0, 0)
+        round_w(0, 1)
         quantise_w(0, 0)
-        weave_all("w_bf0_0")
         quantise_w(0, 1)
-        quantise_x(1, 0, "w_raw0")
+        for src, c0, width, share in last:
+            round_x(1, 1, src, c0, 0, share, False)
+            if share < width:
+                round_x(1, 1, src, c0, share, width, True)
+        gather(1, 1, 0, HALF // 2, HALF)
+        weave(1, 0, False, HALF // 2, HALF)
+        gather(1, 1, 0, 0, HALF // 2)
+        weave(1, 0, False, 0, HALF // 2)
+        gather(1, 1, 1)
         for t in range(PACK):
             for a in range(HALVES):
-                first_product(0, t, a)
+                if (t, a) not in [(2, 1), (3, 1)]:
+                    first_product(0, t, a)
+        for t in range(PACK - WARM, PACK):
+            nc.tensor.matmul_mx(out=banks[t, 1][:], lhsT=w2_w[:].bitcast(FP8X4), lhsT_scale=g_scales[0, 0][:, :P], rhs=g_words[0, 0][:].bitcast(FP8X4), rhs_scale=g_scales[0, 0][:], start=True, stop=True)
+        for t in range(PACK - WARM, PACK):
+            first_product(0, t, 1)
+        round_w(1, 0)
+        round_w(1, 1)
+        quantise_x(1, 0)
+        weave(1, 1, True)
         quantise_w(1, 0)
-        quantise_x(1, 1, "w_bf1_0")
+        quantise_x(1, 1)
         quantise_w(1, 1)
         for t, a in [(0, 0), (1, 0), (0, 1), (1, 1), (2, 0), (2, 1), (3, 0), (3, 1)]:
             first_product(1, t, a)

@@ -21,9 +21,9 @@ K_PASS = P * PACK
 PASSES = K // K_PASS
 HALF = 512
 HALVES = S // HALF
-X_LAST = [(1280, 832), (768, 272)]
-SHARED = 1216
-WARM = 2
+X_SECOND = [(1024, 1024), (1024, 352)]
+X_LAST = [(960, 960), (704, 0), (384, 128)]
+SHARED = T - X_LAST[0][0]
 PAIR = 2
 Z_SPLIT = 512
 Z_PIECES = [(0, 256), (256, 512), (512, 768), (768, 896), (896, 1024)]
@@ -33,6 +33,7 @@ def tile_picked_deepset_relu_e_kernel(tc, xT, w1, w2_words, w2_scales, offs, out
     nc = tc.nc
     with ExitStack() as ctx:
         keep = ctx.enter_context(tc.tile_pool(name="keep", bufs=1))
+        turns = ctx.enter_context(tc.tile_pool(name="turns", bufs=1))
         psum = ctx.enter_context(tc.psum_pool(name="psum", bufs=1))
 
         offsets = keep.tile([P, S // 16], U16, name="offsets")
@@ -60,6 +61,16 @@ def tile_picked_deepset_relu_e_kernel(tc, xT, w1, w2_words, w2_scales, offs, out
                 lo = T + done
             return flat.rearrange("p (e w) -> p w e", e=PAIR)
 
+        def load_columns(g, u, pieces):
+            loaded = []
+            c0 = 0
+            for c, (width, share) in enumerate(pieces):
+                raw = keep.tile([P, PAIR, width], F32, name=f"x_raw{g}_{u}_{c}", align_bytes=64)
+                nc.sync.dma_start(out=raw[:], in_=x_rows(g, u)[:, :, c0:c0 + width])
+                loaded.append((raw[:].rearrange("p e w -> p w e"), c0, width, share))
+                c0 = c0 + width
+            return loaded
+
         def load_w(g):
             raw = keep.tile([P, PACK * H], F32, name=f"w_raw{g}", tag=f"w_raw{g}", align_bytes=64)
             nc.sync.dma_start(out=raw[:], in_=w1[g * K_PASS:(g + 1) * K_PASS, :].rearrange("(p j) w -> p (j w)", j=PACK))
@@ -69,16 +80,10 @@ def tile_picked_deepset_relu_e_kernel(tc, xT, w1, w2_words, w2_scales, offs, out
         w_raw = {}
         x_raw[0, 0] = load_runs(0, 0, [T])
         nc.sync.dma_start(offsets[:], offs)
-        x_raw[0, 1] = load_runs(0, 1, [768, T])
+        x_raw[0, 1] = load_columns(0, 1, X_SECOND)
         x_raw[1, 0] = load_runs(1, 0, [T])
         w_raw[0] = load_w(0)
-        last = []
-        c0 = 0
-        for c, (width, share) in enumerate(X_LAST):
-            raw = keep.tile([P, PAIR, width], F32, name=f"x_last{c}", align_bytes=64)
-            nc.sync.dma_start(out=raw[:], in_=x_rows(1, 1)[:, :, c0:c0 + width])
-            last.append((raw[:].rearrange("p e w -> p w e"), c0, width, share))
-            c0 = c0 + width
+        x_raw[1, 1] = load_columns(1, 1, X_LAST)
         w_raw[1] = load_w(1)
         nc.sync.dma_start(out=w2_w[:].bitcast(I32), in_=w2_words[0].rearrange("p n t -> p (n t)").bitcast(I32))
         for q in range(4):
@@ -91,15 +96,16 @@ def tile_picked_deepset_relu_e_kernel(tc, xT, w1, w2_words, w2_scales, offs, out
         picked = {}
         for g in range(PASSES):
             for a in range(HALVES):
-                lead = PAIR * HALF - 16 if (g, a) == (1, 0) else 0
-                flat = keep.tile([P, 4 * HALF if lead else PAIR * HALF], U32, name=f"picked{g}_{a}", align_bytes=64)
-                picked[g, a] = flat[:, lead:lead + PAIR * HALF]
-                if lead:
-                    shared = flat
-        woven = {(1, 1): shared[:, :PAIR * HALF], (0, 1): x_tile[1, 0][:, :PAIR * HALF].bitcast(U32)}
+                if (g, a) == (1, 0):
+                    flat = turns.tile([P, PAIR * HALF], U32, name="picked1_0", align_bytes=64, offset=4096 - 64)
+                else:
+                    flat = keep.tile([P, PAIR * HALF], U32, name=f"picked{g}_{a}", align_bytes=64)
+                picked[g, a] = flat[:]
+        woven = {(0, 1): x_tile[1, 0][:, :PAIR * HALF].bitcast(U32)}
         g_words = {}
         g_scales = {}
         w_bf = {}
+        w_bf_first = keep.tile([P, PACK * K_PASS], BF16, name="w_bf_first", align_bytes=64)
         w_words = {}
         w_scales = {}
 
@@ -110,10 +116,20 @@ def tile_picked_deepset_relu_e_kernel(tc, xT, w1, w2_words, w2_scales, offs, out
             else:
                 nc.scalar.activation(out=dst, in_=src[:, lo:hi], func=ACT.Copy)
 
+        def round_pieces(g, u):
+            for src, c0, width, share in x_raw[g, u]:
+                if share > 0:
+                    round_x(g, u, src, c0, 0, share, False)
+                if share < width:
+                    round_x(g, u, src, c0, share, width, True)
+
         def gather(g, u, a, lo=0, hi=HALF):
             nc.vector.tensor_copy(out=picked[g, a][:, u * HALF + lo:u * HALF + hi], in_=pairs[g, u].indirect(offsets[:, (a * HALF + lo) // 16:(a * HALF + hi) // 16]))
 
         def weave(g, a, on_vector, lo=0, hi=HALF):
+            if (g, a) == (1, 1):
+                tile = turns.tile([P, HALF * PAIR], U32, name="woven1_1", align_bytes=64, offset=0)
+                woven[g, a] = tile[:]
             if (g, a) not in woven:
                 tile = keep.tile([P, HALF * PAIR], U32, name=f"woven{g}_{a}", align_bytes=64)
                 woven[g, a] = tile[:]
@@ -122,17 +138,20 @@ def tile_picked_deepset_relu_e_kernel(tc, xT, w1, w2_words, w2_scales, offs, out
             else:
                 nc.scalar.copy(out=woven[g, a].rearrange("p (n u) -> p n u", u=PAIR)[:, lo:hi], in_=picked[g, a].rearrange("p (u n) -> p n u", u=PAIR)[:, lo:hi])
 
-        def quantise_x(g, a, tag=None):
-            g_words[g, a] = keep.tile([P, HALF], U32, name=f"g_words{g}_{a}", tag=tag or f"g_words{g}_{a}", align_bytes=64)
+        def quantise_x(g, a):
+            if (g, a) == (1, 1):
+                g_words[g, a] = turns.tile([P, HALF], U32, name="g_words1_1", align_bytes=64, offset=4096)
+            else:
+                g_words[g, a] = keep.tile([P, HALF], U32, name=f"g_words{g}_{a}", align_bytes=64)
             g_scales[g, a] = keep.tile([P, HALF], U8, name=f"g_scales{g}_{a}", align_bytes=64)
             nc.vector.quantize_mx(out=g_words[g, a][:].bitcast(FP8X4), scales=g_scales[g, a][:], in_=woven[g, a].bitcast(BF16))
 
         def round_w(g, u):
             if g == 1:
-                w_bf[g, u] = shared[:, (PAIR + u) * HALF:(PAIR + u + 1) * HALF].bitcast(BF16)
-            else:
-                tile = keep.tile([P, PAIR * K_PASS], BF16, name=f"w_bf{g}_{u}", tag=f"w_bf{g}_{u}", align_bytes=64)
+                tile = turns.tile([P, PAIR * K_PASS], BF16, name=f"w_bf1_{u}", align_bytes=64, offset=4096 + 2048 * u)
                 w_bf[g, u] = tile[:]
+            else:
+                w_bf[g, u] = w_bf_first[:, u * PAIR * K_PASS:(u + 1) * PAIR * K_PASS]
             dst = w_bf[g, u].rearrange("p (t m j) -> p m j t", t=PAIR, j=PACK)
             src = w_raw[g][:].rearrange("p (j m t) -> p m j t", j=PACK, t=PACK)
             nc.scalar.activation(out=dst, in_=src[:, :, :, PAIR * u:PAIR * (u + 1)], func=ACT.Copy)
@@ -141,6 +160,14 @@ def tile_picked_deepset_relu_e_kernel(tc, xT, w1, w2_words, w2_scales, offs, out
             w_words[g, u] = keep.tile([P, PAIR * P], U32, name=f"w_words{g}_{u}", align_bytes=64)
             w_scales[g, u] = keep.tile([P, PAIR * P], U8, name=f"w_scales{g}_{u}", align_bytes=64)
             nc.vector.quantize_mx(out=w_words[g, u][:].bitcast(FP8X4), scales=w_scales[g, u][:], in_=w_bf[g, u])
+
+        def quantise_w_first():
+            words = keep.tile([P, PACK * P], U32, name="w_words0", align_bytes=64)
+            scales = keep.tile([P, PACK * P], U8, name="w_scales0", align_bytes=64)
+            nc.vector.quantize_mx(out=words[:].bitcast(FP8X4), scales=scales[:], in_=w_bf_first[:])
+            for u in range(PAIR):
+                w_words[0, u] = words[:, u * PAIR * P:(u + 1) * PAIR * P]
+                w_scales[0, u] = scales[:, u * PAIR * P:(u + 1) * PAIR * P]
 
         banks = {}
         for t in range(PACK):
@@ -159,9 +186,7 @@ def tile_picked_deepset_relu_e_kernel(tc, xT, w1, w2_words, w2_scales, offs, out
         round_x(0, 0, x_raw[0, 0], 0, 704, T, True)
         gather(0, 0, 0)
         gather(0, 0, 1)
-        round_x(0, 1, x_raw[0, 1], 0, 0, 768, False)
-        round_x(0, 1, x_raw[0, 1], 0, 768, 1120, False)
-        round_x(0, 1, x_raw[0, 1], 0, 1120, T, True)
+        round_pieces(0, 1)
         gather(0, 1, 0)
         weave(0, 0, False)
         gather(0, 1, 1)
@@ -175,12 +200,8 @@ def tile_picked_deepset_relu_e_kernel(tc, xT, w1, w2_words, w2_scales, offs, out
         quantise_x(0, 1)
         round_w(0, 0)
         round_w(0, 1)
-        quantise_w(0, 0)
-        quantise_w(0, 1)
-        for src, c0, width, share in last:
-            round_x(1, 1, src, c0, 0, share, False)
-            if share < width:
-                round_x(1, 1, src, c0, share, width, True)
+        quantise_w_first()
+        round_pieces(1, 1)
         gather(1, 1, 0, HALF // 2, HALF)
         weave(1, 0, False, HALF // 2, HALF)
         gather(1, 1, 0, 0, HALF // 2)
@@ -190,13 +211,13 @@ def tile_picked_deepset_relu_e_kernel(tc, xT, w1, w2_words, w2_scales, offs, out
             for a in range(HALVES):
                 if (t, a) not in [(2, 1), (3, 1)]:
                     first_product(0, t, a)
-        for t in range(PACK - WARM, PACK):
-            nc.tensor.matmul_mx(out=banks[t, 1][:], lhsT=w2_w[:].bitcast(FP8X4), lhsT_scale=g_scales[0, 0][:, :P], rhs=g_words[0, 0][:].bitcast(FP8X4), rhs_scale=g_scales[0, 0][:], start=True, stop=True)
-        for t in range(PACK - WARM, PACK):
-            first_product(0, t, 1)
+        nc.tensor.matmul_mx(out=banks[2, 1][:], lhsT=w2_w[:].bitcast(FP8X4), lhsT_scale=g_scales[0, 0][:, :P], rhs=g_words[0, 0][:].bitcast(FP8X4), rhs_scale=g_scales[0, 0][:], start=True, stop=True)
+        first_product(0, 2, 1)
         round_w(1, 0)
         round_w(1, 1)
         quantise_x(1, 0)
+        nc.tensor.matmul_mx(out=banks[3, 1][:], lhsT=w2_w[:].bitcast(FP8X4), lhsT_scale=g_scales[0, 0][:, :P], rhs=g_words[1, 0][:].bitcast(FP8X4), rhs_scale=g_scales[1, 0][:], start=True, stop=True)
+        first_product(0, 3, 1)
         weave(1, 1, True)
         quantise_w(1, 0)
         quantise_x(1, 1)

@@ -211,12 +211,10 @@ def tile_picked_deepset_relu_e_kernel(tc, xT, w1, w2_words, w2_scales, offs, out
             for a in range(HALVES):
                 if (t, a) not in [(2, 1), (3, 1)]:
                     first_product(0, t, a)
-        nc.tensor.matmul_mx(out=banks[2, 1][:], lhsT=w2_w[:].bitcast(FP8X4), lhsT_scale=g_scales[0, 0][:, :P], rhs=g_words[0, 0][:].bitcast(FP8X4), rhs_scale=g_scales[0, 0][:], start=True, stop=True)
         first_product(0, 2, 1)
         round_w(1, 0)
         round_w(1, 1)
         quantise_x(1, 0)
-        nc.tensor.matmul_mx(out=banks[3, 1][:], lhsT=w2_w[:].bitcast(FP8X4), lhsT_scale=g_scales[0, 0][:, :P], rhs=g_words[1, 0][:].bitcast(FP8X4), rhs_scale=g_scales[1, 0][:], start=True, stop=True)
         first_product(0, 3, 1)
         weave(1, 1, True)
         quantise_w(1, 0)

@@ -21,19 +21,19 @@ K_PASS = P * PACK
 PASSES = K // K_PASS
 HALF = 512
 HALVES = S // HALF
-X_SECOND = [(1024, 1024), (1024, 352)]
-X_LAST = [(960, 960), (704, 0), (384, 128)]
-SHARED = T - X_LAST[0][0]
 PAIR = 2
-Z_SPLIT = 512
-Z_PIECES = [(0, 256), (256, 512), (512, 768), (768, 896), (896, 1024)]
+DIRECT = 256
+PIECES = [(256, 512), (512, 768), (768, 1024)]
+LAST_CUT = 96
+Z_SPLIT = 384
+Z_PIECES = [(0, 256), (256, 384), (384, 640), (640, 896), (896, 1024)]
+STORES = [(0, 384, False), (384, 640, False), (640, 896, True), (896, 1024, True)]
 
 
 def tile_picked_deepset_relu_e_kernel(tc, xT, w1, w2_words, w2_scales, offs, out):
     nc = tc.nc
     with ExitStack() as ctx:
         keep = ctx.enter_context(tc.tile_pool(name="keep", bufs=1))
-        turns = ctx.enter_context(tc.tile_pool(name="turns", bufs=1))
         psum = ctx.enter_context(tc.psum_pool(name="psum", bufs=1))
 
         offsets = keep.tile([P, S // 16], U16, name="offsets")
@@ -41,133 +41,80 @@ def tile_picked_deepset_relu_e_kernel(tc, xT, w1, w2_words, w2_scales, offs, out
         nc.vector.memset(w2_sc[:].bitcast(I32), 0)
         w2_w = keep.tile([P, N], U32, name="w2_w", align_bytes=64)
 
-        def load_scales(q):
-            nc.sync.dma_start(out=w2_sc[32 * q:32 * q + 4, :].bitcast(I32), in_=w2_scales[0, 4 * q:4 * q + 4, :].bitcast(I32))
-
-        def x_rows(g, u):
-            return xT[g * K_PASS:(g + 1) * K_PASS, :].rearrange("(p j) w -> p j w", j=PACK)[:, PAIR * u:PAIR * (u + 1), :]
-
-        x_tile = {}
-
-        def load_runs(g, u, cuts):
-            lead = HALF if (g, u) == (1, 0) else 0
-            whole = keep.tile([P, lead + PAIR * T], F32, name=f"x_raw{g}_{u}", align_bytes=64)
-            x_tile[g, u] = whole
-            flat = whole[:, lead:]
-            run = x_rows(g, u).rearrange("p e w -> p (e w)")
-            lo = 0
-            for done in cuts:
-                nc.sync.dma_start(out=flat[:, lo:T + done], in_=run[:, lo:T + done])
-                lo = T + done
-            return flat.rearrange("p (e w) -> p w e", e=PAIR)
-
-        def load_columns(g, u, pieces):
-            loaded = []
-            c0 = 0
-            for c, (width, share) in enumerate(pieces):
-                raw = keep.tile([P, PAIR, width], F32, name=f"x_raw{g}_{u}_{c}", align_bytes=64)
-                nc.sync.dma_start(out=raw[:], in_=x_rows(g, u)[:, :, c0:c0 + width])
-                loaded.append((raw[:].rearrange("p e w -> p w e"), c0, width, share))
-                c0 = c0 + width
-            return loaded
-
-        def load_w(g):
-            raw = keep.tile([P, PACK * H], F32, name=f"w_raw{g}", tag=f"w_raw{g}", align_bytes=64)
-            nc.sync.dma_start(out=raw[:], in_=w1[g * K_PASS:(g + 1) * K_PASS, :].rearrange("(p j) w -> p (j w)", j=PACK))
-            return raw
-
         x_raw = {}
         w_raw = {}
-        x_raw[0, 0] = load_runs(0, 0, [T])
+
+        def load_x(g, j):
+            x_raw[g, j] = keep.tile([P, T], F32, name=f"x_raw{g}_{j}", align_bytes=64)
+            nc.sync.dma_start(out=x_raw[g, j][:], in_=xT[g * K_PASS:(g + 1) * K_PASS, :].rearrange("(p j) w -> p j w", j=PACK)[:, j, :])
+
+        def load_w(g):
+            w_raw[g] = keep.tile([P, PACK * H], F32, name=f"w_raw{g}", align_bytes=64)
+            nc.sync.dma_start(out=w_raw[g][:], in_=w1[g * K_PASS:(g + 1) * K_PASS, :].rearrange("(p j) w -> p (j w)", j=PACK))
+
+        load_x(0, 0)
         nc.sync.dma_start(offsets[:], offs)
-        x_raw[0, 1] = load_columns(0, 1, X_SECOND)
-        x_raw[1, 0] = load_runs(1, 0, [T])
-        w_raw[0] = load_w(0)
-        x_raw[1, 1] = load_columns(1, 1, X_LAST)
-        w_raw[1] = load_w(1)
+        for g, j in [(0, 1), (0, 2), (0, 3), (1, 0), (1, 1), (1, 2)]:
+            load_x(g, j)
+        load_w(0)
+        load_x(1, 3)
+        load_w(1)
         nc.sync.dma_start(out=w2_w[:].bitcast(I32), in_=w2_words[0].rearrange("p n t -> p (n t)").bitcast(I32))
         for q in range(4):
-            load_scales(q)
+            nc.sync.dma_start(out=w2_sc[32 * q:32 * q + 4, :].bitcast(I32), in_=w2_scales[0, 4 * q:4 * q + 4, :].bitcast(I32))
 
-        pairs = {}
-        for g, u in [(0, 0), (0, 1)]:
-            whole = keep.tile([P, T], U32, name=f"pairs{g}_{u}")
-            pairs[g, u] = whole[:]
-        picked = {}
-        for g in range(PASSES):
-            for a in range(HALVES):
-                if (g, a) == (1, 0):
-                    flat = turns.tile([P, PAIR * HALF], U32, name="picked1_0", align_bytes=64, offset=4096 - 64)
-                else:
-                    flat = keep.tile([P, PAIR * HALF], U32, name=f"picked{g}_{a}", align_bytes=64)
-                picked[g, a] = flat[:]
-        woven = {(0, 1): x_tile[1, 0][:, :PAIR * HALF].bitcast(U32)}
+        rest = S - DIRECT
+        planes = [keep.tile([P, PACK * rest], BF16, name=f"planes{g}", align_bytes=64) for g in range(PASSES)]
+        woven = [keep.tile([P, PACK * S], BF16, name=f"woven{g}", align_bytes=64) for g in range(PASSES)]
         g_words = {}
         g_scales = {}
+        shared_scales = keep.tile([P, HALF], U8, name="shared_scales", align_bytes=64)
         w_bf = {}
-        w_bf_first = keep.tile([P, PACK * K_PASS], BF16, name="w_bf_first", align_bytes=64)
         w_words = {}
         w_scales = {}
 
-        def round_x(g, u, src, c0, lo, hi, on_vector):
-            dst = pairs[g, u].bitcast(BF16).rearrange("p (w e) -> p w e", e=PAIR)[:, c0 + lo:c0 + hi]
-            if on_vector:
-                nc.vector.tensor_copy(out=dst, in_=src[:, lo:hi])
-            else:
-                nc.scalar.activation(out=dst, in_=src[:, lo:hi], func=ACT.Copy)
+        def gather_direct(g, j):
+            nc.vector.tensor_copy(out=woven[g][:].rearrange("p (n j) -> p n j", j=PACK)[:, :DIRECT, j], in_=x_raw[g, j][:].indirect(offsets[:, :DIRECT // 16]))
 
-        def round_pieces(g, u):
-            for src, c0, width, share in x_raw[g, u]:
-                if share > 0:
-                    round_x(g, u, src, c0, 0, share, False)
-                if share < width:
-                    round_x(g, u, src, c0, share, width, True)
+        def gather_plane(g, j, lo, hi):
+            nc.scalar.activation(out=planes[g][:, j * rest + lo - DIRECT:j * rest + hi - DIRECT], in_=x_raw[g, j][:].indirect(offsets[:, lo // 16:hi // 16]), func=ACT.Copy)
 
-        def gather(g, u, a, lo=0, hi=HALF):
-            nc.vector.tensor_copy(out=picked[g, a][:, u * HALF + lo:u * HALF + hi], in_=pairs[g, u].indirect(offsets[:, (a * HALF + lo) // 16:(a * HALF + hi) // 16]))
+        def weave(g, lo, hi, j0, j1):
+            dst = woven[g][:, lo * PACK:hi * PACK].rearrange("p (c i j) -> p c j i", i=4, j=PACK)[:, :, j0:j1, :]
+            src = planes[g][:].rearrange("p (j n) -> p j n", j=PACK)[:, j0:j1, lo - DIRECT:hi - DIRECT].rearrange("p j (c i) -> p c j i", i=4)
+            nc.vector.tensor_copy(out=dst, in_=src)
 
-        def weave(g, a, on_vector, lo=0, hi=HALF):
-            if (g, a) == (1, 1):
-                tile = turns.tile([P, HALF * PAIR], U32, name="woven1_1", align_bytes=64, offset=0)
-                woven[g, a] = tile[:]
-            if (g, a) not in woven:
-                tile = keep.tile([P, HALF * PAIR], U32, name=f"woven{g}_{a}", align_bytes=64)
-                woven[g, a] = tile[:]
-            if on_vector:
-                nc.vector.tensor_copy(out=woven[g, a].bitcast(I32).rearrange("p (n u) -> p n u", u=PAIR), in_=picked[g, a].bitcast(I32).rearrange("p (u n) -> p n u", u=PAIR))
-            else:
-                nc.scalar.copy(out=woven[g, a].rearrange("p (n u) -> p n u", u=PAIR)[:, lo:hi], in_=picked[g, a].rearrange("p (u n) -> p n u", u=PAIR)[:, lo:hi])
-
-        def quantise_x(g, a):
-            if (g, a) == (1, 1):
-                g_words[g, a] = turns.tile([P, HALF], U32, name="g_words1_1", align_bytes=64, offset=4096)
-            else:
+        def quantise_x(g, a, lo=0, hi=HALF):
+            if lo == 0:
                 g_words[g, a] = keep.tile([P, HALF], U32, name=f"g_words{g}_{a}", align_bytes=64)
-            g_scales[g, a] = keep.tile([P, HALF], U8, name=f"g_scales{g}_{a}", align_bytes=64)
-            nc.vector.quantize_mx(out=g_words[g, a][:].bitcast(FP8X4), scales=g_scales[g, a][:], in_=woven[g, a].bitcast(BF16))
+                if (g, a) == (1, 0):
+                    g_scales[g, a] = shared_scales[4:, :]
+                else:
+                    own = keep.tile([P, HALF], U8, name=f"g_scales{g}_{a}", align_bytes=64)
+                    g_scales[g, a] = own[:]
+            nc.vector.quantize_mx(out=g_words[g, a][:, lo:hi].bitcast(FP8X4), scales=g_scales[g, a][:, lo:hi], in_=woven[g][:, (a * HALF + lo) * PACK:(a * HALF + hi) * PACK])
 
-        def round_w(g, u):
-            if g == 1:
-                tile = turns.tile([P, PAIR * K_PASS], BF16, name=f"w_bf1_{u}", align_bytes=64, offset=4096 + 2048 * u)
-                w_bf[g, u] = tile[:]
+        def round_w(g, u, cut):
+            w_bf[g, u] = keep.tile([P, PAIR * K_PASS], BF16, name=f"w_bf{g}_{u}", align_bytes=64)
+            dst = w_bf[g, u][:].rearrange("p (t m j) -> p m j t", t=PAIR, j=PACK)
+            src = w_raw[g][:].rearrange("p (j m t) -> p m j t", j=PACK, t=PACK)[:, :, :, PAIR * u:PAIR * (u + 1)]
+            if cut > 0:
+                nc.scalar.activation(out=dst[:, :cut], in_=src[:, :cut], func=ACT.Copy)
+            if cut < P:
+                nc.vector.tensor_copy(out=dst[:, cut:], in_=src[:, cut:])
+
+        def quantise_w(g, t0, t1):
+            words = keep.tile([P, (t1 - t0) * P], U32, name=f"w_words{g}_{t0}", align_bytes=64)
+            if (g, t0) == (0, 1):
+                scales = shared_scales[:, :P]
             else:
-                w_bf[g, u] = w_bf_first[:, u * PAIR * K_PASS:(u + 1) * PAIR * K_PASS]
-            dst = w_bf[g, u].rearrange("p (t m j) -> p m j t", t=PAIR, j=PACK)
-            src = w_raw[g][:].rearrange("p (j m t) -> p m j t", j=PACK, t=PACK)
-            nc.scalar.activation(out=dst, in_=src[:, :, :, PAIR * u:PAIR * (u + 1)], func=ACT.Copy)
-
-        def quantise_w(g, u):
-            w_words[g, u] = keep.tile([P, PAIR * P], U32, name=f"w_words{g}_{u}", align_bytes=64)
-            w_scales[g, u] = keep.tile([P, PAIR * P], U8, name=f"w_scales{g}_{u}", align_bytes=64)
-            nc.vector.quantize_mx(out=w_words[g, u][:].bitcast(FP8X4), scales=w_scales[g, u][:], in_=w_bf[g, u])
-
-        def quantise_w_first():
-            words = keep.tile([P, PACK * P], U32, name="w_words0", align_bytes=64)
-            scales = keep.tile([P, PACK * P], U8, name="w_scales0", align_bytes=64)
-            nc.vector.quantize_mx(out=words[:].bitcast(FP8X4), scales=scales[:], in_=w_bf_first[:])
-            for u in range(PAIR):
-                w_words[0, u] = words[:, u * PAIR * P:(u + 1) * PAIR * P]
-                w_scales[0, u] = scales[:, u * PAIR * P:(u + 1) * PAIR * P]
+                own = keep.tile([P, (t1 - t0) * P], U8, name=f"w_scales{g}_{t0}", align_bytes=64)
+                scales = own[:]
+            lo = t0 % PAIR * K_PASS
+            nc.vector.quantize_mx(out=words[:].bitcast(FP8X4), scales=scales, in_=w_bf[g, t0 // PAIR][:, lo:lo + (t1 - t0) * K_PASS])
+            for t in range(t0, t1):
+                w_words[g, t] = words[:, (t - t0) * P:(t - t0 + 1) * P]
+                w_scales[g, t] = scales[:, (t - t0) * P:(t - t0 + 1) * P]
 
         banks = {}
         for t in range(PACK):
@@ -175,92 +122,76 @@ def tile_picked_deepset_relu_e_kernel(tc, xT, w1, w2_words, w2_scales, offs, out
                 banks[t, a] = psum.tile([P, HALF], F32, name=f"bank{t}_{a}", tag=f"bank{t}_{a}")
 
         def first_product(g, t, a):
-            u, cols = t // PAIR, slice(t % PAIR * P, (t % PAIR + 1) * P)
-            nc.tensor.matmul_mx(out=banks[t, a][:], lhsT=w_words[g, u][:, cols].bitcast(FP8X4), lhsT_scale=w_scales[g, u][:, cols],
-                                rhs=g_words[g, a][:].bitcast(FP8X4), rhs_scale=g_scales[g, a][:], start=(g == 0), stop=(g == PASSES - 1))
+            nc.tensor.matmul_mx(out=banks[t, a][:], lhsT=w_words[g, t].bitcast(FP8X4), lhsT_scale=w_scales[g, t],
+                                rhs=g_words[g, a][:].bitcast(FP8X4), rhs_scale=g_scales[g, a], start=(g == 0), stop=(g == PASSES - 1))
 
-        ring = keep.tile([P, 2 * T - SHARED], U32, name="pairs1")
-        pairs[1, 0] = ring[:, T - SHARED:]
-        pairs[1, 1] = ring[:, :T]
-        round_x(0, 0, x_raw[0, 0], 0, 0, 704, False)
-        round_x(0, 0, x_raw[0, 0], 0, 704, T, True)
-        gather(0, 0, 0)
-        gather(0, 0, 1)
-        round_pieces(0, 1)
-        gather(0, 1, 0)
-        weave(0, 0, False)
-        gather(0, 1, 1)
-        weave(0, 1, False, 0, HALF // 2)
+        for j in range(PACK):
+            gather_direct(0, j)
+            gather_plane(0, j, DIRECT, S)
+        weave(0, DIRECT, S, 0, PACK)
+        gather_direct(1, 0)
+        gather_plane(1, 0, DIRECT, S)
         quantise_x(0, 0)
-        round_x(1, 0, x_raw[1, 0], 0, 0, 704, False)
-        round_x(1, 0, x_raw[1, 0], 0, 704, T, True)
-        weave(0, 1, False, HALF // 2, HALF)
-        gather(1, 0, 0)
-        gather(1, 0, 1)
         quantise_x(0, 1)
-        round_w(0, 0)
-        round_w(0, 1)
-        quantise_w_first()
-        round_pieces(1, 1)
-        gather(1, 1, 0, HALF // 2, HALF)
-        weave(1, 0, False, HALF // 2, HALF)
-        gather(1, 1, 0, 0, HALF // 2)
-        weave(1, 0, False, 0, HALF // 2)
-        gather(1, 1, 1)
+        gather_direct(1, 1)
+        gather_plane(1, 1, DIRECT, S)
+        weave(1, DIRECT, S, 0, PAIR)
+        gather_direct(1, 2)
+        gather_plane(1, 2, DIRECT, S)
+        round_w(0, 0, P)
+        round_w(0, 1, 0)
+        quantise_w(0, 2, 4)
+        quantise_w(0, 0, 1)
+        quantise_w(0, 1, 2)
+        for t in [2, 3, 0]:
+            for a in range(HALVES):
+                first_product(0, t, a)
+        gather_direct(1, 3)
+        for lo, hi in PIECES:
+            gather_plane(1, 3, lo, hi)
+        weave(1, *PIECES[0], PAIR, PACK)
+        weave(1, *PIECES[1], PAIR, PACK)
+        quantise_x(1, 0)
+        for a in range(HALVES):
+            first_product(0, 1, a)
+        weave(1, *PIECES[2], PAIR, PACK)
+        quantise_x(1, 1, 0, HALF // 2)
+        quantise_x(1, 1, HALF // 2, HALF)
+        round_w(1, 0, P)
+        round_w(1, 1, LAST_CUT)
+        quantise_w(1, 0, 2)
+        quantise_w(1, 2, 4)
         for t in range(PACK):
             for a in range(HALVES):
-                if (t, a) not in [(2, 1), (3, 1)]:
-                    first_product(0, t, a)
-        first_product(0, 2, 1)
-        round_w(1, 0)
-        round_w(1, 1)
-        quantise_x(1, 0)
-        first_product(0, 3, 1)
-        weave(1, 1, True)
-        quantise_w(1, 0)
-        quantise_x(1, 1)
-        quantise_w(1, 1)
-        for t, a in [(0, 0), (1, 0), (0, 1), (1, 1), (2, 0), (2, 1), (3, 0), (3, 1)]:
-            first_product(1, t, a)
+                first_product(1, t, a)
 
         h = keep.tile([P, PACK, S], F32, name="h")
-        sums = keep.tile([P, PACK, HALVES], F32, name="sums")
+        sums = keep.tile([P, PACK], F32, name="sums")
+        totals = keep.tile([P, PACK], F32, name="totals")
         neg_mean = keep.tile([P, PACK], F32, name="neg_mean")
 
-        def relu_out(t, a, on_vector):
-            dst = h[:, t, a * HALF:(a + 1) * HALF]
-            if on_vector:
-                nc.vector.tensor_scalar(out=dst, in0=banks[t, a][:], scalar1=0.0, scalar2=None, op0=ALU.max, op1=ALU.add, accum_out=sums[:, t, a:a + 1])
-            else:
-                nc.scalar.activation(out=dst, in_=banks[t, a][:], func=ACT.Relu, accum_out=sums[:, t, a:a + 1])
+        def relu_first(t):
+            nc.scalar.activation(out=h[:, t, :HALF], in_=banks[t, 0][:], func=ACT.Relu, accum_out=sums[:, t:t + 1])
 
-        def mean(t):
-            nc.vector.tensor_scalar(out=neg_mean[:, t:t + 1], in0=sums[:, t, 0:1], scalar1=sums[:, t, 1:2], scalar2=-1.0 / S, op0=ALU.add, op1=ALU.mult)
+        def relu_second(t):
+            nc.vector.tensor_scalar(out=h[:, t, HALF:], in0=banks[t, 1][:], scalar1=0.0, scalar2=sums[:, t:t + 1], op0=ALU.max, op1=ALU.add, accum_out=totals[:, t:t + 1])
 
         z_planes = keep.tile([P, PACK, S - Z_SPLIT], BF16, name="z_planes")
 
         def plane(t, on_vector):
             if on_vector:
-                nc.vector.tensor_scalar(out=z_planes[:, t, :], in0=h[:, t, Z_SPLIT:], scalar1=neg_mean[:, t:t + 1], scalar2=None, op0=ALU.add)
+                nc.vector.tensor_scalar(out=z_planes[:, t, :], in0=h[:, t, Z_SPLIT:], scalar1=-float(S), scalar2=totals[:, t:t + 1], op0=ALU.mult, op1=ALU.add)
             else:
-                nc.scalar.activation(out=z_planes[:, t, :], in_=h[:, t, Z_SPLIT:], func=ACT.Identity, bias=neg_mean[:, t:t + 1], scale=1.0)
+                nc.scalar.activation(out=z_planes[:, t, :], in_=h[:, t, Z_SPLIT:], func=ACT.Identity, bias=totals[:, t:t + 1], scale=-float(S))
 
-        relu_out(0, 0, False)
-        relu_out(1, 0, False)
-        relu_out(0, 1, True)
-        relu_out(1, 1, False)
-        relu_out(2, 0, True)
-        relu_out(2, 1, False)
-        relu_out(3, 0, True)
-        relu_out(3, 1, False)
-        mean(0)
-        mean(1)
-        mean(2)
-        plane(0, True)
-        mean(3)
-        plane(1, True)
-        plane(2, False)
-        plane(3, False)
+        for t in range(PACK):
+            relu_first(t)
+            relu_second(t)
+        plane(0, False)
+        plane(1, False)
+        plane(2, True)
+        nc.vector.tensor_scalar(out=neg_mean[:], in0=totals[:], scalar1=-1.0 / S, scalar2=None, op0=ALU.mult)
+        plane(3, True)
 
         z_words = keep.tile([P, S], U32, name="z_words", align_bytes=64)
         z_scales = keep.tile([P, S], U8, name="z_scales", align_bytes=64)
@@ -279,25 +210,30 @@ def tile_picked_deepset_relu_e_kernel(tc, xT, w1, w2_words, w2_scales, offs, out
         def weave_scalar(lo, hi):
             nc.scalar.copy(out=z_view(lo, hi), in_=z_planes[:, :, lo - Z_SPLIT:hi - Z_SPLIT].rearrange("p t (c i) -> p c t i", i=4))
 
-        def second_product(i, on_vector):
-            lo, hi = Z_PIECES[i]
+        accs = {}
+        for i, (lo, hi, on_vector) in enumerate(STORES):
+            accs[lo] = psum.tile([P, HALF], F32, name=f"acc{i}", tag=f"bank{i}_0")
+
+        def second_product(lo, hi):
+            base = max(b for b in accs if b <= lo)
             nc.vector.quantize_mx(out=z_words[:, lo:hi].bitcast(FP8X4), scales=z_scales[:, lo:hi], in_=z_bf[lo][:])
-            acc = psum.tile([P, HALF], F32, name=f"acc{i}", tag=f"bank{i % PACK}_{i // PACK}")
-            nc.tensor.matmul_mx(out=acc[:, :hi - lo], lhsT=w2_w[:].bitcast(FP8X4), lhsT_scale=w2_sc[:], rhs=z_words[:, lo:hi].bitcast(FP8X4), rhs_scale=z_scales[:, lo:hi], start=True, stop=True)
-            res = keep.tile([P, hi - lo], F32, name=f"res{i}")
+            nc.tensor.matmul_mx(out=accs[base][:, lo - base:hi - base], lhsT=w2_w[:].bitcast(FP8X4), lhsT_scale=w2_sc[:], rhs=z_words[:, lo:hi].bitcast(FP8X4), rhs_scale=z_scales[:, lo:hi], start=True, stop=True)
+
+        def store(lo, hi, on_vector):
+            res = keep.tile([P, hi - lo], F32, name=f"res{lo}")
+            back = 1.0 if lo < Z_SPLIT else -1.0 / S
             if on_vector:
-                nc.vector.tensor_copy(out=res[:], in_=acc[:, :hi - lo])
+                nc.vector.tensor_scalar(out=res[:], in0=accs[lo][:, :hi - lo], scalar1=back, scalar2=None, op0=ALU.mult)
             else:
-                nc.scalar.copy(out=res[:], in_=acc[:, :hi - lo])
+                nc.scalar.activation(out=res[:], in_=accs[lo][:, :hi - lo], func=ACT.Copy, scale=back)
             nc.sync.dma_start(out=out[:, lo:hi], in_=res[:])
 
-        weave_scalar(Z_SPLIT, 768)
-        weave_scalar(768, 896)
-        weave_scalar(896, S)
-        centre_vector(0, 256)
-        centre_vector(256, 512)
-        second_product(0, False)
-        second_product(1, False)
-        second_product(2, False)
-        second_product(3, True)
-        second_product(4, True)
+        for lo, hi in Z_PIECES:
+            if lo >= Z_SPLIT:
+                weave_scalar(lo, hi)
+            else:
+                centre_vector(lo, hi)
+        for lo, hi in Z_PIECES:
+            second_product(lo, hi)
+        for lo, hi, on_vector in STORES:
+            store(lo, hi, on_vector)

@@ -22,9 +22,9 @@ PASSES = K // K_PASS
 HALF = 512
 HALVES = S // HALF
 PAIR = 2
-DIRECT = 256
+DIRECT = [384, 256]
 PIECES = [(256, 512), (512, 768), (768, 1024)]
-LAST_CUT = 96
+LAST_CUT = 80
 Z_SPLIT = 384
 Z_PIECES = [(0, 256), (256, 384), (384, 640), (640, 896), (896, 1024)]
 STORES = [(0, 384, False), (384, 640, False), (640, 896, True), (896, 1024, True)]
@@ -44,44 +44,53 @@ def tile_picked_deepset_relu_e_kernel(tc, xT, w1, w2_words, w2_scales, offs, out
         x_raw = {}
         w_raw = {}
 
-        def load_x(g, j):
-            x_raw[g, j] = keep.tile([P, T], F32, name=f"x_raw{g}_{j}", align_bytes=64)
-            nc.sync.dma_start(out=x_raw[g, j][:], in_=xT[g * K_PASS:(g + 1) * K_PASS, :].rearrange("(p j) w -> p j w", j=PACK)[:, j, :])
+        def load_x(g, j, rows):
+            tile = keep.tile([P, rows * T], F32, name=f"x_raw{g}_{j}", align_bytes=64)
+            nc.sync.dma_start(out=tile[:], in_=xT[g * K_PASS:(g + 1) * K_PASS, :].rearrange("(p j) w -> p (j w)", j=PACK)[:, j * T:(j + rows) * T])
+            for r in range(rows):
+                x_raw[g, j + r] = tile[:, r * T:(r + 1) * T]
 
         def load_w(g):
             w_raw[g] = keep.tile([P, PACK * H], F32, name=f"w_raw{g}", align_bytes=64)
             nc.sync.dma_start(out=w_raw[g][:], in_=w1[g * K_PASS:(g + 1) * K_PASS, :].rearrange("(p j) w -> p (j w)", j=PACK))
 
-        load_x(0, 0)
+        load_x(0, 0, PAIR)
         nc.sync.dma_start(offsets[:], offs)
-        for g, j in [(0, 1), (0, 2), (0, 3), (1, 0), (1, 1), (1, 2)]:
-            load_x(g, j)
+        load_x(0, PAIR, PAIR)
+        for j in range(PACK - 1):
+            load_x(1, j, 1)
         load_w(0)
-        load_x(1, 3)
+        load_x(1, PACK - 1, 1)
         load_w(1)
         nc.sync.dma_start(out=w2_w[:].bitcast(I32), in_=w2_words[0].rearrange("p n t -> p (n t)").bitcast(I32))
         for q in range(4):
             nc.sync.dma_start(out=w2_sc[32 * q:32 * q + 4, :].bitcast(I32), in_=w2_scales[0, 4 * q:4 * q + 4, :].bitcast(I32))
 
-        rest = S - DIRECT
-        planes = [keep.tile([P, PACK * rest], BF16, name=f"planes{g}", align_bytes=64) for g in range(PASSES)]
+        rest = [S - d for d in DIRECT]
+        planes = [keep.tile([P, PACK * rest[g]], [F32, BF16][g], name=f"planes{g}", align_bytes=64) for g in range(PASSES)]
         woven = [keep.tile([P, PACK * S], BF16, name=f"woven{g}", align_bytes=64) for g in range(PASSES)]
         g_words = {}
         g_scales = {}
         shared_scales = keep.tile([P, HALF], U8, name="shared_scales", align_bytes=64)
+        w_last = keep.tile([P, PACK * K_PASS - 64], BF16, name="w_last", align_bytes=64)
         w_bf = {}
         w_words = {}
         w_scales = {}
 
         def gather_direct(g, j):
-            nc.vector.tensor_copy(out=woven[g][:].rearrange("p (n j) -> p n j", j=PACK)[:, :DIRECT, j], in_=x_raw[g, j][:].indirect(offsets[:, :DIRECT // 16]))
+            nc.vector.tensor_copy(out=woven[g][:].rearrange("p (n j) -> p n j", j=PACK)[:, :DIRECT[g], j], in_=x_raw[g, j].indirect(offsets[:, :DIRECT[g] // 16]))
 
         def gather_plane(g, j, lo, hi):
-            nc.scalar.activation(out=planes[g][:, j * rest + lo - DIRECT:j * rest + hi - DIRECT], in_=x_raw[g, j][:].indirect(offsets[:, lo // 16:hi // 16]), func=ACT.Copy)
+            dst = planes[g][:, j * rest[g] + lo - DIRECT[g]:j * rest[g] + hi - DIRECT[g]]
+            src = x_raw[g, j].indirect(offsets[:, lo // 16:hi // 16])
+            if (g, j) == (0, 1):
+                nc.vector.tensor_copy(out=dst, in_=src)
+            else:
+                nc.scalar.activation(out=dst, in_=src, func=ACT.Copy)
 
         def weave(g, lo, hi, j0, j1):
             dst = woven[g][:, lo * PACK:hi * PACK].rearrange("p (c i j) -> p c j i", i=4, j=PACK)[:, :, j0:j1, :]
-            src = planes[g][:].rearrange("p (j n) -> p j n", j=PACK)[:, j0:j1, lo - DIRECT:hi - DIRECT].rearrange("p j (c i) -> p c j i", i=4)
+            src = planes[g][:].rearrange("p (j n) -> p j n", j=PACK)[:, j0:j1, lo - DIRECT[g]:hi - DIRECT[g]].rearrange("p j (c i) -> p c j i", i=4)
             nc.vector.tensor_copy(out=dst, in_=src)
 
         def quantise_x(g, a, lo=0, hi=HALF):
@@ -95,8 +104,13 @@ def tile_picked_deepset_relu_e_kernel(tc, xT, w1, w2_words, w2_scales, offs, out
             nc.vector.quantize_mx(out=g_words[g, a][:, lo:hi].bitcast(FP8X4), scales=g_scales[g, a][:, lo:hi], in_=woven[g][:, (a * HALF + lo) * PACK:(a * HALF + hi) * PACK])
 
         def round_w(g, u, cut):
-            w_bf[g, u] = keep.tile([P, PAIR * K_PASS], BF16, name=f"w_bf{g}_{u}", align_bytes=64)
-            dst = w_bf[g, u][:].rearrange("p (t m j) -> p m j t", t=PAIR, j=PACK)
+            if g == 1:
+                lo = (1 - u) * (PAIR * K_PASS - 64)
+                w_bf[g, u] = w_last[:, lo:lo + PAIR * K_PASS]
+            else:
+                own = keep.tile([P, PAIR * K_PASS], BF16, name=f"w_bf{g}_{u}", align_bytes=64)
+                w_bf[g, u] = own[:]
+            dst = w_bf[g, u].rearrange("p (t m j) -> p m j t", t=PAIR, j=PACK)
             src = w_raw[g][:].rearrange("p (j m t) -> p m j t", j=PACK, t=PACK)[:, :, :, PAIR * u:PAIR * (u + 1)]
             if cut > 0:
                 nc.scalar.activation(out=dst[:, :cut], in_=src[:, :cut], func=ACT.Copy)
@@ -127,17 +141,17 @@ def tile_picked_deepset_relu_e_kernel(tc, xT, w1, w2_words, w2_scales, offs, out
 
         for j in range(PACK):
             gather_direct(0, j)
-            gather_plane(0, j, DIRECT, S)
-        weave(0, DIRECT, S, 0, PACK)
+            gather_plane(0, j, DIRECT[0], S)
         gather_direct(1, 0)
-        gather_plane(1, 0, DIRECT, S)
+        weave(0, DIRECT[0], S, 0, PACK)
+        gather_plane(1, 0, DIRECT[1], S)
         quantise_x(0, 0)
         quantise_x(0, 1)
         gather_direct(1, 1)
-        gather_plane(1, 1, DIRECT, S)
-        weave(1, DIRECT, S, 0, PAIR)
+        gather_plane(1, 1, DIRECT[1], S)
+        weave(1, DIRECT[1], S, 0, PAIR)
         gather_direct(1, 2)
-        gather_plane(1, 2, DIRECT, S)
+        gather_plane(1, 2, DIRECT[1], S)
         round_w(0, 0, P)
         round_w(0, 1, 0)
         quantise_w(0, 2, 4)
@@ -158,8 +172,9 @@ def tile_picked_deepset_relu_e_kernel(tc, xT, w1, w2_words, w2_scales, offs, out
         quantise_x(1, 1, 0, HALF // 2)
         quantise_x(1, 1, HALF // 2, HALF)
         round_w(1, 0, P)
+        quantise_w(1, 0, 1)
+        quantise_w(1, 1, 2)
         round_w(1, 1, LAST_CUT)
-        quantise_w(1, 0, 2)
         quantise_w(1, 2, 4)
         for t in range(PACK):
             for a in range(HALVES):

@@ -25,6 +25,7 @@ PAIR = 2
 DIRECT = [384, 256]
 PIECES = [(256, 512), (512, 768), (768, 1024)]
 LAST_CUT = 80
+FILL = 320
 Z_SPLIT = 384
 Z_PIECES = [(0, 256), (256, 384), (384, 640), (640, 896), (896, 1024)]
 STORES = [(0, 384, False), (384, 640, False), (640, 896, True), (896, 1024, True)]
@@ -181,32 +182,37 @@ def tile_picked_deepset_relu_e_kernel(tc, xT, w1, w2_words, w2_scales, offs, out
                 first_product(1, t, a)
 
         h = keep.tile([P, PACK, S], F32, name="h")
-        sums = keep.tile([P, PACK], F32, name="sums")
+        sums = keep.tile([P, PACK + 1], F32, name="sums")
         totals = keep.tile([P, PACK], F32, name="totals")
         neg_mean = keep.tile([P, PACK], F32, name="neg_mean")
 
-        def relu_first(t):
-            nc.scalar.activation(out=h[:, t, :HALF], in_=banks[t, 0][:], func=ACT.Relu, accum_out=sums[:, t:t + 1])
+        def relu_scalar(t, a):
+            nc.scalar.activation(out=h[:, t, a * HALF:(a + 1) * HALF], in_=banks[t, a][:], func=ACT.Relu, accum_out=sums[:, t + a:t + a + 1])
 
-        def relu_second(t):
+        def relu_vector(t):
             nc.vector.tensor_scalar(out=h[:, t, HALF:], in0=banks[t, 1][:], scalar1=0.0, scalar2=sums[:, t:t + 1], op0=ALU.max, op1=ALU.add, accum_out=totals[:, t:t + 1])
 
         z_planes = keep.tile([P, PACK, S - Z_SPLIT], BF16, name="z_planes")
 
-        def plane(t, on_vector):
+        def plane(t, on_vector, lo=Z_SPLIT, hi=S):
             if on_vector:
-                nc.vector.tensor_scalar(out=z_planes[:, t, :], in0=h[:, t, Z_SPLIT:], scalar1=-float(S), scalar2=totals[:, t:t + 1], op0=ALU.mult, op1=ALU.add)
+                nc.vector.tensor_scalar(out=z_planes[:, t, lo - Z_SPLIT:hi - Z_SPLIT], in0=h[:, t, lo:hi], scalar1=-float(S), scalar2=totals[:, t:t + 1], op0=ALU.mult, op1=ALU.add)
             else:
-                nc.scalar.activation(out=z_planes[:, t, :], in_=h[:, t, Z_SPLIT:], func=ACT.Identity, bias=totals[:, t:t + 1], scale=-float(S))
+                nc.scalar.activation(out=z_planes[:, t, lo - Z_SPLIT:hi - Z_SPLIT], in_=h[:, t, lo:hi], func=ACT.Identity, bias=totals[:, t:t + 1], scale=-float(S))
 
-        for t in range(PACK):
-            relu_first(t)
-            relu_second(t)
-        plane(0, False)
-        plane(1, False)
-        plane(2, True)
-        nc.vector.tensor_scalar(out=neg_mean[:], in0=totals[:], scalar1=-1.0 / S, scalar2=None, op0=ALU.mult)
-        plane(3, True)
+        last = PACK - 1
+        for t in range(last):
+            relu_scalar(t, 0)
+            relu_vector(t)
+        relu_scalar(last, 0)
+        relu_scalar(last, 1)
+        plane(0, True)
+        plane(1, True, Z_SPLIT, S - FILL)
+        nc.vector.tensor_scalar(out=neg_mean[:, :last], in0=totals[:, :last], scalar1=-1.0 / S, scalar2=None, op0=ALU.mult)
+        nc.vector.tensor_scalar(out=neg_mean[:, last:], in0=sums[:, last:PACK], scalar1=sums[:, PACK:], scalar2=-1.0 / S, op0=ALU.add, op1=ALU.mult)
+        plane(1, True, S - FILL, S)
+        plane(2, False)
+        nc.vector.tensor_scalar(out=z_planes[:, last, :], in0=h[:, last, Z_SPLIT:], scalar1=neg_mean[:, last:], scalar2=-float(S), op0=ALU.add, op1=ALU.mult)
 
         z_words = keep.tile([P, S], U32, name="z_words", align_bytes=64)
         z_scales = keep.tile([P, S], U8, name="z_scales", align_bytes=64)

@@ -212,7 +212,8 @@ def tile_picked_deepset_relu_e_kernel(tc, xT, w1, w2_words, w2_scales, offs, out
         nc.vector.tensor_scalar(out=neg_mean[:, last:], in0=sums[:, last:PACK], scalar1=sums[:, PACK:], scalar2=-1.0 / S, op0=ALU.add, op1=ALU.mult)
         plane(1, True, S - FILL, S)
         plane(2, False)
-        nc.vector.tensor_scalar(out=z_planes[:, last, :], in0=h[:, last, Z_SPLIT:], scalar1=neg_mean[:, last:], scalar2=-float(S), op0=ALU.add, op1=ALU.mult)
+        for lo, hi in [(Z_SPLIT, Z_PIECES[2][1]), (Z_PIECES[2][1], S)]:
+            nc.vector.tensor_scalar(out=z_planes[:, last, lo - Z_SPLIT:hi - Z_SPLIT], in0=h[:, last, lo:hi], scalar1=neg_mean[:, last:], scalar2=-float(S), op0=ALU.add, op1=ALU.mult)
 
         z_words = keep.tile([P, S], U32, name="z_words", align_bytes=64)
         z_scales = keep.tile([P, S], U8, name="z_scales", align_bytes=64)

@@ -206,12 +206,12 @@ def tile_picked_deepset_relu_e_kernel(tc, xT, w1, w2_words, w2_scales, offs, out
             relu_vector(t)
         relu_scalar(last, 0)
         relu_scalar(last, 1)
-        plane(0, True)
-        plane(1, True, Z_SPLIT, S - FILL)
+        nc.gpsimd.tensor_scalar(out=z_planes[:, 0, :], in0=h[:, 0, Z_SPLIT:], scalar1=-float(S), scalar2=totals[:, 0:1], op0=ALU.mult, op1=ALU.add)
+        plane(1, True)
         nc.vector.tensor_scalar(out=neg_mean[:, :last], in0=totals[:, :last], scalar1=-1.0 / S, scalar2=None, op0=ALU.mult)
         nc.vector.tensor_scalar(out=neg_mean[:, last:], in0=sums[:, last:PACK], scalar1=sums[:, PACK:], scalar2=-1.0 / S, op0=ALU.add, op1=ALU.mult)
-        plane(1, True, S - FILL, S)
-        plane(2, False)
+        plane(2, False, Z_SPLIT, S - FILL)
+        plane(2, True, S - FILL, S)
         for lo, hi in [(Z_SPLIT, Z_PIECES[2][1]), (Z_PIECES[2][1], S)]:
             nc.vector.tensor_scalar(out=z_planes[:, last, lo - Z_SPLIT:hi - Z_SPLIT], in0=h[:, last, lo:hi], scalar1=neg_mean[:, last:], scalar2=-float(S), op0=ALU.add, op1=ALU.mult)
 

@@ -90,8 +90,9 @@ def tile_picked_deepset_relu_e_kernel(tc, xT, w1, w2_words, w2_scales, offs, out
                 nc.scalar.activation(out=dst, in_=src, func=ACT.Copy)
 
         def weave(g, lo, hi, j0, j1):
-            dst = woven[g][:, lo * PACK:hi * PACK].rearrange("p (c i j) -> p c j i", i=4, j=PACK)[:, :, j0:j1, :]
-            src = planes[g][:].rearrange("p (j n) -> p j n", j=PACK)[:, j0:j1, lo - DIRECT[g]:hi - DIRECT[g]].rearrange("p j (c i) -> p c j i", i=4)
+            run = j1 - j0
+            dst = woven[g][:, lo * PACK:hi * PACK].rearrange("p (c i j) -> p c j i", i=run, j=PACK)[:, :, j0:j1, :]
+            src = planes[g][:].rearrange("p (j n) -> p j n", j=PACK)[:, j0:j1, lo - DIRECT[g]:hi - DIRECT[g]].rearrange("p j (c i) -> p c j i", i=run)
             nc.vector.tensor_copy(out=dst, in_=src)
 
         def quantise_x(g, a, lo=0, hi=HALF):
@@ -221,16 +222,16 @@ def tile_picked_deepset_relu_e_kernel(tc, xT, w1, w2_words, w2_scales, offs, out
         for lo, hi in Z_PIECES:
             z_bf[lo] = keep.tile([P, (hi - lo) * PACK], BF16, name=f"z_bf{lo}", align_bytes=64)
 
-        def z_view(lo, hi):
+        def z_view(lo, hi, run):
             base = max(b for b in z_bf if b <= lo)
-            return z_bf[base][:, (lo - base) * PACK:(hi - base) * PACK].rearrange("p (c i t) -> p c t i", i=4, t=PACK)
+            return z_bf[base][:, (lo - base) * PACK:(hi - base) * PACK].rearrange("p (c i t) -> p c t i", i=run, t=PACK)
 
         def centre_vector(lo, hi):
-            nc.vector.tensor_tensor(out=z_view(lo, hi), in0=h[:, :, lo:hi].rearrange("p t (c i) -> p c t i", i=4),
-                                    in1=neg_mean[:].unsqueeze(1).unsqueeze(3).to_broadcast([P, (hi - lo) // 4, PACK, 4]), op=ALU.add)
+            nc.vector.tensor_tensor(out=z_view(lo, hi, PAIR), in0=h[:, :, lo:hi].rearrange("p t (c i) -> p c t i", i=PAIR),
+                                    in1=neg_mean[:].unsqueeze(1).unsqueeze(3).to_broadcast([P, (hi - lo) // PAIR, PACK, PAIR]), op=ALU.add)
 
         def weave_scalar(lo, hi):
-            nc.scalar.copy(out=z_view(lo, hi), in_=z_planes[:, :, lo - Z_SPLIT:hi - Z_SPLIT].rearrange("p t (c i) -> p c t i", i=4))
+            nc.scalar.copy(out=z_view(lo, hi, 4), in_=z_planes[:, :, lo - Z_SPLIT:hi - Z_SPLIT].rearrange("p t (c i) -> p c t i", i=4))
 
         accs = {}
         for i, (lo, hi, on_vector) in enumerate(STORES):

@@ -25,10 +25,10 @@ PAIR = 2
 DIRECT = [384, 256]
 PIECES = [(256, 512), (512, 768), (768, 1024)]
 LAST_CUT = 80
-FILL = 320
-Z_SPLIT = 384
-Z_PIECES = [(0, 256), (256, 384), (384, 640), (640, 896), (896, 1024)]
-STORES = [(0, 384, False), (384, 640, False), (640, 896, True), (896, 1024, True)]
+QUARTER = 256
+POOL_SHARE = 320
+SCALAR_END = 192
+Z_PIECES = [(512, 768, True), (0, 256, False), (768, 1024, True), (256, 384, False), (384, 512, False)]
 
 
 def tile_picked_deepset_relu_e_kernel(tc, xT, w1, w2_words, w2_scales, offs, out):
@@ -178,85 +178,67 @@ def tile_picked_deepset_relu_e_kernel(tc, xT, w1, w2_words, w2_scales, offs, out
         quantise_w(1, 1, 2)
         round_w(1, 1, LAST_CUT)
         quantise_w(1, 2, 4)
-        for t in range(PACK):
-            for a in range(HALVES):
-                first_product(1, t, a)
+        for t, a in [(0, 0), (1, 0), (0, 1), (1, 1), (2, 0), (2, 1), (3, 0), (3, 1)]:
+            first_product(1, t, a)
+        last = PACK - 1
+
 
         h = keep.tile([P, PACK, S], F32, name="h")
-        sums = keep.tile([P, PACK + 1], F32, name="sums")
+        sums = keep.tile([P, PACK], F32, name="sums")
         totals = keep.tile([P, PACK], F32, name="totals")
-        neg_mean = keep.tile([P, PACK], F32, name="neg_mean")
+        z_planes = keep.tile([P, PACK, S], BF16, name="z_planes", align_bytes=64)
 
-        def relu_scalar(t, a):
-            nc.scalar.activation(out=h[:, t, a * HALF:(a + 1) * HALF], in_=banks[t, a][:], func=ACT.Relu, accum_out=sums[:, t + a:t + a + 1])
-
-        def relu_vector(t):
+        def empty(t):
+            nc.scalar.activation(out=h[:, t, :HALF], in_=banks[t, 0][:], func=ACT.Relu, accum_out=sums[:, t:t + 1])
             nc.vector.tensor_scalar(out=h[:, t, HALF:], in0=banks[t, 1][:], scalar1=0.0, scalar2=sums[:, t:t + 1], op0=ALU.max, op1=ALU.add, accum_out=totals[:, t:t + 1])
 
-        z_planes = keep.tile([P, PACK, S - Z_SPLIT], BF16, name="z_planes")
-
-        def plane(t, on_vector, lo=Z_SPLIT, hi=S):
-            if on_vector:
-                nc.vector.tensor_scalar(out=z_planes[:, t, lo - Z_SPLIT:hi - Z_SPLIT], in0=h[:, t, lo:hi], scalar1=-float(S), scalar2=totals[:, t:t + 1], op0=ALU.mult, op1=ALU.add)
+        def plane(t, lo, hi, engine):
+            if engine is nc.scalar:
+                nc.scalar.activation(out=z_planes[:, t, lo:hi], in_=h[:, t, lo:hi], func=ACT.Identity, bias=totals[:, t:t + 1], scale=-float(S))
             else:
-                nc.scalar.activation(out=z_planes[:, t, lo - Z_SPLIT:hi - Z_SPLIT], in_=h[:, t, lo:hi], func=ACT.Identity, bias=totals[:, t:t + 1], scale=-float(S))
+                engine.tensor_scalar(out=z_planes[:, t, lo:hi], in0=h[:, t, lo:hi], scalar1=-float(S), scalar2=totals[:, t:t + 1], op0=ALU.mult, op1=ALU.add)
 
-        last = PACK - 1
-        for t in range(last):
-            relu_scalar(t, 0)
-            relu_vector(t)
-        relu_scalar(last, 0)
-        relu_scalar(last, 1)
-        nc.gpsimd.tensor_scalar(out=z_planes[:, 0, :], in0=h[:, 0, Z_SPLIT:], scalar1=-float(S), scalar2=totals[:, 0:1], op0=ALU.mult, op1=ALU.add)
-        plane(1, True)
-        nc.vector.tensor_scalar(out=neg_mean[:, :last], in0=totals[:, :last], scalar1=-1.0 / S, scalar2=None, op0=ALU.mult)
-        nc.vector.tensor_scalar(out=neg_mean[:, last:], in0=sums[:, last:PACK], scalar1=sums[:, PACK:], scalar2=-1.0 / S, op0=ALU.add, op1=ALU.mult)
-        plane(2, False, Z_SPLIT, S - FILL)
-        plane(2, True, S - FILL, S)
-        for lo, hi in [(Z_SPLIT, Z_PIECES[2][1]), (Z_PIECES[2][1], S)]:
-            nc.vector.tensor_scalar(out=z_planes[:, last, lo - Z_SPLIT:hi - Z_SPLIT], in0=h[:, last, lo:hi], scalar1=neg_mean[:, last:], scalar2=-float(S), op0=ALU.add, op1=ALU.mult)
+        for t in range(PACK):
+            empty(t)
+        plane(0, 0, S, nc.gpsimd)
+        plane(1, 0, POOL_SHARE, nc.gpsimd)
+        plane(1, POOL_SHARE, S, nc.scalar)
+        plane(2, 0, SCALAR_END, nc.scalar)
+        plane(2, SCALAR_END, S, nc.vector)
+        plane(last, 0, QUARTER, nc.scalar)
+        plane(last, HALF, S, nc.vector)
+        plane(last, QUARTER, HALF, nc.vector)
 
         z_words = keep.tile([P, S], U32, name="z_words", align_bytes=64)
         z_scales = keep.tile([P, S], U8, name="z_scales", align_bytes=64)
         z_bf = {}
-        for lo, hi in Z_PIECES:
-            z_bf[lo] = keep.tile([P, (hi - lo) * PACK], BF16, name=f"z_bf{lo}", align_bytes=64)
-
-        def z_view(lo, hi, run):
-            base = max(b for b in z_bf if b <= lo)
-            return z_bf[base][:, (lo - base) * PACK:(hi - base) * PACK].rearrange("p (c i t) -> p c t i", i=run, t=PACK)
-
-        def centre_vector(lo, hi):
-            nc.vector.tensor_tensor(out=z_view(lo, hi, PAIR), in0=h[:, :, lo:hi].rearrange("p t (c i) -> p c t i", i=PAIR),
-                                    in1=neg_mean[:].unsqueeze(1).unsqueeze(3).to_broadcast([P, (hi - lo) // PAIR, PACK, PAIR]), op=ALU.add)
-
-        def weave_scalar(lo, hi):
-            nc.scalar.copy(out=z_view(lo, hi, 4), in_=z_planes[:, :, lo - Z_SPLIT:hi - Z_SPLIT].rearrange("p t (c i) -> p c t i", i=4))
-
         accs = {}
-        for i, (lo, hi, on_vector) in enumerate(STORES):
-            accs[lo] = psum.tile([P, HALF], F32, name=f"acc{i}", tag=f"bank{i}_0")
 
-        def second_product(lo, hi):
-            base = max(b for b in accs if b <= lo)
+        def weave_z(lo, hi, on_vector):
+            z_bf[lo] = keep.tile([P, (hi - lo) * PACK], BF16, name=f"z_bf{lo}", align_bytes=64)
+            dst = z_bf[lo][:].rearrange("p (c i t) -> p c t i", i=4, t=PACK)
+            src = z_planes[:, :, lo:hi].rearrange("p t (c i) -> p c t i", i=4)
+            if on_vector:
+                nc.vector.tensor_copy(out=dst, in_=src)
+            else:
+                nc.scalar.copy(out=dst, in_=src)
+
+        def second_product(i, lo, hi):
+            accs[lo] = psum.tile([P, HALF], F32, name=f"acc{i}", tag=f"bank{i % PACK}_{i // PACK}")
             nc.vector.quantize_mx(out=z_words[:, lo:hi].bitcast(FP8X4), scales=z_scales[:, lo:hi], in_=z_bf[lo][:])
-            nc.tensor.matmul_mx(out=accs[base][:, lo - base:hi - base], lhsT=w2_w[:].bitcast(FP8X4), lhsT_scale=w2_sc[:], rhs=z_words[:, lo:hi].bitcast(FP8X4), rhs_scale=z_scales[:, lo:hi], start=True, stop=True)
+            nc.tensor.matmul_mx(out=accs[lo][:, :hi - lo], lhsT=w2_w[:].bitcast(FP8X4), lhsT_scale=w2_sc[:], rhs=z_words[:, lo:hi].bitcast(FP8X4), rhs_scale=z_scales[:, lo:hi], start=True, stop=True)
 
         def store(lo, hi, on_vector):
             res = keep.tile([P, hi - lo], F32, name=f"res{lo}")
-            back = 1.0 if lo < Z_SPLIT else -1.0 / S
             if on_vector:
-                nc.vector.tensor_scalar(out=res[:], in0=accs[lo][:, :hi - lo], scalar1=back, scalar2=None, op0=ALU.mult)
+                nc.vector.tensor_scalar(out=res[:], in0=accs[lo][:, :hi - lo], scalar1=-1.0 / S, scalar2=None, op0=ALU.mult)
             else:
-                nc.scalar.activation(out=res[:], in_=accs[lo][:, :hi - lo], func=ACT.Copy, scale=back)
+                nc.scalar.activation(out=res[:], in_=accs[lo][:, :hi - lo], func=ACT.Copy, scale=-1.0 / S)
             nc.sync.dma_start(out=out[:, lo:hi], in_=res[:])
 
-        for lo, hi in Z_PIECES:
-            if lo >= Z_SPLIT:
-                weave_scalar(lo, hi)
-            else:
-                centre_vector(lo, hi)
-        for lo, hi in Z_PIECES:
-            second_product(lo, hi)
-        for lo, hi, on_vector in STORES:
-            store(lo, hi, on_vector)
+        for lo, hi, on_vector in Z_PIECES:
+            weave_z(lo, hi, on_vector)
+        for i, (lo, hi, on_vector) in enumerate(Z_PIECES):
+            second_product(i, lo, hi)
+        for i, (lo, hi, on_vector) in enumerate(Z_PIECES):
+            store(lo, hi, i >= 3)

@@ -26,8 +26,6 @@ DIRECT = [384, 256]
 PIECES = [(256, 512), (512, 768), (768, 1024)]
 LAST_CUT = 80
 QUARTER = 256
-POOL_SHARE = 320
-SCALAR_END = 192
 Z_PIECES = [(512, 768, True), (0, 256, False), (768, 1024, True), (256, 384, False), (384, 512, False)]
 
 
@@ -201,10 +199,8 @@ def tile_picked_deepset_relu_e_kernel(tc, xT, w1, w2_words, w2_scales, offs, out
         for t in range(PACK):
             empty(t)
         plane(0, 0, S, nc.gpsimd)
-        plane(1, 0, POOL_SHARE, nc.gpsimd)
-        plane(1, POOL_SHARE, S, nc.scalar)
-        plane(2, 0, SCALAR_END, nc.scalar)
-        plane(2, SCALAR_END, S, nc.vector)
+        plane(1, 0, S, nc.scalar)
+        plane(2, 0, S, nc.vector)
         plane(last, 0, QUARTER, nc.scalar)
         plane(last, HALF, S, nc.vector)
         plane(last, QUARTER, HALF, nc.vector)

@@ -26,6 +26,7 @@ DIRECT = [384, 256]
 PIECES = [(256, 512), (512, 768), (768, 1024)]
 LAST_CUT = 80
 QUARTER = 256
+SECOND_ROW_CUT = 768
 Z_PIECES = [(512, 768, True), (0, 256, False), (768, 1024, True), (256, 384, False), (384, 512, False)]
 
 
@@ -79,10 +80,10 @@ def tile_picked_deepset_relu_e_kernel(tc, xT, w1, w2_words, w2_scales, offs, out
         def gather_direct(g, j):
             nc.vector.tensor_copy(out=woven[g][:].rearrange("p (n j) -> p n j", j=PACK)[:, :DIRECT[g], j], in_=x_raw[g, j].indirect(offsets[:, :DIRECT[g] // 16]))
 
-        def gather_plane(g, j, lo, hi):
+        def gather_plane(g, j, lo, hi, on_vector=False):
             dst = planes[g][:, j * rest[g] + lo - DIRECT[g]:j * rest[g] + hi - DIRECT[g]]
             src = x_raw[g, j].indirect(offsets[:, lo // 16:hi // 16])
-            if (g, j) == (0, 1):
+            if on_vector:
                 nc.vector.tensor_copy(out=dst, in_=src)
             else:
                 nc.scalar.activation(out=dst, in_=src, func=ACT.Copy)
@@ -139,11 +140,17 @@ def tile_picked_deepset_relu_e_kernel(tc, xT, w1, w2_words, w2_scales, offs, out
             nc.tensor.matmul_mx(out=banks[t, a][:], lhsT=w_words[g, t].bitcast(FP8X4), lhsT_scale=w_scales[g, t],
                                 rhs=g_words[g, a][:].bitcast(FP8X4), rhs_scale=g_scales[g, a], start=(g == 0), stop=(g == PASSES - 1))
 
-        for j in range(PACK):
+        gather_direct(0, 0)
+        gather_plane(0, 0, DIRECT[0], S)
+        gather_direct(0, 1)
+        gather_plane(0, 1, DIRECT[0], SECOND_ROW_CUT, True)
+        gather_plane(0, 1, SECOND_ROW_CUT, S)
+        weave(0, DIRECT[0], S, 0, PAIR)
+        for j in range(PAIR, PACK):
             gather_direct(0, j)
             gather_plane(0, j, DIRECT[0], S)
         gather_direct(1, 0)
-        weave(0, DIRECT[0], S, 0, PACK)
+        weave(0, DIRECT[0], S, PAIR, PACK)
         gather_plane(1, 0, DIRECT[1], S)
         quantise_x(0, 0)
         quantise_x(0, 1)
@@ -224,17 +231,19 @@ def tile_picked_deepset_relu_e_kernel(tc, xT, w1, w2_words, w2_scales, offs, out
             nc.vector.quantize_mx(out=z_words[:, lo:hi].bitcast(FP8X4), scales=z_scales[:, lo:hi], in_=z_bf[lo][:])
             nc.tensor.matmul_mx(out=accs[lo][:, :hi - lo], lhsT=w2_w[:].bitcast(FP8X4), lhsT_scale=w2_sc[:], rhs=z_words[:, lo:hi].bitcast(FP8X4), rhs_scale=z_scales[:, lo:hi], start=True, stop=True)
 
-        def store(lo, hi, on_vector):
-            res = keep.tile([P, hi - lo], F32, name=f"res{lo}")
+        res = keep.tile([P, S], F32, name="res")
+
+        def copy_out(lo, hi, on_vector):
             if on_vector:
-                nc.vector.tensor_scalar(out=res[:], in0=accs[lo][:, :hi - lo], scalar1=-1.0 / S, scalar2=None, op0=ALU.mult)
+                nc.vector.tensor_scalar(out=res[:, lo:hi], in0=accs[lo][:, :hi - lo], scalar1=-1.0 / S, scalar2=None, op0=ALU.mult)
             else:
-                nc.scalar.activation(out=res[:], in_=accs[lo][:, :hi - lo], func=ACT.Copy, scale=-1.0 / S)
-            nc.sync.dma_start(out=out[:, lo:hi], in_=res[:])
+                nc.scalar.activation(out=res[:, lo:hi], in_=accs[lo][:, :hi - lo], func=ACT.Copy, scale=-1.0 / S)
 
         for lo, hi, on_vector in Z_PIECES:
             weave_z(lo, hi, on_vector)
         for i, (lo, hi, on_vector) in enumerate(Z_PIECES):
             second_product(i, lo, hi)
         for i, (lo, hi, on_vector) in enumerate(Z_PIECES):
-            store(lo, hi, i >= 3)
+            copy_out(lo, hi, i >= 3)
+        for lo in [HALF, 0, HALF + QUARTER, QUARTER]:
+            nc.sync.dma_start(out=out[:, lo:lo + QUARTER], in_=res[:, lo:lo + QUARTER])

@@ -26,6 +26,8 @@ DIRECT = [384, 256]
 PIECES = [(256, 512), (512, 768), (768, 1024)]
 LAST_CUT = 80
 QUARTER = 256
+WARM = 5
+WARM_M = 32
 SECOND_ROW_CUT = 768
 Z_PIECES = [(512, 768, True), (0, 256, False), (768, 1024, True), (256, 384, False), (384, 512, False)]
 
@@ -205,6 +207,10 @@ def tile_picked_deepset_relu_e_kernel(tc, xT, w1, w2_words, w2_scales, offs, out
 
         for t in range(PACK):
             empty(t)
+        warm = psum.tile([P, HALF], F32, name="warm", tag=f"bank{last}_1")
+        for i in range(WARM):
+            nc.tensor.matmul_mx(out=warm[:WARM_M, :], lhsT=g_words[0, 0][:, :WARM_M].bitcast(FP8X4), lhsT_scale=g_scales[0, 0][:, :WARM_M],
+                                rhs=g_words[0, 0][:].bitcast(FP8X4), rhs_scale=g_scales[0, 0], start=True, stop=True)
         plane(0, 0, S, nc.gpsimd)
         plane(1, 0, S, nc.scalar)
         plane(2, 0, S, nc.vector)

@@ -22,9 +22,9 @@ PASSES = K // K_PASS
 HALF = 512
 HALVES = S // HALF
 PAIR = 2
-DIRECT = [384, 256]
-PIECES = [(256, 512), (512, 768), (768, 1024)]
-LAST_CUT = 80
+DIRECT = 384
+LAST_ROW = [(512, 768), (384, 512), (768, 1024)]
+CUTS = [60, 76]
 QUARTER = 256
 WARM = 5
 WARM_M = 32
@@ -68,36 +68,39 @@ def tile_picked_deepset_relu_e_kernel(tc, xT, w1, w2_words, w2_scales, offs, out
         for q in range(4):
             nc.sync.dma_start(out=w2_sc[32 * q:32 * q + 4, :].bitcast(I32), in_=w2_scales[0, 4 * q:4 * q + 4, :].bitcast(I32))
 
-        rest = [S - d for d in DIRECT]
-        planes = [keep.tile([P, PACK * rest[g]], [F32, BF16][g], name=f"planes{g}", align_bytes=64) for g in range(PASSES)]
+        rest = S - DIRECT
+        planes = keep.tile([P, PACK * rest], F32, name="planes", align_bytes=64)
         woven = [keep.tile([P, PACK * S], BF16, name=f"woven{g}", align_bytes=64) for g in range(PASSES)]
         g_words = {}
         g_scales = {}
         shared_scales = keep.tile([P, HALF], U8, name="shared_scales", align_bytes=64)
-        w_last = keep.tile([P, PACK * K_PASS - 64], BF16, name="w_last", align_bytes=64)
         w_bf = {}
         w_words = {}
         w_scales = {}
 
-        def gather_direct(g, j):
-            nc.vector.tensor_copy(out=woven[g][:].rearrange("p (n j) -> p n j", j=PACK)[:, :DIRECT[g], j], in_=x_raw[g, j].indirect(offsets[:, :DIRECT[g] // 16]))
-
-        def gather_plane(g, j, lo, hi, on_vector=False):
-            dst = planes[g][:, j * rest[g] + lo - DIRECT[g]:j * rest[g] + hi - DIRECT[g]]
+        def place(g, j, lo, hi, on_vector):
+            dst = woven[g][:].rearrange("p (n j) -> p n j", j=PACK)[:, lo:hi, j]
             src = x_raw[g, j].indirect(offsets[:, lo // 16:hi // 16])
             if on_vector:
                 nc.vector.tensor_copy(out=dst, in_=src)
             else:
                 nc.scalar.activation(out=dst, in_=src, func=ACT.Copy)
 
-        def weave(g, lo, hi, j0, j1):
-            run = j1 - j0
-            dst = woven[g][:, lo * PACK:hi * PACK].rearrange("p (c i j) -> p c j i", i=run, j=PACK)[:, :, j0:j1, :]
-            src = planes[g][:].rearrange("p (j n) -> p j n", j=PACK)[:, j0:j1, lo - DIRECT[g]:hi - DIRECT[g]].rearrange("p j (c i) -> p c j i", i=run)
+        def gather_plane(j, lo, hi, on_vector=False):
+            dst = planes[:, j * rest + lo - DIRECT:j * rest + hi - DIRECT]
+            src = x_raw[0, j].indirect(offsets[:, lo // 16:hi // 16])
+            if on_vector:
+                nc.vector.tensor_copy(out=dst, in_=src)
+            else:
+                nc.scalar.activation(out=dst, in_=src, func=ACT.Copy)
+
+        def weave(j0):
+            dst = woven[0][:, DIRECT * PACK:].rearrange("p (c i j) -> p c j i", i=PAIR, j=PACK)[:, :, j0:j0 + PAIR, :]
+            src = planes[:].rearrange("p (j n) -> p j n", j=PACK)[:, j0:j0 + PAIR, :].rearrange("p j (c i) -> p c j i", i=PAIR)
             nc.vector.tensor_copy(out=dst, in_=src)
 
         def quantise_x(g, a, lo=0, hi=HALF):
-            if lo == 0:
+            if (g, a) not in g_words:
                 g_words[g, a] = keep.tile([P, HALF], U32, name=f"g_words{g}_{a}", align_bytes=64)
                 if (g, a) == (1, 0):
                     g_scales[g, a] = shared_scales[4:, :]
@@ -107,12 +110,8 @@ def tile_picked_deepset_relu_e_kernel(tc, xT, w1, w2_words, w2_scales, offs, out
             nc.vector.quantize_mx(out=g_words[g, a][:, lo:hi].bitcast(FP8X4), scales=g_scales[g, a][:, lo:hi], in_=woven[g][:, (a * HALF + lo) * PACK:(a * HALF + hi) * PACK])
 
         def round_w(g, u, cut):
-            if g == 1:
-                lo = (1 - u) * (PAIR * K_PASS - 64)
-                w_bf[g, u] = w_last[:, lo:lo + PAIR * K_PASS]
-            else:
-                own = keep.tile([P, PAIR * K_PASS], BF16, name=f"w_bf{g}_{u}", align_bytes=64)
-                w_bf[g, u] = own[:]
+            own = keep.tile([P, PAIR * K_PASS], BF16, name=f"w_bf{g}_{u}", align_bytes=64)
+            w_bf[g, u] = own[:]
             dst = w_bf[g, u].rearrange("p (t m j) -> p m j t", t=PAIR, j=PACK)
             src = w_raw[g][:].rearrange("p (j m t) -> p m j t", j=PACK, t=PACK)[:, :, :, PAIR * u:PAIR * (u + 1)]
             if cut > 0:
@@ -142,25 +141,23 @@ def tile_picked_deepset_relu_e_kernel(tc, xT, w1, w2_words, w2_scales, offs, out
             nc.tensor.matmul_mx(out=banks[t, a][:], lhsT=w_words[g, t].bitcast(FP8X4), lhsT_scale=w_scales[g, t],
                                 rhs=g_words[g, a][:].bitcast(FP8X4), rhs_scale=g_scales[g, a], start=(g == 0), stop=(g == PASSES - 1))
 
-        gather_direct(0, 0)
-        gather_plane(0, 0, DIRECT[0], S)
-        gather_direct(0, 1)
-        gather_plane(0, 1, DIRECT[0], SECOND_ROW_CUT, True)
-        gather_plane(0, 1, SECOND_ROW_CUT, S)
-        weave(0, DIRECT[0], S, 0, PAIR)
+        place(0, 0, 0, DIRECT, True)
+        gather_plane(0, DIRECT, S)
+        place(0, 1, 0, DIRECT, True)
+        gather_plane(1, DIRECT, SECOND_ROW_CUT, True)
+        gather_plane(1, SECOND_ROW_CUT, S)
+        weave(0)
         for j in range(PAIR, PACK):
-            gather_direct(0, j)
-            gather_plane(0, j, DIRECT[0], S)
-        gather_direct(1, 0)
-        weave(0, DIRECT[0], S, PAIR, PACK)
-        gather_plane(1, 0, DIRECT[1], S)
+            place(0, j, 0, DIRECT, True)
+            gather_plane(j, DIRECT, S)
+        place(1, 0, 0, DIRECT, True)
+        weave(PAIR)
+        place(1, 0, DIRECT, S, False)
         quantise_x(0, 0)
         quantise_x(0, 1)
-        gather_direct(1, 1)
-        gather_plane(1, 1, DIRECT[1], S)
-        weave(1, DIRECT[1], S, 0, PAIR)
-        gather_direct(1, 2)
-        gather_plane(1, 2, DIRECT[1], S)
+        for j in range(1, PACK - 1):
+            place(1, j, 0, DIRECT, True)
+            place(1, j, DIRECT, S, False)
         round_w(0, 0, P)
         round_w(0, 1, 0)
         quantise_w(0, 2, 4)
@@ -169,21 +166,18 @@ def tile_picked_deepset_relu_e_kernel(tc, xT, w1, w2_words, w2_scales, offs, out
         for t in [2, 3, 0]:
             for a in range(HALVES):
                 first_product(0, t, a)
-        gather_direct(1, 3)
-        for lo, hi in PIECES:
-            gather_plane(1, 3, lo, hi)
-        weave(1, *PIECES[0], PAIR, PACK)
-        weave(1, *PIECES[1], PAIR, PACK)
+        place(1, PACK - 1, 0, DIRECT, True)
+        for lo, hi in LAST_ROW:
+            place(1, PACK - 1, lo, hi, False)
+        quantise_x(1, 1, 0, HALF // 2)
         quantise_x(1, 0)
         for a in range(HALVES):
             first_product(0, 1, a)
-        weave(1, *PIECES[2], PAIR, PACK)
-        quantise_x(1, 1, 0, HALF // 2)
         quantise_x(1, 1, HALF // 2, HALF)
-        round_w(1, 0, P)
+        for u in range(PAIR):
+            round_w(1, u, CUTS[u])
         quantise_w(1, 0, 1)
         quantise_w(1, 1, 2)
-        round_w(1, 1, LAST_CUT)
         quantise_w(1, 2, 4)
         for t, a in [(0, 0), (1, 0), (0, 1), (1, 1), (2, 0), (2, 1), (3, 0), (3, 1)]:
             first_product(1, t, a)

@@ -23,12 +23,12 @@ HALF = 512
 HALVES = S // HALF
 PAIR = 2
 DIRECT = 384
-LAST_ROW = [(512, 768), (384, 512), (768, 1024)]
-CUTS = [60, 76]
+PLACED = 448
+LAST_ROW = [(PLACED, 768), (768, 1024)]
+CUTS = [72, 84]
 QUARTER = 256
 WARM = 5
 WARM_M = 32
-SECOND_ROW_CUT = 768
 Z_PIECES = [(512, 768, True), (0, 256, False), (768, 1024, True), (256, 384, False), (384, 512, False)]
 
 
@@ -56,9 +56,10 @@ def tile_picked_deepset_relu_e_kernel(tc, xT, w1, w2_words, w2_scales, offs, out
             w_raw[g] = keep.tile([P, PACK * H], F32, name=f"w_raw{g}", align_bytes=64)
             nc.sync.dma_start(out=w_raw[g][:], in_=w1[g * K_PASS:(g + 1) * K_PASS, :].rearrange("(p j) w -> p (j w)", j=PACK))
 
-        load_x(0, 0, PAIR)
+        load_x(0, 0, 1)
         nc.sync.dma_start(offsets[:], offs)
-        load_x(0, PAIR, PAIR)
+        for j in range(1, PACK):
+            load_x(0, j, 1)
         for j in range(PACK - 1):
             load_x(1, j, 1)
         load_w(0)
@@ -69,7 +70,7 @@ def tile_picked_deepset_relu_e_kernel(tc, xT, w1, w2_words, w2_scales, offs, out
             nc.sync.dma_start(out=w2_sc[32 * q:32 * q + 4, :].bitcast(I32), in_=w2_scales[0, 4 * q:4 * q + 4, :].bitcast(I32))
 
         rest = S - DIRECT
-        planes = keep.tile([P, PACK * rest], F32, name="planes", align_bytes=64)
+        planes = keep.tile([P, PACK * rest], BF16, name="planes", align_bytes=64)
         woven = [keep.tile([P, PACK * S], BF16, name=f"woven{g}", align_bytes=64) for g in range(PASSES)]
         g_words = {}
         g_scales = {}
@@ -86,13 +87,8 @@ def tile_picked_deepset_relu_e_kernel(tc, xT, w1, w2_words, w2_scales, offs, out
             else:
                 nc.scalar.activation(out=dst, in_=src, func=ACT.Copy)
 
-        def gather_plane(j, lo, hi, on_vector=False):
-            dst = planes[:, j * rest + lo - DIRECT:j * rest + hi - DIRECT]
-            src = x_raw[0, j].indirect(offsets[:, lo // 16:hi // 16])
-            if on_vector:
-                nc.vector.tensor_copy(out=dst, in_=src)
-            else:
-                nc.scalar.activation(out=dst, in_=src, func=ACT.Copy)
+        def gather_plane(j):
+            nc.scalar.activation(out=planes[:, j * rest:(j + 1) * rest], in_=x_raw[0, j].indirect(offsets[:, DIRECT // 16:]), func=ACT.Copy)
 
         def weave(j0):
             dst = woven[0][:, DIRECT * PACK:].rearrange("p (c i j) -> p c j i", i=PAIR, j=PACK)[:, :, j0:j0 + PAIR, :]
@@ -141,23 +137,18 @@ def tile_picked_deepset_relu_e_kernel(tc, xT, w1, w2_words, w2_scales, offs, out
             nc.tensor.matmul_mx(out=banks[t, a][:], lhsT=w_words[g, t].bitcast(FP8X4), lhsT_scale=w_scales[g, t],
                                 rhs=g_words[g, a][:].bitcast(FP8X4), rhs_scale=g_scales[g, a], start=(g == 0), stop=(g == PASSES - 1))
 
-        place(0, 0, 0, DIRECT, True)
-        gather_plane(0, DIRECT, S)
-        place(0, 1, 0, DIRECT, True)
-        gather_plane(1, DIRECT, SECOND_ROW_CUT, True)
-        gather_plane(1, SECOND_ROW_CUT, S)
-        weave(0)
-        for j in range(PAIR, PACK):
+        for j in range(PACK):
             place(0, j, 0, DIRECT, True)
-            gather_plane(j, DIRECT, S)
-        place(1, 0, 0, DIRECT, True)
-        weave(PAIR)
-        place(1, 0, DIRECT, S, False)
+            gather_plane(j)
+            if j % PAIR == 1:
+                weave(j - 1)
+        place(1, 0, 0, PLACED, True)
+        place(1, 0, PLACED, S, False)
         quantise_x(0, 0)
         quantise_x(0, 1)
         for j in range(1, PACK - 1):
-            place(1, j, 0, DIRECT, True)
-            place(1, j, DIRECT, S, False)
+            place(1, j, 0, PLACED, True)
+            place(1, j, PLACED, S, False)
         round_w(0, 0, P)
         round_w(0, 1, 0)
         quantise_w(0, 2, 4)
@@ -166,7 +157,7 @@ def tile_picked_deepset_relu_e_kernel(tc, xT, w1, w2_words, w2_scales, offs, out
         for t in [2, 3, 0]:
             for a in range(HALVES):
                 first_product(0, t, a)
-        place(1, PACK - 1, 0, DIRECT, True)
+        place(1, PACK - 1, 0, PLACED, True)
         for lo, hi in LAST_ROW:
             place(1, PACK - 1, lo, hi, False)
         quantise_x(1, 1, 0, HALF // 2)

@@ -25,7 +25,7 @@ PAIR = 2
 DIRECT = 384
 PLACED = 448
 LAST_ROW = [(PLACED, 768), (768, 1024)]
-CUTS = [72, 84]
+CUTS = [56, 84]
 QUARTER = 256
 WARM = 5
 WARM_M = 32
@@ -71,7 +71,7 @@ def tile_picked_deepset_relu_e_kernel(tc, xT, w1, w2_words, w2_scales, offs, out
 
         rest = S - DIRECT
         planes = keep.tile([P, PACK * rest], BF16, name="planes", align_bytes=64)
-        woven = [keep.tile([P, PACK * S], BF16, name=f"woven{g}", align_bytes=64) for g in range(PASSES)]
+        woven = [keep.tile([P, PACK * S + g * PAIR * K_PASS], BF16, name=f"woven{g}", align_bytes=64) for g in range(PASSES)]
         g_words = {}
         g_scales = {}
         shared_scales = keep.tile([P, HALF], U8, name="shared_scales", align_bytes=64)
@@ -80,7 +80,7 @@ def tile_picked_deepset_relu_e_kernel(tc, xT, w1, w2_words, w2_scales, offs, out
         w_scales = {}
 
         def place(g, j, lo, hi, on_vector):
-            dst = woven[g][:].rearrange("p (n j) -> p n j", j=PACK)[:, lo:hi, j]
+            dst = woven[g][:, :PACK * S].rearrange("p (n j) -> p n j", j=PACK)[:, lo:hi, j]
             src = x_raw[g, j].indirect(offsets[:, lo // 16:hi // 16])
             if on_vector:
                 nc.vector.tensor_copy(out=dst, in_=src)
@@ -97,17 +97,21 @@ def tile_picked_deepset_relu_e_kernel(tc, xT, w1, w2_words, w2_scales, offs, out
 
         def quantise_x(g, a, lo=0, hi=HALF):
             if (g, a) not in g_words:
-                g_words[g, a] = keep.tile([P, HALF], U32, name=f"g_words{g}_{a}", align_bytes=64)
+                width = HALF + P if (g, a) == (1, 1) else HALF
+                g_words[g, a] = keep.tile([P, width], U32, name=f"g_words{g}_{a}", align_bytes=64)
                 if (g, a) == (1, 0):
                     g_scales[g, a] = shared_scales[4:, :]
                 else:
-                    own = keep.tile([P, HALF], U8, name=f"g_scales{g}_{a}", align_bytes=64)
+                    own = keep.tile([P, width], U8, name=f"g_scales{g}_{a}", align_bytes=64)
                     g_scales[g, a] = own[:]
             nc.vector.quantize_mx(out=g_words[g, a][:, lo:hi].bitcast(FP8X4), scales=g_scales[g, a][:, lo:hi], in_=woven[g][:, (a * HALF + lo) * PACK:(a * HALF + hi) * PACK])
 
         def round_w(g, u, cut):
-            own = keep.tile([P, PAIR * K_PASS], BF16, name=f"w_bf{g}_{u}", align_bytes=64)
-            w_bf[g, u] = own[:]
+            if (g, u) == (1, 0):
+                w_bf[g, u] = woven[g][:, PACK * S:]
+            else:
+                own = keep.tile([P, PAIR * K_PASS], BF16, name=f"w_bf{g}_{u}", align_bytes=64)
+                w_bf[g, u] = own[:]
             dst = w_bf[g, u].rearrange("p (t m j) -> p m j t", t=PAIR, j=PACK)
             src = w_raw[g][:].rearrange("p (j m t) -> p m j t", j=PACK, t=PACK)[:, :, :, PAIR * u:PAIR * (u + 1)]
             if cut > 0:
@@ -135,7 +139,7 @@ def tile_picked_deepset_relu_e_kernel(tc, xT, w1, w2_words, w2_scales, offs, out
 
         def first_product(g, t, a):
             nc.tensor.matmul_mx(out=banks[t, a][:], lhsT=w_words[g, t].bitcast(FP8X4), lhsT_scale=w_scales[g, t],
-                                rhs=g_words[g, a][:].bitcast(FP8X4), rhs_scale=g_scales[g, a], start=(g == 0), stop=(g == PASSES - 1))
+                                rhs=g_words[g, a][:, :HALF].bitcast(FP8X4), rhs_scale=g_scales[g, a][:, :HALF], start=(g == 0), stop=(g == PASSES - 1))
 
         for j in range(PACK):
             place(0, j, 0, DIRECT, True)
@@ -164,13 +168,14 @@ def tile_picked_deepset_relu_e_kernel(tc, xT, w1, w2_words, w2_scales, offs, out
         quantise_x(1, 0)
         for a in range(HALVES):
             first_product(0, 1, a)
-        quantise_x(1, 1, HALF // 2, HALF)
         for u in range(PAIR):
             round_w(1, u, CUTS[u])
-        quantise_w(1, 0, 1)
         quantise_w(1, 1, 2)
+        quantise_x(1, 1, HALF // 2, HALF + P)
+        w_words[1, 0] = g_words[1, 1][:, HALF:]
+        w_scales[1, 0] = g_scales[1, 1][:, HALF:]
         quantise_w(1, 2, 4)
-        for t, a in [(0, 0), (1, 0), (0, 1), (1, 1), (2, 0), (2, 1), (3, 0), (3, 1)]:
+        for t, a in [(1, 0), (1, 1), (0, 0), (0, 1), (2, 0), (2, 1), (3, 0), (3, 1)]:
             first_product(1, t, a)
         last = PACK - 1
 
@@ -190,14 +195,14 @@ def tile_picked_deepset_relu_e_kernel(tc, xT, w1, w2_words, w2_scales, offs, out
             else:
                 engine.tensor_scalar(out=z_planes[:, t, lo:hi], in0=h[:, t, lo:hi], scalar1=-float(S), scalar2=totals[:, t:t + 1], op0=ALU.mult, op1=ALU.add)
 
-        for t in range(PACK):
+        for t in [1, 0, 2, 3]:
             empty(t)
         warm = psum.tile([P, HALF], F32, name="warm", tag=f"bank{last}_1")
         for i in range(WARM):
             nc.tensor.matmul_mx(out=warm[:WARM_M, :], lhsT=g_words[0, 0][:, :WARM_M].bitcast(FP8X4), lhsT_scale=g_scales[0, 0][:, :WARM_M],
                                 rhs=g_words[0, 0][:].bitcast(FP8X4), rhs_scale=g_scales[0, 0], start=True, stop=True)
-        plane(0, 0, S, nc.gpsimd)
-        plane(1, 0, S, nc.scalar)
+        plane(1, 0, S, nc.gpsimd)
+        plane(0, 0, S, nc.scalar)
         plane(2, 0, S, nc.vector)
         plane(last, 0, QUARTER, nc.scalar)
         plane(last, HALF, S, nc.vector)

@@ -39,21 +39,21 @@ def tile_picked_deepset_relu_e_kernel(tc, xT, w1, w2_words, w2_scales, offs, out
         psum = ctx.enter_context(tc.psum_pool(name="psum", bufs=1))
 
         offsets = keep.tile([P, S // 16], U16, name="offsets")
-        w2_sc = keep.tile([P, N], U8, name="w2_sc", align_bytes=64)
+        w2_sc = keep.tile([P, N], U8, name="w2_sc", align_bytes=256)
         nc.vector.memset(w2_sc[:].bitcast(I32), 0)
-        w2_w = keep.tile([P, N], U32, name="w2_w", align_bytes=64)
+        w2_w = keep.tile([P, N], U32, name="w2_w", align_bytes=256)
 
         x_raw = {}
         w_raw = {}
 
         def load_x(g, j, rows):
-            tile = keep.tile([P, rows * T], F32, name=f"x_raw{g}_{j}", align_bytes=64)
+            tile = keep.tile([P, rows * T], F32, name=f"x_raw{g}_{j}", align_bytes=256)
             nc.sync.dma_start(out=tile[:], in_=xT[g * K_PASS:(g + 1) * K_PASS, :].rearrange("(p j) w -> p (j w)", j=PACK)[:, j * T:(j + rows) * T])
             for r in range(rows):
                 x_raw[g, j + r] = tile[:, r * T:(r + 1) * T]
 
         def load_w(g):
-            w_raw[g] = keep.tile([P, PACK * H], F32, name=f"w_raw{g}", align_bytes=64)
+            w_raw[g] = keep.tile([P, PACK * H], F32, name=f"w_raw{g}", align_bytes=256)
             nc.sync.dma_start(out=w_raw[g][:], in_=w1[g * K_PASS:(g + 1) * K_PASS, :].rearrange("(p j) w -> p (j w)", j=PACK))
 
         load_x(0, 0, 1)
@@ -70,11 +70,11 @@ def tile_picked_deepset_relu_e_kernel(tc, xT, w1, w2_words, w2_scales, offs, out
             nc.sync.dma_start(out=w2_sc[32 * q:32 * q + 4, :].bitcast(I32), in_=w2_scales[0, 4 * q:4 * q + 4, :].bitcast(I32))
 
         rest = S - DIRECT
-        planes = keep.tile([P, PACK * rest], BF16, name="planes", align_bytes=64)
-        woven = [keep.tile([P, PACK * S + g * PAIR * K_PASS], BF16, name=f"woven{g}", align_bytes=64) for g in range(PASSES)]
+        planes = keep.tile([P, PACK * rest], BF16, name="planes", align_bytes=256)
+        woven = [keep.tile([P, PACK * S + g * PAIR * K_PASS], BF16, name=f"woven{g}", align_bytes=256) for g in range(PASSES)]
         g_words = {}
         g_scales = {}
-        shared_scales = keep.tile([P, HALF], U8, name="shared_scales", align_bytes=64)
+        shared_scales = keep.tile([P, HALF], U8, name="shared_scales", align_bytes=256)
         w_bf = {}
         w_words = {}
         w_scales = {}
@@ -98,11 +98,11 @@ def tile_picked_deepset_relu_e_kernel(tc, xT, w1, w2_words, w2_scales, offs, out
         def quantise_x(g, a, lo=0, hi=HALF):
             if (g, a) not in g_words:
                 width = HALF + P if (g, a) == (1, 1) else HALF
-                g_words[g, a] = keep.tile([P, width], U32, name=f"g_words{g}_{a}", align_bytes=64)
+                g_words[g, a] = keep.tile([P, width], U32, name=f"g_words{g}_{a}", align_bytes=256)
                 if (g, a) == (1, 0):
                     g_scales[g, a] = shared_scales[4:, :]
                 else:
-                    own = keep.tile([P, width], U8, name=f"g_scales{g}_{a}", align_bytes=64)
+                    own = keep.tile([P, width], U8, name=f"g_scales{g}_{a}", align_bytes=256)
                     g_scales[g, a] = own[:]
             nc.vector.quantize_mx(out=g_words[g, a][:, lo:hi].bitcast(FP8X4), scales=g_scales[g, a][:, lo:hi], in_=woven[g][:, (a * HALF + lo) * PACK:(a * HALF + hi) * PACK])
 
@@ -110,7 +110,7 @@ def tile_picked_deepset_relu_e_kernel(tc, xT, w1, w2_words, w2_scales, offs, out
             if (g, u) == (1, 0):
                 w_bf[g, u] = woven[g][:, PACK * S:]
             else:
-                own = keep.tile([P, PAIR * K_PASS], BF16, name=f"w_bf{g}_{u}", align_bytes=64)
+                own = keep.tile([P, PAIR * K_PASS], BF16, name=f"w_bf{g}_{u}", align_bytes=256)
                 w_bf[g, u] = own[:]
             dst = w_bf[g, u].rearrange("p (t m j) -> p m j t", t=PAIR, j=PACK)
             src = w_raw[g][:].rearrange("p (j m t) -> p m j t", j=PACK, t=PACK)[:, :, :, PAIR * u:PAIR * (u + 1)]
@@ -120,11 +120,11 @@ def tile_picked_deepset_relu_e_kernel(tc, xT, w1, w2_words, w2_scales, offs, out
                 nc.vector.tensor_copy(out=dst[:, cut:], in_=src[:, cut:])
 
         def quantise_w(g, t0, t1):
-            words = keep.tile([P, (t1 - t0) * P], U32, name=f"w_words{g}_{t0}", align_bytes=64)
+            words = keep.tile([P, (t1 - t0) * P], U32, name=f"w_words{g}_{t0}", align_bytes=256)
             if (g, t0) == (0, 1):
                 scales = shared_scales[:, :P]
             else:
-                own = keep.tile([P, (t1 - t0) * P], U8, name=f"w_scales{g}_{t0}", align_bytes=64)
+                own = keep.tile([P, (t1 - t0) * P], U8, name=f"w_scales{g}_{t0}", align_bytes=256)
                 scales = own[:]
             lo = t0 % PAIR * K_PASS
             nc.vector.quantize_mx(out=words[:].bitcast(FP8X4), scales=scales, in_=w_bf[g, t0 // PAIR][:, lo:lo + (t1 - t0) * K_PASS])
@@ -180,10 +180,10 @@ def tile_picked_deepset_relu_e_kernel(tc, xT, w1, w2_words, w2_scales, offs, out
         last = PACK - 1
 
 
-        h = keep.tile([P, PACK, S], F32, name="h")
+        h = keep.tile([P, PACK, S], F32, name="h", align_bytes=256)
         sums = keep.tile([P, PACK], F32, name="sums")
         totals = keep.tile([P, PACK], F32, name="totals")
-        z_planes = keep.tile([P, PACK, S], BF16, name="z_planes", align_bytes=64)
+        z_planes = keep.tile([P, PACK, S], BF16, name="z_planes", align_bytes=256)
 
         def empty(t):
             nc.scalar.activation(out=h[:, t, :HALF], in_=banks[t, 0][:], func=ACT.Relu, accum_out=sums[:, t:t + 1])
@@ -208,13 +208,13 @@ def tile_picked_deepset_relu_e_kernel(tc, xT, w1, w2_words, w2_scales, offs, out
         plane(last, HALF, S, nc.vector)
         plane(last, QUARTER, HALF, nc.vector)
 
-        z_words = keep.tile([P, S], U32, name="z_words", align_bytes=64)
-        z_scales = keep.tile([P, S], U8, name="z_scales", align_bytes=64)
+        z_words = keep.tile([P, S], U32, name="z_words", align_bytes=256)
+        z_scales = keep.tile([P, S], U8, name="z_scales", align_bytes=256)
         z_bf = {}
         accs = {}
 
         def weave_z(lo, hi, on_vector):
-            z_bf[lo] = keep.tile([P, (hi - lo) * PACK], BF16, name=f"z_bf{lo}", align_bytes=64)
+            z_bf[lo] = keep.tile([P, (hi - lo) * PACK], BF16, name=f"z_bf{lo}", align_bytes=256)
             dst = z_bf[lo][:].rearrange("p (c i t) -> p c t i", i=4, t=PACK)
             src = z_planes[:, :, lo:hi].rearrange("p t (c i) -> p c t i", i=4)
             if on_vector:
@@ -227,7 +227,7 @@ def tile_picked_deepset_relu_e_kernel(tc, xT, w1, w2_words, w2_scales, offs, out
             nc.vector.quantize_mx(out=z_words[:, lo:hi].bitcast(FP8X4), scales=z_scales[:, lo:hi], in_=z_bf[lo][:])
             nc.tensor.matmul_mx(out=accs[lo][:, :hi - lo], lhsT=w2_w[:].bitcast(FP8X4), lhsT_scale=w2_sc[:], rhs=z_words[:, lo:hi].bitcast(FP8X4), rhs_scale=z_scales[:, lo:hi], start=True, stop=True)
 
-        res = keep.tile([P, S], F32, name="res")
+        res = keep.tile([P, S], F32, name="res", align_bytes=256)
 
         def copy_out(lo, hi, on_vector):
             if on_vector:

@@ -26,6 +26,7 @@ DIRECT = 384
 PLACED = 448
 LAST_ROW = [(PLACED, 768), (768, 1024)]
 CUTS = [56, 84]
+FIRST_CUT = 104
 QUARTER = 256
 WARM = 5
 WARM_M = 32
@@ -71,6 +72,7 @@ def tile_picked_deepset_relu_e_kernel(tc, xT, w1, w2_words, w2_scales, offs, out
 
         rest = S - DIRECT
         planes = keep.tile([P, PACK * rest], BF16, name="planes", align_bytes=256)
+        own_planes = keep.tile([P, PAIR, PLACED], BF16, name="own_planes", align_bytes=256)
         woven = [keep.tile([P, PACK * S + g * PAIR * K_PASS], BF16, name=f"woven{g}", align_bytes=256) for g in range(PASSES)]
         g_words = {}
         g_scales = {}
@@ -94,6 +96,13 @@ def tile_picked_deepset_relu_e_kernel(tc, xT, w1, w2_words, w2_scales, offs, out
             dst = woven[0][:, DIRECT * PACK:].rearrange("p (c i j) -> p c j i", i=PAIR, j=PACK)[:, :, j0:j0 + PAIR, :]
             src = planes[:].rearrange("p (j n) -> p j n", j=PACK)[:, j0:j0 + PAIR, :].rearrange("p j (c i) -> p c j i", i=PAIR)
             nc.vector.tensor_copy(out=dst, in_=src)
+
+        def gather_own(j):
+            nc.vector.tensor_copy(out=own_planes[:, j, :], in_=x_raw[1, j].indirect(offsets[:, :PLACED // 16]))
+
+        def weave_own():
+            dst = woven[1][:, :PLACED * PACK].rearrange("p (c i j) -> p c j i", i=PACK, j=PACK)[:, :, :PAIR, :]
+            nc.vector.tensor_copy(out=dst, in_=own_planes[:].rearrange("p j (c i) -> p c j i", i=PACK))
 
         def quantise_x(g, a, lo=0, hi=HALF):
             if (g, a) not in g_words:
@@ -146,14 +155,16 @@ def tile_picked_deepset_relu_e_kernel(tc, xT, w1, w2_words, w2_scales, offs, out
             gather_plane(j)
             if j % PAIR == 1:
                 weave(j - 1)
-        place(1, 0, 0, PLACED, True)
+        gather_own(0)
         place(1, 0, PLACED, S, False)
         quantise_x(0, 0)
         quantise_x(0, 1)
-        for j in range(1, PACK - 1):
-            place(1, j, 0, PLACED, True)
-            place(1, j, PLACED, S, False)
-        round_w(0, 0, P)
+        gather_own(1)
+        place(1, 1, PLACED, S, False)
+        weave_own()
+        place(1, 2, 0, PLACED, True)
+        place(1, 2, PLACED, S, False)
+        round_w(0, 0, FIRST_CUT)
         round_w(0, 1, 0)
         quantise_w(0, 2, 4)
         quantise_w(0, 0, 1)

@@ -25,8 +25,7 @@ PAIR = 2
 DIRECT = 384
 PLACED = 448
 LAST_ROW = [(PLACED, 768), (768, 1024)]
-CUTS = [56, 84]
-FIRST_CUT = 104
+CUTS = [[112, 24], [72, 96]]
 QUARTER = 256
 WARM = 5
 WARM_M = 32
@@ -164,12 +163,12 @@ def tile_picked_deepset_relu_e_kernel(tc, xT, w1, w2_words, w2_scales, offs, out
         weave_own()
         place(1, 2, 0, PLACED, True)
         place(1, 2, PLACED, S, False)
-        round_w(0, 0, FIRST_CUT)
-        round_w(0, 1, 0)
-        quantise_w(0, 2, 4)
+        for u in range(PAIR):
+            round_w(0, u, CUTS[0][u])
         quantise_w(0, 0, 1)
         quantise_w(0, 1, 2)
-        for t in [2, 3, 0]:
+        quantise_w(0, 2, 4)
+        for t in [0, 2, 3]:
             for a in range(HALVES):
                 first_product(0, t, a)
         place(1, PACK - 1, 0, PLACED, True)
@@ -180,7 +179,7 @@ def tile_picked_deepset_relu_e_kernel(tc, xT, w1, w2_words, w2_scales, offs, out
         for a in range(HALVES):
             first_product(0, 1, a)
         for u in range(PAIR):
-            round_w(1, u, CUTS[u])
+            round_w(1, u, CUTS[1][u])
         quantise_w(1, 1, 2)
         quantise_x(1, 1, HALF // 2, HALF + P)
         w_words[1, 0] = g_words[1, 1][:, HALF:]

@@ -25,7 +25,7 @@ PAIR = 2
 DIRECT = 384
 PLACED = 448
 LAST_ROW = [(PLACED, 768), (768, 1024)]
-CUTS = [[112, 24], [72, 96]]
+CUTS = [[112, 24], [64, 90]]
 QUARTER = 256
 WARM = 5
 WARM_M = 32

from contextlib import ExitStack

import concourse.mybir as mybir

K, T, S, H, N = 1024, 2048, 1024, 512, 128
FLOPS = 2 * K * H * S + 2 * H * N * S

F32 = mybir.dt.float32
BF16 = mybir.dt.bfloat16
I32 = mybir.dt.int32
U32 = mybir.dt.uint32
U16 = mybir.dt.uint16
U8 = mybir.dt.uint8
FP8X4 = mybir.dt.float8_e4m3fn_x4
ALU = mybir.AluOpType
ACT = mybir.ActivationFunctionType

P = 128
PACK = 4
K_PASS = P * PACK
PASSES = K // K_PASS
HALF = 512
HALVES = S // HALF
PAIR = 2
DIRECT = 384
PLACED = 448
LAST_ROW = [(PLACED, 768), (768, 1024)]
CUTS = [[112, 24], [64, 90]]
QUARTER = 256
WARM = 5
WARM_M = 32
Z_PIECES = [(512, 768, True), (0, 256, False), (768, 1024, True), (256, 384, False), (384, 512, False)]


def tile_picked_deepset_relu_e_kernel(tc, xT, w1, w2_words, w2_scales, offs, out):
    nc = tc.nc
    with ExitStack() as ctx:
        keep = ctx.enter_context(tc.tile_pool(name="keep", bufs=1))
        psum = ctx.enter_context(tc.psum_pool(name="psum", bufs=1))

        offsets = keep.tile([P, S // 16], U16, name="offsets")
        w2_sc = keep.tile([P, N], U8, name="w2_sc", align_bytes=256)
        nc.vector.memset(w2_sc[:].bitcast(I32), 0)
        w2_w = keep.tile([P, N], U32, name="w2_w", align_bytes=256)

        x_raw = {}
        w_raw = {}

        def load_x(g, j, rows):
            tile = keep.tile([P, rows * T], F32, name=f"x_raw{g}_{j}", align_bytes=256)
            nc.sync.dma_start(out=tile[:], in_=xT[g * K_PASS:(g + 1) * K_PASS, :].rearrange("(p j) w -> p (j w)", j=PACK)[:, j * T:(j + rows) * T])
            for r in range(rows):
                x_raw[g, j + r] = tile[:, r * T:(r + 1) * T]

        def load_w(g):
            w_raw[g] = keep.tile([P, PACK * H], F32, name=f"w_raw{g}", align_bytes=256)
            nc.sync.dma_start(out=w_raw[g][:], in_=w1[g * K_PASS:(g + 1) * K_PASS, :].rearrange("(p j) w -> p (j w)", j=PACK))

        load_x(0, 0, 1)
        nc.sync.dma_start(offsets[:], offs)
        for j in range(1, PACK):
            load_x(0, j, 1)
        for j in range(PACK - 1):
            load_x(1, j, 1)
        load_w(0)
        load_x(1, PACK - 1, 1)
        load_w(1)
        nc.sync.dma_start(out=w2_w[:].bitcast(I32), in_=w2_words[0].rearrange("p n t -> p (n t)").bitcast(I32))
        for q in range(4):
            nc.sync.dma_start(out=w2_sc[32 * q:32 * q + 4, :].bitcast(I32), in_=w2_scales[0, 4 * q:4 * q + 4, :].bitcast(I32))

        rest = S - DIRECT
        planes = keep.tile([P, PACK * rest], BF16, name="planes", align_bytes=256)
        own_planes = keep.tile([P, PAIR, PLACED], BF16, name="own_planes", align_bytes=256)
        woven = [keep.tile([P, PACK * S + g * PAIR * K_PASS], BF16, name=f"woven{g}", align_bytes=256) for g in range(PASSES)]
        g_words = {}
        g_scales = {}
        shared_scales = keep.tile([P, HALF], U8, name="shared_scales", align_bytes=256)
        w_bf = {}
        w_words = {}
        w_scales = {}

        def place(g, j, lo, hi, on_vector):
            dst = woven[g][:, :PACK * S].rearrange("p (n j) -> p n j", j=PACK)[:, lo:hi, j]
            src = x_raw[g, j].indirect(offsets[:, lo // 16:hi // 16])
            if on_vector:
                nc.vector.tensor_copy(out=dst, in_=src)
            else:
                nc.scalar.activation(out=dst, in_=src, func=ACT.Copy)

        def gather_plane(j):
            nc.scalar.activation(out=planes[:, j * rest:(j + 1) * rest], in_=x_raw[0, j].indirect(offsets[:, DIRECT // 16:]), func=ACT.Copy)

        def weave(j0):
            dst = woven[0][:, DIRECT * PACK:].rearrange("p (c i j) -> p c j i", i=PAIR, j=PACK)[:, :, j0:j0 + PAIR, :]
            src = planes[:].rearrange("p (j n) -> p j n", j=PACK)[:, j0:j0 + PAIR, :].rearrange("p j (c i) -> p c j i", i=PAIR)
            nc.vector.tensor_copy(out=dst, in_=src)

        def gather_own(j):
            nc.vector.tensor_copy(out=own_planes[:, j, :], in_=x_raw[1, j].indirect(offsets[:, :PLACED // 16]))

        def weave_own():
            dst = woven[1][:, :PLACED * PACK].rearrange("p (c i j) -> p c j i", i=PACK, j=PACK)[:, :, :PAIR, :]
            nc.vector.tensor_copy(out=dst, in_=own_planes[:].rearrange("p j (c i) -> p c j i", i=PACK))

        def quantise_x(g, a, lo=0, hi=HALF):
            if (g, a) not in g_words:
                width = HALF + P if (g, a) == (1, 1) else HALF
                g_words[g, a] = keep.tile([P, width], U32, name=f"g_words{g}_{a}", align_bytes=256)
                if (g, a) == (1, 0):
                    g_scales[g, a] = shared_scales[4:, :]
                else:
                    own = keep.tile([P, width], U8, name=f"g_scales{g}_{a}", align_bytes=256)
                    g_scales[g, a] = own[:]
            nc.vector.quantize_mx(out=g_words[g, a][:, lo:hi].bitcast(FP8X4), scales=g_scales[g, a][:, lo:hi], in_=woven[g][:, (a * HALF + lo) * PACK:(a * HALF + hi) * PACK])

        def round_w(g, u, cut):
            if (g, u) == (1, 0):
                w_bf[g, u] = woven[g][:, PACK * S:]
            else:
                own = keep.tile([P, PAIR * K_PASS], BF16, name=f"w_bf{g}_{u}", align_bytes=256)
                w_bf[g, u] = own[:]
            dst = w_bf[g, u].rearrange("p (t m j) -> p m j t", t=PAIR, j=PACK)
            src = w_raw[g][:].rearrange("p (j m t) -> p m j t", j=PACK, t=PACK)[:, :, :, PAIR * u:PAIR * (u + 1)]
            if cut > 0:
                nc.scalar.activation(out=dst[:, :cut], in_=src[:, :cut], func=ACT.Copy)
            if cut < P:
                nc.vector.tensor_copy(out=dst[:, cut:], in_=src[:, cut:])

        def quantise_w(g, t0, t1):
            words = keep.tile([P, (t1 - t0) * P], U32, name=f"w_words{g}_{t0}", align_bytes=256)
            if (g, t0) == (0, 1):
                scales = shared_scales[:, :P]
            else:
                own = keep.tile([P, (t1 - t0) * P], U8, name=f"w_scales{g}_{t0}", align_bytes=256)
                scales = own[:]
            lo = t0 % PAIR * K_PASS
            nc.vector.quantize_mx(out=words[:].bitcast(FP8X4), scales=scales, in_=w_bf[g, t0 // PAIR][:, lo:lo + (t1 - t0) * K_PASS])
            for t in range(t0, t1):
                w_words[g, t] = words[:, (t - t0) * P:(t - t0 + 1) * P]
                w_scales[g, t] = scales[:, (t - t0) * P:(t - t0 + 1) * P]

        banks = {}
        for t in range(PACK):
            for a in range(HALVES):
                banks[t, a] = psum.tile([P, HALF], F32, name=f"bank{t}_{a}", tag=f"bank{t}_{a}")

        def first_product(g, t, a):
            nc.tensor.matmul_mx(out=banks[t, a][:], lhsT=w_words[g, t].bitcast(FP8X4), lhsT_scale=w_scales[g, t],
                                rhs=g_words[g, a][:, :HALF].bitcast(FP8X4), rhs_scale=g_scales[g, a][:, :HALF], start=(g == 0), stop=(g == PASSES - 1))

        for j in range(PACK):
            place(0, j, 0, DIRECT, True)
            gather_plane(j)
            if j % PAIR == 1:
                weave(j - 1)
        gather_own(0)
        place(1, 0, PLACED, S, False)
        quantise_x(0, 0)
        quantise_x(0, 1)
        gather_own(1)
        place(1, 1, PLACED, S, False)
        weave_own()
        place(1, 2, 0, PLACED, True)
        place(1, 2, PLACED, S, False)
        for u in range(PAIR):
            round_w(0, u, CUTS[0][u])
        quantise_w(0, 0, 1)
        quantise_w(0, 1, 2)
        quantise_w(0, 2, 4)
        for t in [0, 2, 3]:
            for a in range(HALVES):
                first_product(0, t, a)
        place(1, PACK - 1, 0, PLACED, True)
        for lo, hi in LAST_ROW:
            place(1, PACK - 1, lo, hi, False)
        quantise_x(1, 1, 0, HALF // 2)
        quantise_x(1, 0)
        for a in range(HALVES):
            first_product(0, 1, a)
        for u in range(PAIR):
            round_w(1, u, CUTS[1][u])
        quantise_w(1, 1, 2)
        quantise_x(1, 1, HALF // 2, HALF + P)
        w_words[1, 0] = g_words[1, 1][:, HALF:]
        w_scales[1, 0] = g_scales[1, 1][:, HALF:]
        quantise_w(1, 2, 4)
        for t, a in [(1, 0), (1, 1), (0, 0), (0, 1), (2, 0), (2, 1), (3, 0), (3, 1)]:
            first_product(1, t, a)
        last = PACK - 1


        h = keep.tile([P, PACK, S], F32, name="h", align_bytes=256)
        sums = keep.tile([P, PACK], F32, name="sums")
        totals = keep.tile([P, PACK], F32, name="totals")
        z_planes = keep.tile([P, PACK, S], BF16, name="z_planes", align_bytes=256)

        def empty(t):
            nc.scalar.activation(out=h[:, t, :HALF], in_=banks[t, 0][:], func=ACT.Relu, accum_out=sums[:, t:t + 1])
            nc.vector.tensor_scalar(out=h[:, t, HALF:], in0=banks[t, 1][:], scalar1=0.0, scalar2=sums[:, t:t + 1], op0=ALU.max, op1=ALU.add, accum_out=totals[:, t:t + 1])

        def plane(t, lo, hi, engine):
            if engine is nc.scalar:
                nc.scalar.activation(out=z_planes[:, t, lo:hi], in_=h[:, t, lo:hi], func=ACT.Identity, bias=totals[:, t:t + 1], scale=-float(S))
            else:
                engine.tensor_scalar(out=z_planes[:, t, lo:hi], in0=h[:, t, lo:hi], scalar1=-float(S), scalar2=totals[:, t:t + 1], op0=ALU.mult, op1=ALU.add)

        for t in [1, 0, 2, 3]:
            empty(t)
        warm = psum.tile([P, HALF], F32, name="warm", tag=f"bank{last}_1")
        for i in range(WARM):
            nc.tensor.matmul_mx(out=warm[:WARM_M, :], lhsT=g_words[0, 0][:, :WARM_M].bitcast(FP8X4), lhsT_scale=g_scales[0, 0][:, :WARM_M],
                                rhs=g_words[0, 0][:].bitcast(FP8X4), rhs_scale=g_scales[0, 0], start=True, stop=True)
        plane(1, 0, S, nc.gpsimd)
        plane(0, 0, S, nc.scalar)
        plane(2, 0, S, nc.vector)
        plane(last, 0, QUARTER, nc.scalar)
        plane(last, HALF, S, nc.vector)
        plane(last, QUARTER, HALF, nc.vector)

        z_words = keep.tile([P, S], U32, name="z_words", align_bytes=256)
        z_scales = keep.tile([P, S], U8, name="z_scales", align_bytes=256)
        z_bf = {}
        accs = {}

        def weave_z(lo, hi, on_vector):
            z_bf[lo] = keep.tile([P, (hi - lo) * PACK], BF16, name=f"z_bf{lo}", align_bytes=256)
            dst = z_bf[lo][:].rearrange("p (c i t) -> p c t i", i=4, t=PACK)
            src = z_planes[:, :, lo:hi].rearrange("p t (c i) -> p c t i", i=4)
            if on_vector:
                nc.vector.tensor_copy(out=dst, in_=src)
            else:
                nc.scalar.copy(out=dst, in_=src)

        def second_product(i, lo, hi):
            accs[lo] = psum.tile([P, HALF], F32, name=f"acc{i}", tag=f"bank{i % PACK}_{i // PACK}")
            nc.vector.quantize_mx(out=z_words[:, lo:hi].bitcast(FP8X4), scales=z_scales[:, lo:hi], in_=z_bf[lo][:])
            nc.tensor.matmul_mx(out=accs[lo][:, :hi - lo], lhsT=w2_w[:].bitcast(FP8X4), lhsT_scale=w2_sc[:], rhs=z_words[:, lo:hi].bitcast(FP8X4), rhs_scale=z_scales[:, lo:hi], start=True, stop=True)

        res = keep.tile([P, S], F32, name="res", align_bytes=256)

        def copy_out(lo, hi, on_vector):
            if on_vector:
                nc.vector.tensor_scalar(out=res[:, lo:hi], in0=accs[lo][:, :hi - lo], scalar1=-1.0 / S, scalar2=None, op0=ALU.mult)
            else:
                nc.scalar.activation(out=res[:, lo:hi], in_=accs[lo][:, :hi - lo], func=ACT.Copy, scale=-1.0 / S)

        for lo, hi, on_vector in Z_PIECES:
            weave_z(lo, hi, on_vector)
        for i, (lo, hi, on_vector) in enumerate(Z_PIECES):
            second_product(i, lo, hi)
        for i, (lo, hi, on_vector) in enumerate(Z_PIECES):
            copy_out(lo, hi, i >= 3)
        for lo in [HALF, 0, HALF + QUARTER, QUARTER]:
            nc.sync.dma_start(out=out[:, lo:lo + QUARTER], in_=res[:, lo:lo + QUARTER])
